import numpy as np, ml_dtypes
CORES = [16,17,18,19,32,33,34,35]
N = 8
BF = ml_dtypes.bfloat16
def gentries(a):
    return np.ascontiguousarray(a.reshape(8, 16, -1).transpose(0, 2, 1)).reshape(8, -1)
def gtable(e):
    e = np.asarray(e); return np.ascontiguousarray(e.reshape(8, -1, 16).transpose(0, 2, 1)).reshape(128, -1).astype(np.int32)
G, C, K, RO, SH = 512, 4096, 192, 5, 9
NONE = N * G
def batch(rng, keep=(), high=()):
    key = rng.random((8, C)) * np.where(np.arange(C) >> SH == 0, 3.0, 1.0)
    for c in keep: key[:, c] += 4
    for g in high: key[g, :1 << SH] += 4
    s = np.ascontiguousarray(np.argsort(key, axis=1)[:, :N * K]); w = rng.integers(0, NONE, (8, 16, 4)); ro = np.zeros((8, 16, N * K), np.int64)
    for r in range(N):
        for t in range(16):
            if t < RO: ro[:, t, r * K:(r + 1) * K] = (r + t) % N * G + np.argsort(rng.random((8, G)), axis=1)[:, :K]
            else: ro[:, t, r * K:(r + 1) * K] = np.take_along_axis(w[:, t], rng.integers(0, 4, (8, K)), 1)
    return s, ro, w
def living(rng, s, ro, w, share):
    pa = np.full((8, 16, C), NONE, np.int64); live, dead = [], []
    for g in range(8):
        rest = rng.permutation(np.setdiff1d(np.arange(C), s[g])); h = max(int(len(rest) * share), 8)
        a = rest[h:]; m = len(a); v = rng.integers(0, NONE, (16, m))
        for k in range(RO, 16): v[k] = w[g, k][rng.integers(0, 4, m)]
        v = np.where(rng.random((16, m)) < 0.8 * rng.random((1, m)), ro[g][:, np.arange(m) % (N * K)], v)
        no = rng.random((16, m)) < 0.9 * rng.random((1, m)); no[rng.integers(0, 16, m), np.arange(m)] = False
        pa[g][:, a] = np.where(no, NONE, v); live.append(a); dead.append(rest[:h])
    return pa, live, dead
def trunks(rng, s, ro, live, dead):
    op = rng.integers(0, N * K, (N, 8, G))
    for t in rng.permutation(RO):
        for q in range(N):
            r = int((q - t) % N); np.put_along_axis(op[q], ro[:, t, r * K:(r + 1) * K] - q * G, np.ascontiguousarray(np.broadcast_to(r * K + np.arange(K), (8, K))), 1)
    tr = np.zeros((N, 8, 16, G), np.int64); sh = (N, 16, G)
    for g in range(8):
        a = live[g]; m = len(a); top = np.sort(a)[-(m >> 3):]; x = a[rng.integers(0, m, sh)]
        x = np.where(rng.random(sh) < rng.choice(np.array([0.3, 0.6, 0.8, 0.9, 1.0]), (N, 1, G)), top[rng.integers(0, len(top), sh)], x)
        x = np.where(rng.random(sh) < rng.choice(np.array([0.0, 0.1, 0.25]), (N, 1, G)), a[(op[:, g][:, None, :] + N * K * rng.integers(0, 2, sh)) % m], x)
        gone = np.concatenate([dead[g], s[g][::4]])
        tr[:, g] = np.where(rng.random(sh) < rng.choice(np.array([0.0, 0.0, 0.1, 0.3]), (N, 1, G)), gone[rng.integers(0, len(gone), sh)], x)
    return tr
def pack(tr, pa, s, ro):
    return {"trunk": np.ascontiguousarray(tr.reshape(N, 128, G)).astype(np.int32), "paths": np.stack([pa.reshape(128, C)] * N).astype(np.int32),
            "calls": np.stack([gtable(s[:, r * K:(r + 1) * K]) for r in range(N)]), "routes": np.stack([ro[:, :, r * K:(r + 1) * K].reshape(128, K) for r in range(N)]).astype(np.int32)}
def setup_inputs(rng):
    s, ro, w = batch(rng); pa, live, dead = living(rng, s, ro, w, 0.05)
    return pack(trunks(rng, s, ro, live, dead), pa, s, ro)
def setup_inputs_ties(rng):
    edge = np.array([0, C - 1] + [e for b in range(1, C >> SH) for e in ((b << SH) - 1, b << SH)])
    s, ro, w = batch(rng, edge); pa, live, dead = living(rng, s, ro, w, 0.05); tr = trunks(rng, s, ro, live, dead); sh = (N, 16, G); k = np.arange(16)[None, :, None]
    for g in range(8):
        a = np.union1d(live[g], edge); d = np.setdiff1d(np.append(dead[g], s[g][0]), edge)
        few = pa[g][:, live[g][:3]]; pa[g][:, a] = few[:, rng.integers(0, 3, len(a))]
        x = tr[:, g].copy(); x[:, 8:] = x[:, :8][:, ::-1].copy()
        kind = rng.integers(0, 5, (N, 1, G)); end = rng.choice(np.array([0, 15]), (N, 1, G)); z = a[rng.integers(0, len(a), sh)]
        x = np.where(kind == 1, edge[rng.integers(0, len(edge), sh)], np.where(kind == 2, z, x))
        tr[:, g] = np.where(kind == 3, np.where(k == end, d[rng.integers(0, len(d), sh)], z), x)
        j = rng.permutation(N * K)[:64]; r = j // K; c = rng.permutation(live[g])[:64]
        pa[g][:, c] = ro[g][:, j]; tr[r, g, rng.integers(0, 16, 64), ro[g, 0, j] - r * G] = c
        u = rng.permutation(np.setdiff1d(np.nonzero(s[g] >> SH == (C - 1) >> SH)[0], j))[:16]; q = u // K; at = ro[g, 0, u] - q * G
        b = np.sort(rng.permutation(np.setdiff1d(live[g][live[g] >> SH == 0], np.append(edge, c)))[:32].reshape(2, 16), axis=0)
        pa[g][:, b[0]] = ro[g][:, u]; pa[g][:, b[1]] = ro[g][:, u]; h = rng.integers(0, 16, 16)
        pa[g, h, b[0]] = np.where(rng.random(16) < 0.5, NONE, (ro[g, h, u] + 1) % NONE)
        y = tr[:, g]; e = rng.integers(0, 16, 16)
        y[q, :, at] = b[rng.integers(0, 2, (16, 16)), np.arange(16)[:, None]]
        y[q, e, at] = b[1]; y[q, (e + 8) & 15, at] = b[0]
    return pack(tr, pa, s, ro)
def setup_inputs_same(rng):
    few = np.array([0, 1, 2, (1 << SH) - 1]); keep = np.append(few, C - 1)
    s, ro, w = batch(rng, keep, (5, 6, 7)); pa, live, dead = living(rng, s, ro, w, 0.05); tr = trunks(rng, s, ro, live, dead); sh = (N, 16, G)
    for g in range(8):
        pa[g][:, keep] = ro[g][:, rng.integers(0, N * K, len(keep))]
        top = np.union1d(live[g][live[g] >> SH == (C - 1) >> SH], np.array([C - 1])); x = top[rng.integers(0, len(top), sh)]
        if g > 4:
            low = rng.permutation(live[g][live[g] >> SH == 0]); n = rng.permutation(N * K); q = np.arange(N * K) // K; at = ro[g, 0] - q * G
            if g == 5: i = (n >= 256).astype(np.int64) + (n >= 768)
            elif g == 6: i = (n >= 1024).astype(np.int64)
            else: i = np.arange(N * K) % len(low)
            y = np.where(tr[:, g] >> SH == 0, x, tr[:, g]); y[q, :, at] = x[q, :, at]
            y[q, rng.integers(0, 16, N * K), at] = low[i]; tr[:, g] = y
            continue
        one = few[rng.integers(0, (1, 2, 4)[g % 3], (N, 1, G))]
        x = np.where(np.arange(16)[None, :, None] == rng.integers(0, 16, (N, 1, G)), one, x)
        tr[:, g] = np.where(rng.random((N, 1, G)) < (1.0 if g < 4 else 0.6), x, tr[:, g])
    return pack(tr, pa, s, ro)
def setup_inputs_block(rng):
    s, ro, w = batch(rng, [C - 1]); o = rng.permutation(8); f = int(o[4])
    if not np.any(s[f] == 0): s[f, int(rng.integers(0, N * K))] = 0
    for r in range(N):
        p = rng.permutation(G); v = (r - 1) % N
        ro[f, 0, r * K:(r + 1) * K] = r * G + p[:K]; ro[f, 1, v * K:(v + 1) * K] = r * G + p[K:2 * K]
    pa, live, dead = living(rng, s, ro, w, 0.05); tr = trunks(rng, s, ro, live, dead); sh = (N, 16, G); q = int(rng.integers(0, N))
    for h in range(5):
        g = int(o[h]); pa[g][:, C - 1] = ro[g][:, 0]
        top = np.union1d(live[g][live[g] >> SH == (C - 1) >> SH], np.array([C - 1])); d = np.setdiff1d(dead[g], np.array([C - 1]))
        full = top[rng.integers(0, len(top), sh)]; free = d[rng.integers(0, len(d), sh)]
        if h == 0: tr[:, g] = full
        if h == 1 or h == 2: tr[:, g] = free
        if h == 2: tr[q, g] = full[q]
        if h == 3: pa[g] = NONE
        if h == 4:
            a = np.arange(N * K) // K; b = (a + 1) % N; u = ro[g, 0] - a * G; v = ro[g, 1] - b * G; y = tr[:, g]
            y[a, rng.integers(0, 16, N * K), u] = d[rng.integers(0, len(d), N * K)]
            y[b, :, v] = full[b, :, v]; y[b[::4], rng.integers(0, 16, len(b[::4])), v[::4]] = s[g][::4]
    return pack(tr, pa, s, ro)
def setup_inputs_late(rng):
    s, ro, w = batch(rng); pa, live, dead = living(rng, s, ro, w, 0.05); tr = trunks(rng, s, ro, live, dead); sh = (N, 16, G)
    for g in range(8):
        tr[:, g] = np.where(rng.random(sh) < rng.choice(np.array([0.0, 0.5, 1.0]), (N, 1, G)), s[g][rng.integers(0, N * K, sh)], tr[:, g])
        u = np.argsort(s[g, :K])[:16]; v = K + np.argsort(s[g, K:2 * K])[-16:]
        y = tr[2, g]; y[:, ro[g, 1, v] - 2 * G] = s[g][u]
        for a, r, t in ((u, 0, 0), (v, 1, 0), (u, 0, 1)):
            y = tr[r + t, g]; y[:2, ro[g, t, a] - (r + t) * G] = dead[g][0]
        e = np.argsort(s[g, :K])[16:]; e = e[np.isin(ro[g, 1, e], ro[g, 0, K:2 * K], invert=True)]; lo, hi = e[:16], e[-16:]
        top = live[g][live[g] >> SH == (C - 1) >> SH]
        assert len(e) >= 32 and len(top) > 0 and np.all((s[g][lo] >> SH) < (s[g][hi] >> SH))
        assert np.all(np.any(pa[g][:, top] != NONE, axis=0)) and np.all(pa[g][:, dead[g][0]] == NONE)
        y = tr[0, g]; y[:2, ro[g, 0, np.append(lo, hi)]] = dead[g][0]
        y = tr[1, g]; y[:, ro[g, 1, lo] - G] = top[rng.integers(0, len(top), 16)]; y[:, ro[g, 1, hi] - G] = s[g][lo]
    return pack(tr, pa, s, ro)
def setup_inputs_spread(rng):
    s, ro, w = batch(rng); late = ro[:, RO:]; ro[:, RO:] = np.where(rng.random(late.shape) < 0.5, rng.integers(0, NONE, late.shape), late)
    pa, live, dead = living(rng, s, ro, w, 0.02); tr = trunks(rng, s, ro, live, dead)
    pa = np.where((pa != NONE) & (rng.random(pa.shape) < 0.5), np.minimum((NONE * rng.random(pa.shape) ** 4).astype(np.int64), NONE - 1), pa)
    x = np.minimum((C * rng.random(tr.shape) ** rng.choice(np.array([0.25, 1.0, 4.0]), (N, 8, 1, G))).astype(np.int64), C - 1)
    return pack(np.where(rng.random((N, 8, 1, G)) < 0.5, x, tr), pa, s, ro)
def check_inputs(d):
    bad = []
    for k, lo, hi in (("trunk", 0, C - 1), ("paths", 0, NONE), ("calls", 0, C - 1), ("routes", 0, NONE - 1)):
        if np.min(d[k]) < lo or np.max(d[k]) > hi: bad.append("range of " + k)
    if bad: return bad
    if np.any(d["paths"] != d["paths"][:1]): bad.append("paths alike on all ranks")
    s = np.concatenate([gentries(a) for a in d["calls"]], axis=1).astype(np.int64)
    if np.any(np.diff(np.sort(s, axis=1), axis=1) == 0): bad.append("calls of a group all different")
    if np.any(np.take_along_axis(d["paths"][0].reshape(8, 16, C), s[:, None, :], 2) != NONE): bad.append("paths of the seekers are none")
    own = (np.arange(N)[:, None] + np.arange(RO)[None, :]) % N
    at = d["routes"].astype(np.int64).reshape(N, 8, 16, K)[:, :, :RO] - own[:, None, :, None] * G
    if np.min(at) < 0 or np.max(at) > G - 1: bad.append("row t of routes names bundles of rank (r + t) mod N")
    if np.any(np.diff(np.sort(at, axis=3), axis=3) == 0): bad.append("row t of routes names different bundles")
    return bad
def reference(trunk, paths, calls, routes):
    tr = trunk.astype(np.int64).reshape(N, 8, 16, G); pa = paths[0].astype(np.int64).reshape(8, 16, C)
    sl = np.stack([gentries(a) for a in calls]).astype(np.int64); ro = routes.astype(np.int64).reshape(N, 8, 16, K)
    row = np.arange(16)[None, :, None]; D = C // N
    for t in range(RO):
        new = pa.copy(); gone = np.zeros((8, C), bool)
        for q in range(N):
            r = (q - t) % N; s = sl[r]; at = ro[r, :, t] - q * G
            hold = np.take_along_axis(tr[q], at[:, None, :], 2)
            hop = np.take_along_axis(pa, hold.reshape(8, 1, 16 * K), 2).reshape(8, 16, 16, K)
            dead = np.logical_not(np.any(hop != NONE, axis=1))
            like = np.add.reduce((hop == ro[r][:, :, None, :]).astype(np.int64), axis=1)
            may = (hold >> SH) < (s >> SH)[:, None, :]
            key = np.where(dead, 2 ** 22 + 15 - row, np.where(may, (like * C + C - 1 - hold) * 16 + 15 - row, -1))
            best = np.max(key, axis=1); p = 15 - (best & 15)
            go = np.any(np.take_along_axis(pa, s[:, None, :], 2) != NONE, axis=1) | (t == 0)
            won = go & (best >= 0); vic = np.take_along_axis(hold, p[:, None, :], 1)[:, 0]
            b, i = np.nonzero(won); tr[q, b, p[b, i], at[b, i]] = s[b, i]; new[b, t, s[b, i]] = ro[r, b, t, i]
            b, i = np.nonzero(won & (best < 2 ** 22)); gone[b, vic[b, i]] = True
            b, i = np.nonzero(go & (best < 0)); gone[b, s[b, i]] = True
        pa = np.where(gone[:, None, :], NONE, new)
    return {"yt": tr.reshape(N, 128, G).astype(np.float32), "yp": np.stack([pa[:, :, r * D:(r + 1) * D].reshape(128, D) for r in range(N)]).astype(np.float32)}

@@ -1,0 +1,398 @@
+from concourse.bass import DstId, RemoteDMATransfer
+from concourse.mybir import AluOpType, ActivationFunctionType
+
+RO = 5
+F32, BF, I32, U16 = "float32", "bfloat16", "int32", "uint16"
+SCRATCH = {}
+
+
+def _b(where, dtype, **kw):
+    for k, s in kw.items():
+        SCRATCH[k] = (where, s, dtype)
+
+
+_b("dram", I32, stR=[8, 128, 24], stC=[8, 128, 2], stT=[8, 128, 64], landR=[8, 128, 24], landC=[8, 128, 2], landT=[8, 128, 64])
+_b("dram", F32, stV=[8, 128, 64], landV=[8, 128, 64], stY=[8, 128, 64], landY=[8, 128, 64])
+_b("dram", BF, stD=[8, 128, 4], landD=[8, 128, 4])
+_b("sbuf", I32, P=[128, 4096], XP=[64, 1024], P2=[128, 512], ii=[128, 192], col=[128, 256], cp=[128, 1], ci=[128, 4],
+   cq8=[128, 256], iia=[128, 192], cola=[128, 192], t12b=[128, 12], Cl=[128, 12], Cti=[128, 12], R=[128, 192],
+   OT=[128, 60], Tki=[128, 512], BI=[128, 12], UI=[128, 24], C2=[128, 12], NI=[128, 12], NI2=[128, 24], RI=[128, 192],
+   RIh=[128, 192], RIl=[128, 192], ccq=[128, 128])
+_b("sbuf", U16, LI=[128, 12], LB=[128, 12], AT=[128, 60], SN=[128, 60], H16=[128, 192])
+_b("sbuf", F32, KC=[128, 16], IDf=[128, 128], I64s=[128, 64], REPf=[128, 256], SELq=[128, 16], EM=[128, 192], DM=[128, 192],
+   REP8=[8, 128], Clf=[128, 12], Cs=[128, 12], Ctf=[128, 12], E=[128, 192], Es=[128, 192], Et=[128, 192],
+   SG=[128, 960], TH=[128, 960], RJ=[128, 960], RA=[128, 3072], RB=[128, 3072], Tk=[128, 512], Hf=[128, 192],
+   Dg=[128, 192], M=[128, 192], A1=[128, 192], KEY=[128, 192], KB=[128, 192], T1=[128, 96], T2=[128, 48], T3=[128, 24],
+   BEST=[128, 12], BW=[128, 8], Bm=[128, 8], bT=[8, 192], W=[128, 192], UF=[128, 24], OK=[128, 12], NF=[128, 24],
+   S0=[128, 192], S1=[128, 96], S2=[128, 48], S3=[128, 24], S4=[128, 12], VAL=[128, 512], VR=[128, 512], YP=[128, 512])
+_b("sbuf", BF, iot=[128, 64], iotR=[128, 64], WST=[128, 144], W0=[128, 144], DW=[128, 2048], OUTW=[128, 128], YS=[128, 240],
+   YS64=[128, 240], R8b=[8, 128], ID64=[64, 64], F=[128, 4096], ZA=[128, 4096], ZB=[128, 4096], EQ=[128, 3072], FG=[128, 3072],
+   FS=[128, 192], OHI=[128, 768], OLO=[128, 768], SHI=[128, 768], SLO=[128, 768], D=[64, 64], ZVa=[128, 192], ZVb=[128, 192],
+   KD=[8, 512])
+_b("psum", F32, KPa=[128, 512], KPb=[128, 512], pBa=[128, 512], pBb=[128, 512], pTR=[128, 512], pD=[128, 512], pM=[128, 512],
+   pZ=[128, 512])
+
+_ARR = ["arrR", "arrC", "arrT", "arrV", "arrY", "arrD"]
+_DMA = ["dR", "dC", "dT", "dP", "dX", "dP2", "dF", "dCl", "dRl", "dO", "dTk", "dRR", "dRJ", "dSN", "dV", "dVR", "dY", "dD", "dKD",
+        "oY1", "oY2", "oP"]
+SEMAPHORES = ["cv", "cs", "cpe", "cg", "sent"] + _ARR + _DMA
+
+
+def rank_program(g, core, T, topo):
+    me = T.rank_of(core)
+    if me is None:
+        return
+    A, AF = AluOpType, ActivationFunctionType
+    eng = {"v": g.vector, "s": g.scalar, "p": g.tensor, "g": g, "y": g.sync}
+    own = {"v": "cv", "s": "cs", "p": "cpe", "g": "cg"}
+    cnt = {s: 0 for s in SEMAPHORES}
+    seen = {q: {} for q in eng}
+
+    def need(q, deps):
+        best = {}
+        for d in deps:
+            if d is not None:
+                best[d[0]] = max(best.get(d[0], 0), d[1])
+        for s, n in best.items():
+            if seen[q].get(s, 0) < n:
+                eng[q].wait_ge(T.sem[s], n)
+                seen[q][s] = n
+
+    def op(q, f, *deps):
+        need(q, deps)
+        s = own[q]
+        f(eng[q]).then_inc(T.sem[s], 1)
+        cnt[s] += 1
+        return (s, cnt[s])
+
+    def V(f, *deps):
+        return op("v", f, *deps)
+
+    def S(f, *deps):
+        return op("s", f, *deps)
+
+    def MM(deps, *ms):
+        need("p", deps)
+        for n, m in enumerate(ms):
+            i = eng["p"].matmul(m[0], m[1], m[2], start=m[3], stop=m[4])
+            if n == len(ms) - 1:
+                i.then_inc(T.sem["cpe"], 1)
+        cnt["cpe"] += 1
+        return ("cpe", cnt["cpe"])
+
+    def dma(q, out, in_, sem, *deps):
+        need(q, deps)
+        eng[q].dma_start(out, in_).then_inc(T.sem[sem], 16)
+        cnt[sem] += 16
+        return (sem, cnt[sem])
+
+    def ts(out, in0, s1, op0, s2=None, op1=None):
+        if op1 is None:
+            return lambda e: e.tensor_scalar(out, in0, s1, None, op0)
+        return lambda e: e.tensor_scalar(out, in0, s1, s2, op0, op1)
+
+    def tt(out, a, b, o):
+        return lambda e: e.tensor_tensor(out, a, b, o)
+
+    def cpy(out, in_):
+        return lambda e: e.tensor_copy(out, in_)
+
+    def act(out, in_, f=AF.Copy):
+        return lambda e: e.activation(out, in_, f)
+
+    def send(src, dst, sem, *deps):
+        need("g", deps)
+        order = sorted([(me + k) % 8 for k in range(1, 8)], key=lambda n: len(topo.engines(core, T.cores[n])))
+        used, tr = [], []
+        for n in order:
+            c = T.cores[n]
+            es = [e for e in topo.engines(core, c) if e not in used][:2]
+            used += es
+            a = topo.addr(c)
+            tr.append(RemoteDMATransfer(dst_ids=[DstId(rid=a[0], pnc=a[1])], dma_engine_mask=sum(1 << e for e in es),
+                                        remote_sem=T.sem[sem], srcs=[T[src][n]], dsts=[T[dst][me]], alu_op=0))
+        g.remote_dma_fused(tr, local_sem=T.sem["sent"])
+        cnt["sent"] += 14
+        cnt[sem] += 14
+
+    lo, hi = 16 * me, 16 * me + 16
+    dma("y", T.stC[:, 0:96, :], T.calls[:], "dC")
+    dma("y", T.stC[:, 96:128, :], T.trunk[0:1, :], "dC")
+    tC = dma("y", T.landC[me, 0:96, :], T.calls[lo:hi, :], "dC")
+    dma("y", T.stR[:], T.routes[:], "dR")
+    tR = dma("y", T.landR[me], T.routes[lo:hi, :], "dR")
+    dma("y", T.stT[:], T.trunk[:], "dT")
+    tT = dma("y", T.landT[me], T.trunk[lo:hi, :], "dT")
+    for q in range(8):
+        tP = dma("s", T.P[16 * q:16 * q + 16, :], T.paths[lo:hi, :], "dP")
+    for k in range(16):
+        tX = dma("y", T.XP[:, 64 * k:64 * k + 64], T.paths[lo + k:lo + k + 1, :], "dX")
+    for q in range(8):
+        tP2 = dma("s", T.P2[16 * q:16 * q + 16, :], T.paths[lo:hi, 512 * q:512 * q + 512], "dP2")
+    g1 = op("g", lambda e: e.iota(T.cp[:, 0:1], [[0, 1]], 0, 1))
+    g2 = op("g", lambda e: e.iota(T.col[:, :], [[1, 256]], 0, 0))
+    g3 = op("g", lambda e: e.iota(T.ii[:, :], [[1, 12], [12, 16]], 0, 0))
+    send("stC", "landC", "arrC", tC)
+    send("stR", "landR", "arrR", tR)
+    send("stT", "landT", "arrT", tT)
+    gz = op("g", lambda e: e.iota(T.ZA[:, :], [[0, 4096]], 0, 0, allow_small_or_imprecise_dtypes=True))
+    gz = op("g", lambda e: e.iota(T.ZB[:, :], [[0, 4096]], 0, 0, allow_small_or_imprecise_dtypes=True))
+
+    vF = V(lambda e: e.memset(T.F[:, :], 0.0))
+    V(lambda e: e.memset(T.Bm[:, :], 0.0))
+    KC, col, ci = T.KC, T.col, T.ci
+
+    def kc(n):
+        return KC[:, n:n + 1]
+    V(ts(ci[:, 0:1], T.cp[:, 0:1], 15, A.bitwise_and), g1)
+    V(ts(ci[:, 1:2], T.cp[:, 0:1], 4, A.arith_shift_right))
+    V(ts(ci[:, 2:3], T.cp[:, 0:1], 63, A.bitwise_and))
+    V(cpy(kc(0), T.cp[:, 0:1]))
+    v = V(ts(T.cq8[:, :], col[:, :], 4, A.arith_shift_right, 7, A.bitwise_and), g2)
+    V(ts(T.cola[:, :], col[:, 0:192], 15, A.bitwise_and))
+    V(ts(T.iia[:, :], T.ii[:, :], 15, A.bitwise_and), g3)
+    V(ts(T.ccq[:, 0:16], col[:, 0:16], 7, A.bitwise_and))
+    V(cpy(kc(1), ci[:, 0:1]), v)
+    V(cpy(kc(2), ci[:, 1:2]))
+    V(cpy(kc(7), ci[:, 2:3]))
+    V(ts(kc(3), ci[:, 1:2], 512.0, A.mult))
+    V(ts(kc(4), ci[:, 1:2], 16.0, A.mult, 15.0, A.add))
+    V(ts(kc(8), ci[:, 0:1], 112.0, A.add))
+    V(ts(kc(9), ci[:, 0:1], -1.0, A.mult, float(2 ** 21 + 15), A.add))
+    V(ts(kc(10), ci[:, 0:1], 5.0, A.is_lt))
+    V(ts(kc(11), ci[:, 0:1], 0.0, A.is_equal))
+    V(ts(kc(12), ci[:, 1:2], 16.0, A.mult, 16.0, A.add))
+    V(ts(kc(14), ci[:, 0:1], 12.0, A.mult))
+    v = V(ts(kc(13), ci[:, 1:2], 1.0, A.add))
+    V(tt(kc(12), kc(12), kc(11), A.mult), v)
+    v = V(tt(kc(13), kc(13), kc(11), A.mult))
+    V(ts(kc(5), kc(12), -1.0, A.add), v)
+    v = V(ts(kc(6), kc(13), -1.0, A.add))
+    V(ts(T.WST[:, :], col[:, 0:144], kc(4), A.is_equal, 65536.0, A.mult), v)
+    V(ts(T.W0[:, :], col[:, 0:144], kc(5), A.is_equal))
+    v = V(ts(T.t12b[:, :], col[:, 0:12], kc(14), A.add))
+    V(cpy(T.LI[:, :], T.t12b[:, :]), v)
+    v = V(ts(T.Cti[:, :], T.t12b[:, :], 4, A.arith_shift_right))
+    vLB = V(cpy(T.LB[:, :], T.Cti[:, :]), v)
+    V(ts(T.IDf[:, :], col[:, 0:128], kc(0), A.is_equal))
+    V(ts(T.ID64[:, :], col[0:64, 0:64], KC[0:64, 0:1], A.is_equal))
+    V(ts(T.I64s[:, :], col[:, 0:64], kc(7), A.is_equal))
+    V(ts(T.REPf[:, :], T.cq8[:, :], kc(2), A.is_equal))
+    V(ts(T.SELq[:, :], T.ccq[:, 0:16], kc(2), A.is_equal))
+    V(ts(T.EM[:, :], T.iia[:, :], kc(1), A.is_equal))
+    V(ts(T.DM[:, :], T.cola[:, :], kc(1), A.is_equal))
+    V(ts(T.REP8[:, :], T.cq8[0:8, 0:128], KC[0:8, 0:1], A.is_equal))
+    V(ts(T.R8b[:, :], T.cq8[0:8, 0:128], KC[0:8, 0:1], A.is_equal, 4096.0, A.mult))
+    V(ts(T.OUTW[:, :], T.cq8[:, 0:128], kc(6), A.is_equal, -float(2 ** 27), A.mult))
+    V(ts(T.YS[:, :], col[:, 0:240], kc(8), A.is_equal))
+    V(ts(T.YS64[:, :], col[:, 0:240], kc(8), A.is_equal, 64.0, A.mult))
+    V(cpy(T.iot[:, :], col[:, 0:64]))
+    V(ts(T.iotR[:, :], col[:, 0:64], -1.0, A.mult, 63.0, A.add))
+    for p in range(16):
+        vC = V(ts(T.DW[:, 128 * p:128 * p + 128], T.W0[:, 15 - p:143 - p], float(2 ** 22 * (16 - p)), A.mult))
+    v, n = tX, 512
+    while n >= 64:
+        v = V(tt(T.XP[:, 0:n], T.XP[:, 0:n], T.XP[:, n:2 * n], A.min), v)
+        n //= 2
+    vD = V(ts(T.D[:, :], T.XP[:, 0:64], 4096.0, A.is_ge), v)
+
+    def flags_to_F(tok):
+        for q in range(8):
+            t = dma("y", T.F[16 * q:16 * q + 1, :], T.D[:, :], "dF", tok)
+        return t
+    need("y", [("arrC", 14), tC])
+    tCl = dma("y", T.Cl[:, :], T.landC[:, 0:96, :], "dCl")
+    need("y", [("arrR", 14), tR])
+    tRl = dma("y", T.R[:, :], T.landR[:], "dRl")
+    for t in range(RO):
+        tO = dma("y", T.OT[16 * t:128, 12 * t:12 * t + 12], T.landR[0:8 - t, 8 * t:8 * t + 8, :], "dO")
+        if t:
+            tO = dma("y", T.OT[0:16 * t, 12 * t:12 * t + 12], T.landR[8 - t:8, 8 * t:8 * t + 8, :], "dO")
+    need("y", [("arrT", 14), tT])
+    tTk = dma("y", T.Tki[:, :], T.landT[:], "dTk")
+    tF = flags_to_F(vD)
+
+    v = V(cpy(T.Clf[:, :], T.Cl[:, :]), tCl, vC, vLB)
+    V(ts(T.Cti[:, :], T.Cl[:, :], 3584, A.bitwise_and))
+    v = V(ts(T.Cs[:, :], T.Cl[:, :], -16.0, A.mult, 65520.0, A.add))
+    V(cpy(T.Ctf[:, :], T.Cti[:, :]), v)
+    vE = V(tt(T.E[:, :], T.Clf[:, :].indirect(T.LB[:, :]), T.EM[:, :], A.mult))
+    V(tt(T.Es[:, :], T.Cs[:, :].indirect(T.LB[:, :]), T.EM[:, :], A.mult))
+    vE = V(tt(T.Et[:, :], T.Ctf[:, :].indirect(T.LB[:, :]), T.EM[:, :], A.mult), vE)
+    vRJ = V(cpy(T.RJ[:, 0:192], T.R[:, :].indirect(T.LI[:, :])), tRl)
+    pn = MM([vE], (T.pBa[:, 0:8], T.E[:, 0:128], T.SELq[:, 8:16], True, True),
+            (T.pBa[0:64, 8:12], T.E[:, 128:192], T.SELq[:, 8:12], True, True),
+            (T.pBa[64:128, 8:12], T.E[:, 128:192], T.SELq[:, 12:16], True, True))
+
+    def rep(t):
+        return T.REPf[:, 16 * (8 - t):16 * (16 - t)]
+    sprep = [None] * RO
+
+    def prep(t):
+        m = MM([vE, sprep[t - 1] if t else None], (T.pM[:, 0:192], rep(t), T.E[:, :], True, True),
+               (T.pM[:, 192:384], rep(t), T.Et[:, :], True, True))
+        S(act(T.SG[:, 192 * t:192 * t + 192], T.pM[:, 0:192]), m)
+        sprep[t] = S(act(T.TH[:, 192 * t:192 * t + 192], T.pM[:, 192:384]))
+
+    rr = [None] * RO
+    RRb = [T.RA, T.RB]
+    for p in range(8):
+        a = V(cpy(T.RA[:, p::16], T.RJ[:, 0:192]), vRJ)
+        b = S(act(T.RA[:, 8 + p::16], T.RJ[:, 0:192]), vRJ)
+    rr[0] = [a, b]
+    prep(0)
+    vNI = V(cpy(T.NI[:, :], T.pBa[:, 0:12]), pn)
+    vAT = V(ts(T.AT[:, :], T.OT[:, :], kc(3), A.subtract), tO)
+    vTk = V(cpy(T.Tk[:, :], T.Tki[:, :]), tTk)
+    dma("y", T.RB[16:128, :], T.RA[0:112, :], "dRR", *rr[0])
+    rr[1] = [dma("y", T.RB[0:16, :], T.RA[112:128, :], "dRR")]
+    for t in (2, 3, 4):
+        dma("y", T.RJ[16 * t:128, 192 * t:192 * t + 192], T.RJ[0:128 - 16 * t, 0:192], "dRJ", vRJ)
+        tRJ = dma("y", T.RJ[0:16 * t, 192 * t:192 * t + 192], T.RJ[128 - 16 * t:128, 0:192], "dRJ")
+    tSN = None
+    vD1 = vD
+
+    def zmm(half):
+        z, w = (T.ZA, T.YS64) if half == 0 else (T.ZB, T.YS)
+        return MM([vZ], *[(T.pZ[:, :], w[:, 112 - 16 * q:240 - 16 * q], z[:, 512 * q:512 * q + 512], half == 0 and q == 0,
+                          half == 1 and q == 7) for q in range(8)])
+
+    for t in range(RO):
+        at = T.AT[:, 12 * t:12 * t + 12]
+        RR = RRb[t % 2]
+        SGt, THt = T.SG[:, 192 * t:192 * t + 192], T.TH[:, 192 * t:192 * t + 192]
+        h16 = V(cpy(T.H16[:, :], T.Tk[:, :].indirect(at)), vTk, vAT)
+        hf = S(act(T.Hf[:, :], T.Tk[:, :].indirect(at)), vTk, vAT)
+
+        def eq(c):
+            return V(tt(T.EQ[:, 1024 * c:1024 * c + 1024], T.P[:, :].indirect(T.H16[:, 64 * c:64 * c + 64]),
+                        RR[:, 1024 * c:1024 * c + 1024], A.is_equal), h16, tP, *rr[t])
+
+        def fg(q, c):
+            o, w = T.FG[:, 1024 * c:1024 * c + 1024], T.F[:, :].indirect(T.H16[:, 64 * c:64 * c + 64])
+            return op(q, act(o, w) if q == "s" else cpy(o, w), h16, tF, vF)
+        if t < 4:
+            prep(t + 1)
+        if 1 <= t < 4:
+            for p in range(16):
+                x = S(act(RRb[(t + 1) % 2][:, p::16], T.RJ[:, 192 * (t + 1):192 * (t + 2)]), tRJ, *rr[t])
+            rr[t + 1] = [x]
+        e0 = eq(0)
+        v = V(tt(T.Dg[:, :], SGt, T.Hf[:, :], A.subtract), hf, sprep[t])
+        vM = V(tt(T.M[:, :], T.Hf[:, :], THt, A.is_lt))
+        e1 = eq(1)
+        sA = S(lambda e: e.activation(T.A1[:, :], T.Dg[:, :], AF.Identity, bias=kc(9), scale=16.0), v)
+        f0 = fg("s", 0)
+        f1 = fg("s", 1)
+        if t:
+            fs = S(act(T.FS[:, :], T.F[:, :].indirect(T.SN[:, 12 * t:12 * t + 12])), tSN)
+        e2 = eq(2)
+        vA = V(tt(T.A1[:, :], T.M[:, :], T.A1[:, :], A.mult), sA, vM)
+        f2 = fg("v" if t else "s", 2)
+
+        def dst(c):
+            return T.KPb[:, 0:64] if c == 2 else T.KPa[:, 64 * c:64 * c + 64]
+
+        def eqm(c, tok):
+            return MM([tok], *[(dst(c), T.WST[:, 15 - p:143 - p], T.EQ[:, 1024 * c + p:1024 * c + 1024:16], False, False)
+                               for p in range(16)])
+
+        def fgm(c, tok, last):
+            return MM([tok], *[(dst(c), T.DW[:, 128 * p:128 * p + 128], T.FG[:, 1024 * c + p:1024 * c + 1024:16], False,
+                                last and p == 15) for p in range(16)])
+        MM([vE], (T.KPa[:, 0:128], rep(t), T.Es[:, 0:128], True, False))
+        MM([vE], (T.KPb[:, 0:64], rep(t), T.Es[:, 128:192], True, False))
+        eqm(0, e0)
+        eqm(1, e1)
+        eqm(2, e2)
+        fgm(0, f0, False)
+        pa = fgm(1, f1, t == 0)
+        if t:
+            pa = MM([fs], (T.KPa[:, 0:128], T.OUTW[:, :], T.FS[:, 0:128], False, True))
+            MM([fs], (T.KPb[:, 0:64], T.OUTW[:, :], T.FS[:, 128:192], False, False))
+        pb = fgm(2, f2, True)
+        ka = V(tt(T.KEY[:, 0:128], T.KPa[:, 0:128], T.A1[:, 0:128], A.add), pa, vA)
+        kb = V(tt(T.KEY[:, 128:192], T.KPb[:, 0:64], T.A1[:, 128:192], A.add), pb)
+        xa = MM([ka], (T.pBa[:, 0:128], T.KEY[:, 0:128], T.IDf[:, :], True, True))
+        sa = S(act(T.KB[:, 0:128], T.pBa[:, 0:128]), xa)
+        xb = MM([kb], (T.pBb[0:64, 0:64], T.KEY[:, 128:192], T.IDf[:, 0:64], True, True),
+                (T.pBb[64:128, 0:64], T.KEY[:, 128:192], T.IDf[:, 64:128], True, True))
+        sb = S(act(T.KB[:, 128:192], T.pBb[:, 0:64]), xb)
+        if t == 0:
+            v = V(tt(T.S0[:, :], SGt, T.DM[:, :], A.mult))
+            for x, y in ((T.S0, T.S1), (T.S1, T.S2), (T.S2, T.S3), (T.S3, T.S4)):
+                v = V(tt(y[:, :], x[:, 0::2], x[:, 1::2], A.add), v)
+            vSN = V(cpy(T.SN[:, 0:12], T.S4[:, :]), v)
+            for u in range(1, RO):
+                dma("y", T.SN[16 * u:128, 12 * u:12 * u + 12], T.SN[0:128 - 16 * u, 0:12], "dSN", vSN)
+                tSN = dma("y", T.SN[0:16 * u, 12 * u:12 * u + 12], T.SN[128 - 16 * u:128, 0:12], "dSN")
+            V(ts(T.NI2[:, 0:12], T.NI[:, :], 6, A.arith_shift_right), vNI)
+            v = V(ts(T.NI2[:, 12:24], T.NI[:, :], 63, A.bitwise_and))
+            v = V(cpy(T.NF[:, :], T.NI2[:, :]), v)
+            for c in range(12):
+                V(ts(T.SHI[:, 64 * c:64 * c + 64], T.iot[:, :], T.NF[:, c:c + 1], A.is_equal), v)
+                vS = V(ts(T.SLO[:, 64 * c:64 * c + 64], T.iot[:, :], T.NF[:, 12 + c:13 + c], A.is_equal, -1.0, A.mult))
+        if t == 1:
+            v = V(cpy(T.RI[:, :], T.RJ[:, 0:192]))
+            V(ts(T.RIh[:, :], T.RI[:, :], 6, A.arith_shift_right), v)
+            v = V(ts(T.RIl[:, :], T.RI[:, :], 63, A.bitwise_and))
+            V(ts(T.ZVa[:, :], T.RIh[:, :], -64.0, A.add, kc(10), A.mult), v)
+            v = V(ts(T.ZVb[:, :], T.RIl[:, :], kc(10), A.mult))
+            V(cpy(T.ZA[:, :].indirect(T.SN[:, 0:12]), T.ZVa[:, :]), v, gz)
+            vZ = V(cpy(T.ZB[:, :].indirect(T.SN[:, 0:12]), T.ZVb[:, :]))
+        if t == 3:
+            vV = V(tt(T.VAL[:, :], T.pZ[:, :], T.P2[:, :], A.add), pz, tP2)
+            dma("y", T.stV[:], T.VAL[:, :], "dV", vV)
+            tV = dma("y", T.landV[me], T.VAL[lo:hi, :], "dV")
+            send("stV", "landV", "arrV", tV)
+        v = V(tt(T.T1[:, :], T.KB[:, 0::2], T.KB[:, 1::2], A.max), sa, sb)
+        v = V(tt(T.T2[:, :], T.T1[:, 0::2], T.T1[:, 1::2], A.max), v)
+        v = V(tt(T.T3[:, :], T.T2[:, 0::2], T.T2[:, 1::2], A.max), v)
+        vb = V(tt(T.BEST[:, :], T.T3[:, 0::2], T.T3[:, 1::2], A.max), v)
+        vi = V(tt(T.BI[:, :], T.T3[:, 0::2], T.T3[:, 1::2], A.max))
+        w = float(2 ** 21) - 0.5
+        V(ts(T.BW[:, :], T.BEST[:, 0:8], w, A.max), vb)
+        V(ts(T.Bm[0:64, 0:4], T.BEST[0:64, 8:12], w, A.max))
+        v = V(ts(T.Bm[64:128, 4:8], T.BEST[64:128, 8:12], w, A.max))
+        m = MM([v], (T.pTR[0:8, 0:128], T.BW[:, :], T.IDf[:, :], True, True),
+               (T.pTR[0:8, 128:192], T.Bm[:, :], T.I64s[:, :], True, True))
+        sT = S(act(T.bT[:, :], T.pTR[0:8, 0:192]), m)
+        pR = MM([sT], (T.pTR[:, 192:384], T.REP8[:, :], T.bT[:, :], True, True))
+        V(ts(T.UI[:, 0:12], T.BI[:, :], 10, A.arith_shift_right, 63, A.bitwise_and), vi)
+        V(ts(T.UI[:, 12:24], T.BI[:, :], 4, A.arith_shift_right, 63, A.bitwise_and))
+        v = V(ts(T.C2[:, :], T.BI[:, :], 22, A.arith_shift_right))
+        V(cpy(T.UF[:, :], T.UI[:, :]), v)
+        v = V(ts(T.OK[:, :], T.C2[:, :], 0.0, A.is_equal))
+        ms = [(T.pD[0:64, 0:64], T.ID64[:, :], T.D[:, :], True, False)]
+        if t == 0:
+            ms += [(T.pD[0:64, 0:64], T.SHI[:, 64 * c:64 * c + 64], T.SLO[:, 64 * c:64 * c + 64], False, False) for c in range(12)]
+        MM([vD1, vS], *ms)
+        for c in range(12):
+            V(ts(T.OHI[:, 64 * c:64 * c + 64], T.iotR[:, :], T.UF[:, c:c + 1], A.is_equal, T.OK[:, c:c + 1], A.mult), v)
+            x = V(ts(T.OLO[:, 64 * c:64 * c + 64], T.iotR[:, :], T.UF[:, 12 + c:13 + c], A.is_equal))
+            pd = MM([x], (T.pD[0:64, 0:64], T.OHI[:, 64 * c:64 * c + 64], T.OLO[:, 64 * c:64 * c + 64], False, c == 11))
+        vD1 = S(act(T.D[:, :], T.pD[0:64, 0:64], AF.Sign), pd)
+        if t < 4:
+            tF = flags_to_F(vD1)
+        v = V(tt(T.W[:, :], T.pTR[:, 192:384], T.KEY[:, :], A.is_equal), pR)
+        v = V(tt(T.W[:, :], T.W[:, :], T.Dg[:, :], A.mult), v)
+        vTk = V(lambda e: e.tensor_tensor(T.Tk[:, :].indirect(at), T.Hf[:, :], T.W[:, :], A.add), v)
+        if t in (1, 2):
+            pz = zmm(t - 1)
+    dma("y", T.stD[:], T.D[:, :], "dD", vD1)
+    tD = dma("y", T.landD[me], T.D[8 * me:8 * me + 8, :], "dD")
+    tY = dma("y", T.stY[:], T.Tk[:, :], "dY", vTk)
+    dma("s", T.yt[lo:hi, :], T.Tk[lo:hi, :], "oY1", vTk)
+    send("stD", "landD", "arrD", tD)
+    send("stY", "landY", "arrY", tY)
+    tVR = dma("y", T.VR[:, :], T.landV[:], "dVR", ("arrV", 14), tV)
+    tKD = dma("y", T.KD[:, :], T.landD[:], "dKD", ("arrD", 14), tD)
+    m = MM([tKD], (T.pZ[:, :], T.R8b[:, :], T.KD[:, :], True, True))
+    v = V(tt(T.YP[:, :], T.pZ[:, :], T.VR[:, :], A.max), m, tVR)
+    dma("y", T.yp[:], T.YP[:, :], "oP", v)
+    need("s", [("arrY", 14)])
+    if me > 0:
+        dma("s", T.yt[0:lo, :], T.landY[0:me], "oY2")
+    if me < 7:
+        dma("s", T.yt[hi:128, :], T.landY[me + 1:8], "oY2")
+    need("g", [(s, n) for s, n in cnt.items() if n])

@@ -2,7 +2,7 @@ from concourse.bass import DstId, RemoteDMATransfer
 from concourse.mybir import AluOpType, ActivationFunctionType
 
 RO = 5
-F32, BF, I32, U16 = "float32", "bfloat16", "int32", "uint16"
+F32, BF, FH, I32, U16 = "float32", "bfloat16", "float16", "int32", "uint16"
 SCRATCH = {}
 
 
@@ -11,30 +11,28 @@ def _b(where, dtype, **kw):
         SCRATCH[k] = (where, s, dtype)
 
 
-_b("dram", I32, stR=[8, 128, 24], stC=[8, 128, 2], stT=[8, 128, 64], landR=[8, 128, 24], landC=[8, 128, 2], landT=[8, 128, 64])
+_b("dram", I32, stR=[8, 128, 32], stT=[8, 128, 64], landR=[8, 128, 32], landT=[8, 128, 64])
 _b("dram", F32, stV=[8, 128, 64], landV=[8, 128, 64], stY=[8, 128, 64], landY=[8, 128, 64])
 _b("dram", BF, stD=[8, 128, 4], landD=[8, 128, 4])
-_b("sbuf", I32, P=[128, 4096], XP=[64, 1024], P2=[128, 512], ii=[128, 192], col=[128, 256], cp=[128, 1], ci=[128, 4],
-   cq8=[128, 256], iia=[128, 192], cola=[128, 192], t12b=[128, 12], Cl=[128, 12], Cti=[128, 12], R=[128, 192],
-   OT=[128, 60], Tki=[128, 512], BI=[128, 12], UI=[128, 24], C2=[128, 12], NI=[128, 12], NI2=[128, 24], RI=[128, 192],
-   RIh=[128, 192], RIl=[128, 192], ccq=[128, 128])
-_b("sbuf", U16, LI=[128, 12], LB=[128, 12], AT=[128, 60], SN=[128, 60], H16=[128, 192])
-_b("sbuf", F32, KC=[128, 16], IDf=[128, 128], I64s=[128, 64], REPf=[128, 256], SELq=[128, 16], EM=[128, 192], DM=[128, 192],
-   REP8=[8, 128], Clf=[128, 12], Cs=[128, 12], Ctf=[128, 12], E=[128, 192], Es=[128, 192], Et=[128, 192],
-   SG=[128, 960], TH=[128, 960], RJ=[128, 960], RA=[128, 3072], RB=[128, 3072], Tk=[128, 512], Hf=[128, 192],
-   Dg=[128, 192], M=[128, 192], A1=[128, 192], KEY=[128, 192], KB=[128, 192], T1=[128, 96], T2=[128, 48], T3=[128, 24],
-   BEST=[128, 12], BW=[128, 8], Bm=[128, 8], bT=[8, 192], W=[128, 192], UF=[128, 24], OK=[128, 12], NF=[128, 24],
-   S0=[128, 192], S1=[128, 96], S2=[128, 48], S3=[128, 24], S4=[128, 12], VAL=[128, 512], VR=[128, 512], YP=[128, 512])
-_b("sbuf", BF, iot=[128, 64], iotR=[128, 64], WST=[128, 144], W0=[128, 144], DW=[128, 2048], OUTW=[128, 128], YS=[128, 240],
-   YS64=[128, 240], R8b=[8, 128], ID64=[64, 64], F=[128, 4096], ZA=[128, 4096], ZB=[128, 4096], EQ=[128, 3072], FG=[128, 3072],
-   FS=[128, 192], OHI=[128, 768], OLO=[128, 768], SHI=[128, 768], SLO=[128, 768], D=[64, 64], ZVa=[128, 192], ZVb=[128, 192],
-   KD=[8, 512])
-_b("psum", F32, KPa=[128, 512], KPb=[128, 512], pBa=[128, 512], pBb=[128, 512], pTR=[128, 512], pD=[128, 512], pM=[128, 512],
-   pZ=[128, 512])
+_b("sbuf", I32, P2=[128, 512], ii=[128, 192], col=[128, 272], cp=[128, 1], ci=[128, 4], cq8=[128, 256], iia=[128, 192],
+   cola=[128, 192], t12b=[128, 12], seg=[128, 272], slot=[128, 272], Cl=[128, 12], Cti=[128, 12], R=[128, 192], OT=[128, 60],
+   Tki=[128, 512], BI=[128, 12], UI=[128, 36], FI=[128, 12], F5=[128, 12])
+_b("sbuf", U16, LI=[128, 12], LB=[128, 12], LC=[128, 12], AT=[128, 60], SN=[128, 60], H16=[128, 192])
+_b("sbuf", F32, P=[128, 4096], KC=[128, 24], IN=[128, 128], IJ=[128, 136], REPf=[128, 256], R0=[128, 272], EM=[128, 192],
+   DM=[128, 192], SM=[128, 192], C15=[128, 192], INC=[128, 204], SH1=[128, 128], Clf=[128, 12], Ctf=[128, 12], E=[128, 192],
+   RJ=[128, 192], RR0=[128, 3072], RR1=[128, 3072], RR2=[128, 3072], RR3=[128, 3072], RR4=[128, 3072], Tk=[128, 512],
+   Hf=[128, 192], Dg=[128, 192], WD=[128, 192], AS=[128, 204], XS=[128, 204], UF=[128, 24], S0=[128, 192], S1=[128, 192],
+   VAL=[128, 512], VR=[128, 512], YP=[128, 512])
+_b("sbuf", FH, P2h=[128, 512], GY=[128, 1024], Ih=[128, 128])
+_b("sbuf", BF, iotA=[128, 32], iotB=[128, 128], SelF=[128, 8], SelE=[128, 8], Ib=[128, 128], IM=[128, 128], RS=[128, 272],
+   NEG=[128, 128], C16=[128, 204], C4=[128, 36], SH2=[128, 128], YS=[128, 240], R8b=[8, 128], Et=[128, 192], N0=[128, 512],
+   N1=[128, 512], hib=[128, 192], ZV=[128, 192], F=[128, 4096], Z=[128, 4096], EQ=[128, 3072], FG=[128, 3072], FS=[128, 192],
+   M=[128, 204], Wt=[128, 192], TA=[128, 384], OA=[128, 384], OB=[128, 1536], D=[32, 128], KD=[8, 512])
+_BANKS = ["pA", "pX", "pM", "pG", "pW", "pD", "pZ", "pE"]
+_b("psum", F32, **{k: [128, 512] for k in _BANKS})
 
-_ARR = ["arrR", "arrC", "arrT", "arrV", "arrY", "arrD"]
-_DMA = ["dR", "dC", "dT", "dP", "dX", "dP2", "dF", "dCl", "dRl", "dO", "dTk", "dRR", "dRJ", "dSN", "dV", "dVR", "dY", "dD", "dKD",
-        "oY1", "oY2", "oP"]
+_ARR = ["arrR", "arrT", "arrV", "arrY", "arrD"]
+_DMA = ["dR", "dT", "dP2", "dF", "dCl", "dRl", "dO", "dTk", "dRR0", "dRR1", "dRR2", "dRR3", "dSN", "dV", "dVR", "dY", "dD", "dKD", "oY1", "oY2", "oP"]
 SEMAPHORES = ["cv", "cs", "cpe", "cg", "sent"] + _ARR + _DMA
 
 
@@ -97,8 +95,14 @@ def rank_program(g, core, T, topo):
     def cpy(out, in_):
         return lambda e: e.tensor_copy(out, in_)
 
-    def act(out, in_, f=AF.Copy):
-        return lambda e: e.activation(out, in_, f)
+    def act(out, in_, f=AF.Copy, **kw):
+        return lambda e: e.activation(out, in_, f, **kw)
+
+    def scan(out, d0, d1, o0, o1):
+        return lambda e: e.tensor_tensor_scan(out, d0, d1, 0.0, o0, o1)
+
+    def fill(out, x):
+        return lambda e: e.memset(out, x)
 
     def send(src, dst, sem, *deps):
         need("g", deps)
@@ -116,278 +120,234 @@ def rank_program(g, core, T, topo):
         cnt[sem] += 14
 
     lo, hi = 16 * me, 16 * me + 16
-    dma("y", T.stC[:, 0:96, :], T.calls[:], "dC")
-    dma("y", T.stC[:, 96:128, :], T.trunk[0:1, :], "dC")
-    tC = dma("y", T.landC[me, 0:96, :], T.calls[lo:hi, :], "dC")
-    dma("y", T.stR[:], T.routes[:], "dR")
-    tR = dma("y", T.landR[me], T.routes[lo:hi, :], "dR")
+    dma("y", T.stR[:, 0:96, :], T.routes[:], "dR")
+    dma("s", T.stR[:, 96:102, :], T.calls[:], "dR")
+    dma("s", T.stR[:, 102:128, :], T.trunk[0:13, :], "dR")
+    dma("y", T.landR[me, 0:96, :], T.routes[lo:hi, :], "dR")
+    tR = dma("s", T.landR[me, 96:102, :], T.calls[lo:hi, :], "dR")
     dma("y", T.stT[:], T.trunk[:], "dT")
     tT = dma("y", T.landT[me], T.trunk[lo:hi, :], "dT")
     for q in range(8):
-        tP = dma("s", T.P[16 * q:16 * q + 16, :], T.paths[lo:hi, :], "dP")
-    for k in range(16):
-        tX = dma("y", T.XP[:, 64 * k:64 * k + 64], T.paths[lo + k:lo + k + 1, :], "dX")
-    for q in range(8):
         tP2 = dma("s", T.P2[16 * q:16 * q + 16, :], T.paths[lo:hi, 512 * q:512 * q + 512], "dP2")
     g1 = op("g", lambda e: e.iota(T.cp[:, 0:1], [[0, 1]], 0, 1))
-    g2 = op("g", lambda e: e.iota(T.col[:, :], [[1, 256]], 0, 0))
+    g2 = op("g", lambda e: e.iota(T.col[:, :], [[1, 272]], 0, 0))
     g3 = op("g", lambda e: e.iota(T.ii[:, :], [[1, 12], [12, 16]], 0, 0))
-    send("stC", "landC", "arrC", tC)
+    g4 = op("g", lambda e: e.iota(T.seg[:, :], [[0, 2], [1, 8], [0, 17]], 0, 0))
+    g5 = op("g", lambda e: e.iota(T.slot[:, :], [[0, 16], [1, 17]], 0, 0))
     send("stR", "landR", "arrR", tR)
     send("stT", "landT", "arrT", tT)
-    gz = op("g", lambda e: e.iota(T.ZA[:, :], [[0, 4096]], 0, 0, allow_small_or_imprecise_dtypes=True))
-    gz = op("g", lambda e: e.iota(T.ZB[:, :], [[0, 4096]], 0, 0, allow_small_or_imprecise_dtypes=True))
 
-    vF = V(lambda e: e.memset(T.F[:, :], 0.0))
-    V(lambda e: e.memset(T.Bm[:, :], 0.0))
+    vF = V(fill(T.F[:, :], 0.0))
     KC, col, ci = T.KC, T.col, T.ci
 
     def kc(n):
         return KC[:, n:n + 1]
     V(ts(ci[:, 0:1], T.cp[:, 0:1], 15, A.bitwise_and), g1)
     V(ts(ci[:, 1:2], T.cp[:, 0:1], 4, A.arith_shift_right))
-    V(ts(ci[:, 2:3], T.cp[:, 0:1], 63, A.bitwise_and))
     V(cpy(kc(0), T.cp[:, 0:1]))
-    v = V(ts(T.cq8[:, :], col[:, :], 4, A.arith_shift_right, 7, A.bitwise_and), g2)
-    V(ts(T.cola[:, :], col[:, 0:192], 15, A.bitwise_and))
-    V(ts(T.iia[:, :], T.ii[:, :], 15, A.bitwise_and), g3)
-    V(ts(T.ccq[:, 0:16], col[:, 0:16], 7, A.bitwise_and))
+    v = V(ts(T.cola[:, :], col[:, 0:192], 15, A.bitwise_and), g2)
     V(cpy(kc(1), ci[:, 0:1]), v)
-    V(cpy(kc(2), ci[:, 1:2]))
-    V(cpy(kc(7), ci[:, 2:3]))
-    V(ts(kc(3), ci[:, 1:2], 512.0, A.mult))
-    V(ts(kc(4), ci[:, 1:2], 16.0, A.mult, 15.0, A.add))
-    V(ts(kc(8), ci[:, 0:1], 112.0, A.add))
-    V(ts(kc(9), ci[:, 0:1], -1.0, A.mult, float(2 ** 21 + 15), A.add))
-    V(ts(kc(10), ci[:, 0:1], 5.0, A.is_lt))
-    V(ts(kc(11), ci[:, 0:1], 0.0, A.is_equal))
-    V(ts(kc(12), ci[:, 1:2], 16.0, A.mult, 16.0, A.add))
-    V(ts(kc(14), ci[:, 0:1], 12.0, A.mult))
-    v = V(ts(kc(13), ci[:, 1:2], 1.0, A.add))
-    V(tt(kc(12), kc(12), kc(11), A.mult), v)
-    v = V(tt(kc(13), kc(13), kc(11), A.mult))
-    V(ts(kc(5), kc(12), -1.0, A.add), v)
-    v = V(ts(kc(6), kc(13), -1.0, A.add))
-    V(ts(T.WST[:, :], col[:, 0:144], kc(4), A.is_equal, 65536.0, A.mult), v)
-    V(ts(T.W0[:, :], col[:, 0:144], kc(5), A.is_equal))
-    v = V(ts(T.t12b[:, :], col[:, 0:12], kc(14), A.add))
-    V(cpy(T.LI[:, :], T.t12b[:, :]), v)
-    v = V(ts(T.Cti[:, :], T.t12b[:, :], 4, A.arith_shift_right))
-    vLB = V(cpy(T.LB[:, :], T.Cti[:, :]), v)
-    V(ts(T.IDf[:, :], col[:, 0:128], kc(0), A.is_equal))
-    V(ts(T.ID64[:, :], col[0:64, 0:64], KC[0:64, 0:1], A.is_equal))
-    V(ts(T.I64s[:, :], col[:, 0:64], kc(7), A.is_equal))
-    V(ts(T.REPf[:, :], T.cq8[:, :], kc(2), A.is_equal))
-    V(ts(T.SELq[:, :], T.ccq[:, 0:16], kc(2), A.is_equal))
-    V(ts(T.EM[:, :], T.iia[:, :], kc(1), A.is_equal))
-    V(ts(T.DM[:, :], T.cola[:, :], kc(1), A.is_equal))
-    V(ts(T.REP8[:, :], T.cq8[0:8, 0:128], KC[0:8, 0:1], A.is_equal))
-    V(ts(T.R8b[:, :], T.cq8[0:8, 0:128], KC[0:8, 0:1], A.is_equal, 4096.0, A.mult))
-    V(ts(T.OUTW[:, :], T.cq8[:, 0:128], kc(6), A.is_equal, -float(2 ** 27), A.mult))
-    V(ts(T.YS[:, :], col[:, 0:240], kc(8), A.is_equal))
-    V(ts(T.YS64[:, :], col[:, 0:240], kc(8), A.is_equal, 64.0, A.mult))
-    V(cpy(T.iot[:, :], col[:, 0:64]))
-    V(ts(T.iotR[:, :], col[:, 0:64], -1.0, A.mult, 63.0, A.add))
-    for p in range(16):
-        vC = V(ts(T.DW[:, 128 * p:128 * p + 128], T.W0[:, 15 - p:143 - p], float(2 ** 22 * (16 - p)), A.mult))
-    v, n = tX, 512
-    while n >= 64:
-        v = V(tt(T.XP[:, 0:n], T.XP[:, 0:n], T.XP[:, n:2 * n], A.min), v)
-        n //= 2
-    vD = V(ts(T.D[:, :], T.XP[:, 0:64], 4096.0, A.is_ge), v)
+    v = V(cpy(kc(2), ci[:, 1:2]))
+    V(ts(T.DM[:, :], T.cola[:, :], kc(1), A.is_equal), v)
+    v = V(ts(KC[:, 16:24], col[:, 0:8], kc(2), A.is_equal))
+    for y in range(8):
+        V(ts(T.GY[:, 128 * y:128 * y + 128], T.DM[:, 0:128], kc(16 + y), A.mult), v)
+    V(ts(kc(3), ci[:, 1:2], 4.0, A.mult, 3.0, A.add))
+    vPh = V(ts(T.P2h[:, :], T.P2[:, :], -2048.0, A.add), tP2)
+    for y in range(8):
+        m = MM([vPh], (T[_BANKS[y]][:, :], T.GY[:, 128 * y:128 * y + 128], T.P2h[:, :], True, True))
+        tP = S(act(T.P[:, 512 * y:512 * y + 512], T[_BANKS[y]][:, :], AF.Identity, bias=-2048.0), m)
+    V(ts(T.C4[:, :], col[:, 0:36], kc(3), A.is_equal), vPh)
+    vN0 = V(ts(T.N0[:, :], T.P2[:, :], 4096.0, A.is_ge))
 
-    def flags_to_F(tok):
+    def count_none(n, last):
+        return [(T.pD[0:32, 0:128], T.C4[:, 3 - u:35 - u], n[:, 128 * u:128 * u + 128], u == 0, last and u == 3) for u in range(4)]
+    m = MM([vN0, tP], *count_none(T.N0, True))
+    vD = S(act(T.D[:, :], T.pD[0:32, 0:128], AF.Sign, bias=-15.5), m)
+
+    def flags_to_F(*tok):
         for q in range(8):
-            t = dma("y", T.F[16 * q:16 * q + 1, :], T.D[:, :], "dF", tok)
+            t = dma("ys"[q % 2], T.F[16 * q:16 * q + 1, :], T.D[:, :], "dF", *tok)
         return t
-    need("y", [("arrC", 14), tC])
-    tCl = dma("y", T.Cl[:, :], T.landC[:, 0:96, :], "dCl")
+    vZ0 = V(fill(T.Z[:, :], 0.0))
+    V(ts(T.cq8[:, :], col[:, 0:256], 4, A.arith_shift_right, 7, A.bitwise_and))
+    V(ts(T.iia[:, :], T.ii[:, :], 15, A.bitwise_and), g3)
+    V(ts(kc(4), ci[:, 0:1], 12.0, A.mult))
+    V(ts(kc(5), ci[:, 1:2], 512.0, A.mult))
+    V(ts(kc(6), ci[:, 0:1], 0.0, A.is_equal, 1024.0, A.mult))
+    V(ts(kc(7), ci[:, 0:1], 5.0, A.is_lt))
+    V(ts(kc(8), ci[:, 0:1], 5.0, A.is_ge, -5.0, A.mult))
+    V(ts(kc(9), T.cp[:, 0:1], 5.0, A.add))
+    V(ts(kc(10), T.cp[:, 0:1], 0.0, A.is_equal, 16.0, A.mult))
+    v = V(ts(kc(11), T.cp[:, 0:1], kc(2), A.add, 1.0, A.add))
+    V(ts(T.t12b[:, :], col[:, 0:12], kc(4), A.add), v)
+    V(ts(kc(12), ci[:, 0:1], kc(8), A.add, 112.0, A.add))
+    V(ts(T.EM[:, :], T.iia[:, :], kc(1), A.is_equal))
+    v = V(ts(T.REPf[:, :], T.cq8[:, :], kc(2), A.is_equal))
+    V(cpy(T.LI[:, :], T.t12b[:, :]), v)
+    V(cpy(T.LC[:, :], col[:, 0:12]))
+    v = V(ts(T.Cti[:, :], T.t12b[:, :], 4, A.arith_shift_right))
+    V(ts(T.SH1[:, :], col[:, 0:128], kc(9), A.is_equal, kc(7), A.mult))
+    V(ts(T.S0[:, 0:128], col[:, 0:128], kc(0), A.is_equal, kc(7), A.mult))
+    V(ts(T.SM[:, :], T.cola[:, :], 0.0, A.not_equal))
+    v = V(cpy(T.LB[:, :], T.Cti[:, :]), v)
+    V(tt(T.SH2[:, :], T.S0[:, 0:128], T.SH1[:, :], A.subtract), v)
+    V(ts(T.YS[:, :], col[:, 0:240], kc(12), A.is_equal))
+    V(ts(T.Ih[:, :], col[:, 0:128], kc(0), A.is_equal))
+    V(ts(T.IN[:, :], col[:, 0:128], kc(0), A.is_equal, -1.0, A.mult))
+    V(ts(T.IJ[:, :], col[:, 0:136], kc(11), A.is_equal, -32.0, A.mult))
+    V(ts(T.Ib[:, :], col[:, 0:128], kc(0), A.is_equal))
+    V(ts(T.IM[:, :], col[:, 0:128], kc(0), A.is_equal, float(2 ** 22), A.mult))
+    V(ts(T.SelF[:, :], col[:, 0:8], kc(2), A.is_equal, kc(6), A.mult))
+    V(ts(T.SelE[:, :], col[:, 0:8], kc(2), A.is_equal, float(2 ** 17), A.mult))
+    V(fill(T.NEG[:, :], -1.0))
+    V(ts(T.C16[:, :], T.slot[:, 0:204], 0.0, A.not_equal, kc(10), A.mult), g5)
+    V(ts(T.INC[:, :], T.slot[:, 0:204], 0.0, A.is_equal, -float(2 ** 24), A.mult))
+    V(fill(T.R0[:, :], 0.0))
+    v = V(ts(T.RS[:, :], T.seg[:, :], kc(2), A.is_equal, 32.0, A.mult), g4)
+    V(ts(T.R0[:, 0::17], T.seg[:, 0::17], kc(2), A.is_equal, -32.0, A.mult), v)
+    V(fill(T.RS[:, 0::17], 0.0))
+    V(ts(T.INC[:, :], T.INC[:, :], 1.0, A.add))
+    V(ts(T.C15[:, :], T.cola[:, :], -1.0, A.mult, 15.0, A.add))
+    V(ts(T.iotA[:, :], col[:, 0:32], -1.0, A.mult, 31.0, A.add))
+    V(ts(T.iotB[:, :], col[:, 0:128], -1.0, A.mult, 127.0, A.add))
+    vC = V(ts(T.R8b[:, :], T.cq8[0:8, 0:128], KC[0:8, 0:1], A.is_equal, 4096.0, A.mult))
+
     need("y", [("arrR", 14), tR])
-    tRl = dma("y", T.R[:, :], T.landR[:], "dRl")
+    tRl = dma("y", T.R[:, :], T.landR[:, 0:96, :], "dRl")
+    tCl = dma("y", T.Cl[:, :], T.landR[:, 96:102, :], "dCl")
     for t in range(RO):
-        tO = dma("y", T.OT[16 * t:128, 12 * t:12 * t + 12], T.landR[0:8 - t, 8 * t:8 * t + 8, :], "dO")
+        tO = dma("y", T.OT[16 * t:128, 12 * t:12 * t + 12], T.landR[0:8 - t, 6 * t:6 * t + 6, :], "dO")
         if t:
-            tO = dma("y", T.OT[0:16 * t, 12 * t:12 * t + 12], T.landR[8 - t:8, 8 * t:8 * t + 8, :], "dO")
+            tO = dma("y", T.OT[0:16 * t, 12 * t:12 * t + 12], T.landR[8 - t:8, 6 * t:6 * t + 6, :], "dO")
     need("y", [("arrT", 14), tT])
     tTk = dma("y", T.Tki[:, :], T.landT[:], "dTk")
-    tF = flags_to_F(vD)
-
-    v = V(cpy(T.Clf[:, :], T.Cl[:, :]), tCl, vC, vLB)
-    V(ts(T.Cti[:, :], T.Cl[:, :], 3584, A.bitwise_and))
-    v = V(ts(T.Cs[:, :], T.Cl[:, :], -16.0, A.mult, 65520.0, A.add))
-    V(cpy(T.Ctf[:, :], T.Cti[:, :]), v)
-    vE = V(tt(T.E[:, :], T.Clf[:, :].indirect(T.LB[:, :]), T.EM[:, :], A.mult))
-    V(tt(T.Es[:, :], T.Cs[:, :].indirect(T.LB[:, :]), T.EM[:, :], A.mult))
-    vE = V(tt(T.Et[:, :], T.Ctf[:, :].indirect(T.LB[:, :]), T.EM[:, :], A.mult), vE)
-    vRJ = V(cpy(T.RJ[:, 0:192], T.R[:, :].indirect(T.LI[:, :])), tRl)
-    pn = MM([vE], (T.pBa[:, 0:8], T.E[:, 0:128], T.SELq[:, 8:16], True, True),
-            (T.pBa[0:64, 8:12], T.E[:, 128:192], T.SELq[:, 8:12], True, True),
-            (T.pBa[64:128, 8:12], T.E[:, 128:192], T.SELq[:, 12:16], True, True))
+    tF = flags_to_F(vD, vF)
 
     def rep(t):
         return T.REPf[:, 16 * (8 - t):16 * (16 - t)]
-    sprep = [None] * RO
-
-    def prep(t):
-        m = MM([vE, sprep[t - 1] if t else None], (T.pM[:, 0:192], rep(t), T.E[:, :], True, True),
-               (T.pM[:, 192:384], rep(t), T.Et[:, :], True, True))
-        S(act(T.SG[:, 192 * t:192 * t + 192], T.pM[:, 0:192]), m)
-        sprep[t] = S(act(T.TH[:, 192 * t:192 * t + 192], T.pM[:, 192:384]))
-
-    rr = [None] * RO
-    RRb = [T.RA, T.RB]
-    for p in range(8):
-        a = V(cpy(T.RA[:, p::16], T.RJ[:, 0:192]), vRJ)
-        b = S(act(T.RA[:, 8 + p::16], T.RJ[:, 0:192]), vRJ)
-    rr[0] = [a, b]
-    prep(0)
-    vNI = V(cpy(T.NI[:, :], T.pBa[:, 0:12]), pn)
-    vAT = V(ts(T.AT[:, :], T.OT[:, :], kc(3), A.subtract), tO)
+    vRJ = V(ts(T.RJ[:, :], T.R[:, :].indirect(T.LI[:, :]), -4096.0, A.add), tRl, vC)
+    v = V(cpy(T.Clf[:, :], T.Cl[:, :]), tCl)
+    V(ts(T.Cti[:, :], T.Cl[:, :], 3584, A.bitwise_and))
+    v = V(tt(T.E[:, :], T.Clf[:, :].indirect(T.LB[:, :]), T.EM[:, :], A.mult), v)
+    pS = MM([v, tP], (T.pE[:, 0:192], rep(0), T.E[:, :], True, True))
+    v = V(cpy(T.Ctf[:, :], T.Cti[:, :]), v)
+    vE = V(tt(T.Et[:, :], T.Ctf[:, :].indirect(T.LB[:, :]), T.EM[:, :], A.mult), v)
+    s = S(act(T.hib[:, :], T.RJ[:, :]), vRJ)
+    m = MM([s], (T.pW[:, 0:192], T.SH1[:, :], T.RJ[:, :], True, False), (T.pW[:, 0:192], T.SH2[:, :], T.hib[:, :], False, True))
+    RR = [T["RR%d" % t] for t in range(RO)]
+    for p in range(11):
+        b = S(act(T.RR0[:, p::16], T.RJ[:, :]), vRJ)
+        if p == 3:
+            sZV = S(act(T.ZV[:, :], T.pW[:, 0:192]), m)
+    v = V(tt(T.S0[:, :], T.pE[:, 0:192], T.DM[:, :], A.mult), pS)
+    v = V(scan(T.S1[:, :], T.SM[:, :], T.S0[:, :], A.mult, A.add), v)
+    vSN = V(cpy(T.SN[:, 0:12], T.S1[:, 15::16]), v)
+    for u in range(1, RO):
+        dma("y", T.SN[16 * u:128, 12 * u:12 * u + 12], T.SN[0:128 - 16 * u, 0:12], "dSN", vSN)
+        tSN = dma("y", T.SN[0:16 * u, 12 * u:12 * u + 12], T.SN[128 - 16 * u:128, 0:12], "dSN")
+    for p in range(11, 16):
+        a = V(cpy(T.RR0[:, p::16], T.RJ[:, :]), vRJ)
+    rr = [[a, b]] + [None] * 4
+    vZ = V(cpy(T.Z[:, :].indirect(T.SN[:, 0:12]), T.ZV[:, :]), sZV, vSN, vZ0)
+    pz = MM([vZ], (T.pZ[:, :], T.Ih[:, :], T.P2h[:, :], True, False),
+            *[(T.pZ[:, :], T.YS[:, 112 - 16 * q:240 - 16 * q], T.Z[:, 512 * q:512 * q + 512], False, q == 7) for q in range(8)])
+    vAT = V(ts(T.AT[:, :], T.OT[:, :], kc(5), A.subtract), tO)
     vTk = V(cpy(T.Tk[:, :], T.Tki[:, :]), tTk)
-    dma("y", T.RB[16:128, :], T.RA[0:112, :], "dRR", *rr[0])
-    rr[1] = [dma("y", T.RB[0:16, :], T.RA[112:128, :], "dRR")]
-    for t in (2, 3, 4):
-        dma("y", T.RJ[16 * t:128, 192 * t:192 * t + 192], T.RJ[0:128 - 16 * t, 0:192], "dRJ", vRJ)
-        tRJ = dma("y", T.RJ[0:16 * t, 192 * t:192 * t + 192], T.RJ[128 - 16 * t:128, 0:192], "dRJ")
-    tSN = None
-    vD1 = vD
 
-    def zmm(half):
-        z, w = (T.ZA, T.YS64) if half == 0 else (T.ZB, T.YS)
-        return MM([vZ], *[(T.pZ[:, :], w[:, 112 - 16 * q:240 - 16 * q], z[:, 512 * q:512 * q + 512], half == 0 and q == 0,
-                          half == 1 and q == 7) for q in range(8)])
+    def to_seekers(out, l, w, o, last):
+        return [(out[0:64, 136:204], l[:, 128:192], w[:, o:o + 68], False, False),
+                (out[64:128, 136:204], l[:, 128:192], w[:, o + 68:o + 136], False, False),
+                (out[:, 0:136], l[:, 0:128], w[:, o:o + 136], False, last)]
+
+    def slots(out, tab, sel, s, part, alone, last=False):
+        if part == 0:
+            return [(out[:, s:136:17], tab[0], sel[:, 0:8], alone, alone or last)]
+        return [(out[0:64, 136 + s:204:17], tab[1], sel[:, 0:4], alone, alone),
+                (out[64:128, 136 + s:204:17], tab[1], sel[:, 4:8], alone, alone)]
+
+    def trunks(out, tab, sel, part, alone):
+        return [m for p in range(16) for m in slots(out, (tab[:, p:2048:16], tab[:, 2048 + p:3072:16]), sel, 1 + p, part, alone, p == 15)]
 
     for t in range(RO):
         at = T.AT[:, 12 * t:12 * t + 12]
-        RR = RRb[t % 2]
-        SGt, THt = T.SG[:, 192 * t:192 * t + 192], T.TH[:, 192 * t:192 * t + 192]
         h16 = V(cpy(T.H16[:, :], T.Tk[:, :].indirect(at)), vTk, vAT)
         hf = S(act(T.Hf[:, :], T.Tk[:, :].indirect(at)), vTk, vAT)
-
-        def eq(c):
-            return V(tt(T.EQ[:, 1024 * c:1024 * c + 1024], T.P[:, :].indirect(T.H16[:, 64 * c:64 * c + 64]),
-                        RR[:, 1024 * c:1024 * c + 1024], A.is_equal), h16, tP, *rr[t])
-
-        def fg(q, c):
-            o, w = T.FG[:, 1024 * c:1024 * c + 1024], T.F[:, :].indirect(T.H16[:, 64 * c:64 * c + 64])
-            return op(q, act(o, w) if q == "s" else cpy(o, w), h16, tF, vF)
         if t < 4:
-            prep(t + 1)
-        if 1 <= t < 4:
-            for p in range(16):
-                x = S(act(RRb[(t + 1) % 2][:, p::16], T.RJ[:, 192 * (t + 1):192 * (t + 2)]), tRJ, *rr[t])
-            rr[t + 1] = [x]
-        e0 = eq(0)
-        v = V(tt(T.Dg[:, :], SGt, T.Hf[:, :], A.subtract), hf, sprep[t])
-        vM = V(tt(T.M[:, :], T.Hf[:, :], THt, A.is_lt))
-        e1 = eq(1)
-        sA = S(lambda e: e.activation(T.A1[:, :], T.Dg[:, :], AF.Identity, bias=kc(9), scale=16.0), v)
-        f0 = fg("s", 0)
-        f1 = fg("s", 1)
+            n = 16 * (t + 1)
+            dma("y", RR[t + 1][n:128, :], T.RR0[0:128 - n, :], "dRR%d" % t, tF, *rr[0])
+            rr[t + 1] = [dma("y", RR[t + 1][0:n, :], T.RR0[128 - n:128, :], "dRR%d" % t)]
+        o = 17 * (8 - t)
+        pm = MM([hf, vE], (T.pM[:, 0:204], T.NEG[:, :], T.C16[:, :], True, False),
+                *(to_seekers(T.pM, T.Et, T.RS, o, False) + to_seekers(T.pM, T.Hf, T.IJ, 0, True)))
+        sM = S(act(T.M[:, :], T.pM[:, 0:204], AF.Sign), pm)
+        pg = MM([], (T.pG[:, 0:192], rep(t), T.E[:, :], True, False), (T.pG[:, 0:192], T.IN[:, :], T.Hf[:, :], False, True))
+        MM([sM], (T.pA[:, 0:204], T.IM[:, :], T.M[:, :], True, False),
+           *(to_seekers(T.pA, T.Hf, T.IJ, 0, False) + to_seekers(T.pA, T.E, T.R0, o, False)))
+
+        def eq(a, b):
+            return V(tt(T.EQ[:, 16 * a:16 * b], T.P[:, :].indirect(T.H16[:, a:b]), RR[t][:, 16 * a:16 * b], A.is_equal), h16, tP, *rr[t])
+
+        def fg(a, b):
+            return S(act(T.FG[:, 16 * a:16 * b], T.F[:, :].indirect(T.H16[:, a:b])), h16, tF)
+        e1 = eq(128, 192)
+        e0 = eq(0, 128)
         if t:
-            fs = S(act(T.FS[:, :], T.F[:, :].indirect(T.SN[:, 12 * t:12 * t + 12])), tSN)
-        e2 = eq(2)
-        vA = V(tt(T.A1[:, :], T.M[:, :], T.A1[:, :], A.mult), sA, vM)
-        f2 = fg("v" if t else "s", 2)
-
-        def dst(c):
-            return T.KPb[:, 0:64] if c == 2 else T.KPa[:, 64 * c:64 * c + 64]
-
-        def eqm(c, tok):
-            return MM([tok], *[(dst(c), T.WST[:, 15 - p:143 - p], T.EQ[:, 1024 * c + p:1024 * c + 1024:16], False, False)
-                               for p in range(16)])
-
-        def fgm(c, tok, last):
-            return MM([tok], *[(dst(c), T.DW[:, 128 * p:128 * p + 128], T.FG[:, 1024 * c + p:1024 * c + 1024:16], False,
-                                last and p == 15) for p in range(16)])
-        MM([vE], (T.KPa[:, 0:128], rep(t), T.Es[:, 0:128], True, False))
-        MM([vE], (T.KPb[:, 0:64], rep(t), T.Es[:, 128:192], True, False))
-        eqm(0, e0)
-        eqm(1, e1)
-        eqm(2, e2)
-        fgm(0, f0, False)
-        pa = fgm(1, f1, t == 0)
-        if t:
-            pa = MM([fs], (T.KPa[:, 0:128], T.OUTW[:, :], T.FS[:, 0:128], False, True))
-            MM([fs], (T.KPb[:, 0:64], T.OUTW[:, :], T.FS[:, 128:192], False, False))
-        pb = fgm(2, f2, True)
-        ka = V(tt(T.KEY[:, 0:128], T.KPa[:, 0:128], T.A1[:, 0:128], A.add), pa, vA)
-        kb = V(tt(T.KEY[:, 128:192], T.KPb[:, 0:64], T.A1[:, 128:192], A.add), pb)
-        xa = MM([ka], (T.pBa[:, 0:128], T.KEY[:, 0:128], T.IDf[:, :], True, True))
-        sa = S(act(T.KB[:, 0:128], T.pBa[:, 0:128]), xa)
-        xb = MM([kb], (T.pBb[0:64, 0:64], T.KEY[:, 128:192], T.IDf[:, 0:64], True, True),
-                (T.pBb[64:128, 0:64], T.KEY[:, 128:192], T.IDf[:, 64:128], True, True))
-        sb = S(act(T.KB[:, 128:192], T.pBb[:, 0:64]), xb)
+            fs = S(act(T.FS[:, :], T.F[:, :].indirect(T.SN[:, 12 * t:12 * t + 12])), tSN, tF)
+        f1 = fg(128, 192)
+        sG = S(act(T.Dg[:, :], T.pG[:, 0:192]), pg)
         if t == 0:
-            v = V(tt(T.S0[:, :], SGt, T.DM[:, :], A.mult))
-            for x, y in ((T.S0, T.S1), (T.S1, T.S2), (T.S2, T.S3), (T.S3, T.S4)):
-                v = V(tt(y[:, :], x[:, 0::2], x[:, 1::2], A.add), v)
-            vSN = V(cpy(T.SN[:, 0:12], T.S4[:, :]), v)
-            for u in range(1, RO):
-                dma("y", T.SN[16 * u:128, 12 * u:12 * u + 12], T.SN[0:128 - 16 * u, 0:12], "dSN", vSN)
-                tSN = dma("y", T.SN[0:16 * u, 12 * u:12 * u + 12], T.SN[128 - 16 * u:128, 0:12], "dSN")
-            V(ts(T.NI2[:, 0:12], T.NI[:, :], 6, A.arith_shift_right), vNI)
-            v = V(ts(T.NI2[:, 12:24], T.NI[:, :], 63, A.bitwise_and))
-            v = V(cpy(T.NF[:, :], T.NI2[:, :]), v)
-            for c in range(12):
-                V(ts(T.SHI[:, 64 * c:64 * c + 64], T.iot[:, :], T.NF[:, c:c + 1], A.is_equal), v)
-                vS = V(ts(T.SLO[:, 64 * c:64 * c + 64], T.iot[:, :], T.NF[:, 12 + c:13 + c], A.is_equal, -1.0, A.mult))
-        if t == 1:
-            v = V(cpy(T.RI[:, :], T.RJ[:, 0:192]))
-            V(ts(T.RIh[:, :], T.RI[:, :], 6, A.arith_shift_right), v)
-            v = V(ts(T.RIl[:, :], T.RI[:, :], 63, A.bitwise_and))
-            V(ts(T.ZVa[:, :], T.RIh[:, :], -64.0, A.add, kc(10), A.mult), v)
-            v = V(ts(T.ZVb[:, :], T.RIl[:, :], kc(10), A.mult))
-            V(cpy(T.ZA[:, :].indirect(T.SN[:, 0:12]), T.ZVa[:, :]), v, gz)
-            vZ = V(cpy(T.ZB[:, :].indirect(T.SN[:, 0:12]), T.ZVb[:, :]))
-        if t == 3:
-            vV = V(tt(T.VAL[:, :], T.pZ[:, :], T.P2[:, :], A.add), pz, tP2)
-            dma("y", T.stV[:], T.VAL[:, :], "dV", vV)
+            sN = S(act(T.N1[:, :], T.pZ[:, :], AF.Relu, bias=-2047.0), pz)
+        f0 = fg(0, 128)
+        MM([e1], *trunks(T.pA, T.EQ, T.SelE, 1, False))
+        mine = (T.FS[:, 0:128], T.FS[:, 128:192]) if t else (T.NEG[:, 0:128], T.NEG[:, 0:64])
+        MM([f1], *(slots(T.pX, mine, T.SelF, 0, 0, True) + slots(T.pX, mine, T.SelF, 0, 1, True) + trunks(T.pX, T.FG, T.SelF, 1, True)))
+        if t:
+            MM([vD], (T.pD[0:32, 0:128], T.Ib[0:32, 0:32], T.D[:, :], True, False))
+        else:
+            MM([sN], *count_none(T.N1, False))
+        pa = MM([e0], *trunks(T.pA, T.EQ, T.SelE, 0, False))
+        px = MM([f0], *trunks(T.pX, T.FG, T.SelF, 0, True))
+        v = V(scan(T.AS[:, :], T.INC[:, :], T.pA[:, 0:204], A.add, A.max), pa)
+        v = V(ts(T.BI[:, :], T.AS[:, 16::17], 131040.0, A.add), v)
+        V(ts(T.UI[:, 12:24], T.BI[:, :], 12, A.arith_shift_right, 31, A.bitwise_and), v)
+        v = V(ts(T.UI[:, 0:12], T.BI[:, :], 5, A.arith_shift_right, 127, A.bitwise_and))
+        vP = V(ts(T.UI[:, 24:36], T.BI[:, :], 31, A.bitwise_and))
+        va = V(cpy(T.UF[:, 12:24], T.UI[:, 12:24]), v)
+        vb = V(ts(T.UF[:, 0:12], T.UI[:, 0:12], 1008.0, A.add))
+        for c in range(12):
+            s = S(act(T.TA[:, 32 * c:32 * c + 32], T.iotA[:, :], AF.Abs, bias=T.UF[:, 12 + c:13 + c], scale=-1.0), va)
+        sA = S(act(T.OA[:, :], T.TA[:, :], AF.Relu, bias=16.0, scale=-16.0), s)
+        vX = V(scan(T.XS[:, :], T.INC[:, :], T.pX[:, 0:204], A.add, A.max), px)
+        for c in range(12):
+            x = V(ts(T.OB[:, 128 * c:128 * c + 128], T.iotB[:, :], T.XS[:, 17 * c + 16:17 * c + 17], A.subtract,
+                     T.UF[:, c:c + 1], A.is_equal), vX, vb)
+            pd = MM([x, sA], (T.pD[0:32, 0:128], T.OA[:, 32 * c:32 * c + 32], T.OB[:, 128 * c:128 * c + 128], False, c == 11))
+        vD = S(act(T.D[:, :], T.pD[0:32, 0:128], AF.Sign, bias=(0.0 if t else -15.5)), pd, tF)
+        if t < 4:
+            tF = flags_to_F(vD)
+        if t == 0:
+            sV = S(act(T.VAL[:, :], T.pZ[:, :], AF.Identity, bias=2048.0))
+            dma("y", T.stV[:], T.VAL[:, :], "dV", sV)
             tV = dma("y", T.landV[me], T.VAL[lo:hi, :], "dV")
             send("stV", "landV", "arrV", tV)
-        v = V(tt(T.T1[:, :], T.KB[:, 0::2], T.KB[:, 1::2], A.max), sa, sb)
-        v = V(tt(T.T2[:, :], T.T1[:, 0::2], T.T1[:, 1::2], A.max), v)
-        v = V(tt(T.T3[:, :], T.T2[:, 0::2], T.T2[:, 1::2], A.max), v)
-        vb = V(tt(T.BEST[:, :], T.T3[:, 0::2], T.T3[:, 1::2], A.max), v)
-        vi = V(tt(T.BI[:, :], T.T3[:, 0::2], T.T3[:, 1::2], A.max))
-        w = float(2 ** 21) - 0.5
-        V(ts(T.BW[:, :], T.BEST[:, 0:8], w, A.max), vb)
-        V(ts(T.Bm[0:64, 0:4], T.BEST[0:64, 8:12], w, A.max))
-        v = V(ts(T.Bm[64:128, 4:8], T.BEST[64:128, 8:12], w, A.max))
-        m = MM([v], (T.pTR[0:8, 0:128], T.BW[:, :], T.IDf[:, :], True, True),
-               (T.pTR[0:8, 128:192], T.Bm[:, :], T.I64s[:, :], True, True))
-        sT = S(act(T.bT[:, :], T.pTR[0:8, 0:192]), m)
-        pR = MM([sT], (T.pTR[:, 192:384], T.REP8[:, :], T.bT[:, :], True, True))
-        V(ts(T.UI[:, 0:12], T.BI[:, :], 10, A.arith_shift_right, 63, A.bitwise_and), vi)
-        V(ts(T.UI[:, 12:24], T.BI[:, :], 4, A.arith_shift_right, 63, A.bitwise_and))
-        v = V(ts(T.C2[:, :], T.BI[:, :], 22, A.arith_shift_right))
-        V(cpy(T.UF[:, :], T.UI[:, :]), v)
-        v = V(ts(T.OK[:, :], T.C2[:, :], 0.0, A.is_equal))
-        ms = [(T.pD[0:64, 0:64], T.ID64[:, :], T.D[:, :], True, False)]
-        if t == 0:
-            ms += [(T.pD[0:64, 0:64], T.SHI[:, 64 * c:64 * c + 64], T.SLO[:, 64 * c:64 * c + 64], False, False) for c in range(12)]
-        MM([vD1, vS], *ms)
-        for c in range(12):
-            V(ts(T.OHI[:, 64 * c:64 * c + 64], T.iotR[:, :], T.UF[:, c:c + 1], A.is_equal, T.OK[:, c:c + 1], A.mult), v)
-            x = V(ts(T.OLO[:, 64 * c:64 * c + 64], T.iotR[:, :], T.UF[:, 12 + c:13 + c], A.is_equal))
-            pd = MM([x], (T.pD[0:64, 0:64], T.OHI[:, 64 * c:64 * c + 64], T.OLO[:, 64 * c:64 * c + 64], False, c == 11))
-        vD1 = S(act(T.D[:, :], T.pD[0:64, 0:64], AF.Sign), pd)
-        if t < 4:
-            tF = flags_to_F(vD1)
-        v = V(tt(T.W[:, :], T.pTR[:, 192:384], T.KEY[:, :], A.is_equal), pR)
-        v = V(tt(T.W[:, :], T.W[:, :], T.Dg[:, :], A.mult), v)
-        vTk = V(lambda e: e.tensor_tensor(T.Tk[:, :].indirect(at), T.Hf[:, :], T.W[:, :], A.add), v)
-        if t in (1, 2):
-            pz = zmm(t - 1)
-    dma("y", T.stD[:], T.D[:, :], "dD", vD1)
-    tD = dma("y", T.landD[me], T.D[8 * me:8 * me + 8, :], "dD")
+        v = V(tt(T.FI[:, :], T.XS[:, 16::17], T.UI[:, 24:36], A.max), vP)
+        v = V(ts(T.F5[:, :], T.FI[:, :], 31, A.bitwise_and), v)
+        v = V(tt(T.Wt[:, :], T.F5[:, :].indirect(T.LC[:, :]), T.C15[:, :], A.is_equal), v)
+        m = MM([v], (T.pW[:, 0:128], T.Wt[:, 0:128], T.Ib[:, :], True, True),
+               (T.pW[0:64, 128:192], T.Wt[:, 128:192], T.Ib[:, 0:64], True, True),
+               (T.pW[64:128, 128:192], T.Wt[:, 128:192], T.Ib[:, 64:128], True, True))
+        v = V(tt(T.WD[:, :], T.pW[:, 0:192], T.Dg[:, :], A.mult), m, sG)
+        vTk = V(lambda e: e.tensor_tensor(T.Tk[:, :].indirect(at), T.Hf[:, :], T.WD[:, :], A.add), v)
+    dma("y", T.stD[:], T.D[:, :], "dD", vD)
+    tD = dma("y", T.landD[me], T.D[4 * me:4 * me + 4, :], "dD")
+    tVR = dma("y", T.VR[:, :], T.landV[:], "dVR", ("arrV", 14), tV)
     tY = dma("y", T.stY[:], T.Tk[:, :], "dY", vTk)
     dma("s", T.yt[lo:hi, :], T.Tk[lo:hi, :], "oY1", vTk)
     send("stD", "landD", "arrD", tD)
     send("stY", "landY", "arrY", tY)
-    tVR = dma("y", T.VR[:, :], T.landV[:], "dVR", ("arrV", 14), tV)
     tKD = dma("y", T.KD[:, :], T.landD[:], "dKD", ("arrD", 14), tD)
-    m = MM([tKD], (T.pZ[:, :], T.R8b[:, :], T.KD[:, :], True, True))
+    m = MM([tKD, sV], (T.pZ[:, :], T.R8b[:, :], T.KD[:, :], True, True))
     v = V(tt(T.YP[:, :], T.pZ[:, :], T.VR[:, :], A.max), m, tVR)
     dma("y", T.yp[:], T.YP[:, :], "oP", v)
     need("s", [("arrY", 14)])

@@ -2,6 +2,7 @@ from concourse.bass import DstId, RemoteDMATransfer
 from concourse.mybir import AluOpType, ActivationFunctionType
 
 RO = 5
+NV = 16
 F32, BF, FH, I32, U16 = "float32", "bfloat16", "float16", "int32", "uint16"
 SCRATCH = {}
 
@@ -11,28 +12,30 @@ def _b(where, dtype, **kw):
         SCRATCH[k] = (where, s, dtype)
 
 
-_b("dram", I32, stR=[8, 128, 32], stT=[8, 128, 64], landR=[8, 128, 32], landT=[8, 128, 64])
-_b("dram", F32, stV=[8, 128, 64], landV=[8, 128, 64], stY=[8, 128, 64], landY=[8, 128, 64])
+_b("dram", U16, stP=[8, 128, 57], landP=[8, 128, 57], stT=[8, 128, 64], landT=[8, 128, 64], stY=[8, 128, 64], landY=[8, 128, 64])
+_b("dram", F32, stV=[8, 128, 64], landV=[8, 128, 64])
 _b("dram", BF, stD=[8, 128, 4], landD=[8, 128, 4])
 _b("sbuf", I32, P2=[128, 512], ii=[128, 192], col=[128, 272], cp=[128, 1], ci=[128, 4], cq8=[128, 256], iia=[128, 192],
-   cola=[128, 192], t12b=[128, 12], seg=[128, 272], slot=[128, 272], Cl=[128, 12], Cti=[128, 12], R=[128, 192], OT=[128, 60],
-   Tki=[128, 512], BI=[128, 12], UI=[128, 36], FI=[128, 12], F5=[128, 12])
-_b("sbuf", U16, LI=[128, 12], LB=[128, 12], LC=[128, 12], AT=[128, 60], SN=[128, 60], H16=[128, 192])
+   cola=[128, 256], t12b=[128, 24], seg=[128, 272], slot=[128, 272], Cl=[128, 12], Cti=[128, 12], RH=[128, 192], OT=[128, 72],
+   TkH=[128, 512], BI=[128, 12], UI=[128, 36], FI=[128, 12], F5=[128, 12], FIN=[128, 96])
+_b("sbuf", U16, LI=[128, 24], LC=[128, 12], LH=[128, 16], AT=[128, 60], SN=[128, 60], H16=[128, 192], PO=[128, 456],
+   PI=[128, 456], TO=[128, 512], TI=[128, 512], YO=[128, 512], YI=[128, 512], AO=[128, 24])
 _b("sbuf", F32, P=[128, 4096], KC=[128, 24], IN=[128, 128], IJ=[128, 136], REPf=[128, 256], R0=[128, 272], EM=[128, 192],
-   DM=[128, 192], SM=[128, 192], C15=[128, 192], INC=[128, 204], SH1=[128, 128], Clf=[128, 12], Ctf=[128, 12], E=[128, 192],
+   DM=[128, 192], SM=[128, 192], C15=[128, 256], INC=[128, 204], SH1=[128, 128], Clf=[128, 12], Ctf=[128, 12], E=[128, 192],
    RJ=[128, 192], RR0=[128, 3072], RR1=[128, 3072], RR2=[128, 3072], RR3=[128, 3072], RR4=[128, 3072], Tk=[128, 512],
    Hf=[128, 192], Dg=[128, 192], WD=[128, 192], AS=[128, 204], XS=[128, 204], UF=[128, 24], S0=[128, 192], S1=[128, 192],
-   VAL=[128, 512], VR=[128, 512], YP=[128, 512])
+   VAL=[128, 512], VR=[128, 512], YP=[128, 512], COf=[128, 12], EO=[128, 192], TkO=[128, 512], HO=[128, 192], DgO=[128, 192])
 _b("sbuf", FH, P2h=[128, 512], GY=[128, 1024], Ih=[128, 128])
 _b("sbuf", BF, iotA=[128, 32], iotB=[128, 128], SelF=[128, 8], SelE=[128, 8], Ib=[128, 128], IM=[128, 128], RS=[128, 272],
    NEG=[128, 128], C16=[128, 204], C4=[128, 36], SH2=[128, 128], YS=[128, 240], R8b=[8, 128], Et=[128, 192], N0=[128, 512],
    N1=[128, 512], hib=[128, 192], ZV=[128, 192], F=[128, 4096], Z=[128, 4096], EQ=[128, 3072], FG=[128, 3072], FS=[128, 192],
-   M=[128, 204], Wt=[128, 192], TA=[128, 384], OA=[128, 384], OB=[128, 1536], D=[32, 128], KD=[8, 512])
+   M=[128, 204], Wt=[128, 256], TA=[128, 384], OA=[128, 384], OB=[128, 1536], D=[32, 128], KD=[8, 512])
 _BANKS = ["pA", "pX", "pM", "pG", "pW", "pD", "pZ", "pE"]
 _b("psum", F32, **{k: [128, 512] for k in _BANKS})
 
-_ARR = ["arrR", "arrT", "arrV", "arrY", "arrD"]
-_DMA = ["dR", "dT", "dP2", "dF", "dCl", "dRl", "dO", "dTk", "dRR0", "dRR1", "dRR2", "dRR3", "dSN", "dV", "dVR", "dY", "dD", "dKD", "oY1", "oY2", "oP"]
+_ARR = ["arrP", "arrT", "arrA", "arrV", "arrY", "arrW", "arrD"]
+_DMA = ["dH", "dO", "dP2", "dP", "dT", "dF", "dPI", "dTI", "dAT", "dRR0", "dRR1", "dRR2", "dRR3", "dSN", "dV", "dVR", "dY", "dYI",
+        "dD", "dKD", "oY", "oP"]
 SEMAPHORES = ["cv", "cs", "cpe", "cg", "sent"] + _ARR + _DMA
 
 
@@ -104,93 +107,107 @@ def rank_program(g, core, T, topo):
     def fill(out, x):
         return lambda e: e.memset(out, x)
 
-    def send(src, dst, sem, *deps):
+    def send(src, dst, sem, *deps, to=None, each=2):
         need("g", deps)
-        order = sorted([(me + k) % 8 for k in range(1, 8)], key=lambda n: len(topo.engines(core, T.cores[n])))
+        order = sorted(to or [(me + k) % 8 for k in range(1, 8)], key=lambda n: len(topo.engines(core, T.cores[n])))
         used, tr = [], []
         for n in order:
             c = T.cores[n]
-            es = [e for e in topo.engines(core, c) if e not in used][:2]
+            es = [e for e in topo.engines(core, c) if e not in used][:each]
             used += es
             a = topo.addr(c)
             tr.append(RemoteDMATransfer(dst_ids=[DstId(rid=a[0], pnc=a[1])], dma_engine_mask=sum(1 << e for e in es),
-                                        remote_sem=T.sem[sem], srcs=[T[src][n]], dsts=[T[dst][me]], alu_op=0))
+                                        remote_sem=T.sem[sem], srcs=[src(n)], dsts=[dst], alu_op=0))
         g.remote_dma_fused(tr, local_sem=T.sem["sent"])
-        cnt["sent"] += 14
-        cnt[sem] += 14
+        cnt["sent"] += len(used)
+        cnt[sem] += len(used)
+        return (sem, cnt[sem])
 
     lo, hi = 16 * me, 16 * me + 16
-    dma("y", T.stR[:, 0:96, :], T.routes[:], "dR")
-    dma("s", T.stR[:, 96:102, :], T.calls[:], "dR")
-    dma("s", T.stR[:, 102:128, :], T.trunk[0:13, :], "dR")
-    dma("y", T.landR[me, 0:96, :], T.routes[lo:hi, :], "dR")
-    tR = dma("s", T.landR[me, 96:102, :], T.calls[lo:hi, :], "dR")
-    dma("y", T.stT[:], T.trunk[:], "dT")
-    tT = dma("y", T.landT[me], T.trunk[lo:hi, :], "dT")
+
+    def exchange(buf, st, land, sem, arr, *deps):
+        dma("y", T[st][:], T[buf][:, :], sem, *deps)
+        t = dma("y", T[land][me], T[buf][lo:hi, :], sem)
+        return [t, send(lambda n: T[st][n], T[land][me], arr, t)]
+
+    dma("y", T.OT[:, 0:12], T.routes[0::16, :], "dH")
+    dma("y", T.RH[:, :], T.routes[:], "dH")
+    dma("y", T.TkH[:, :], T.trunk[:], "dH")
+    for t in range(1, RO):
+        dma("s", T.OT[:, 12 * t:12 * t + 12], T.routes[t::16, :], "dH")
+    tH = dma("s", T.OT[:, 60:72], T.calls[:], "dH")
     for q in range(8):
-        tP2 = dma("s", T.P2[16 * q:16 * q + 16, :], T.paths[lo:hi, 512 * q:512 * q + 512], "dP2")
+        tP2 = dma("ys"[q % 2], T.P2[16 * q:16 * q + 16, :], T.paths[lo:hi, 512 * q:512 * q + 512], "dP2")
     g1 = op("g", lambda e: e.iota(T.cp[:, 0:1], [[0, 1]], 0, 1))
     g2 = op("g", lambda e: e.iota(T.col[:, :], [[1, 272]], 0, 0))
     g3 = op("g", lambda e: e.iota(T.ii[:, :], [[1, 12], [12, 16]], 0, 0))
     g4 = op("g", lambda e: e.iota(T.seg[:, :], [[0, 2], [1, 8], [0, 17]], 0, 0))
     g5 = op("g", lambda e: e.iota(T.slot[:, :], [[0, 16], [1, 17]], 0, 0))
-    send("stR", "landR", "arrR", tR)
-    send("stT", "landT", "arrT", tT)
-
-    vF = V(fill(T.F[:, :], 0.0))
     KC, col, ci = T.KC, T.col, T.ci
 
     def kc(n):
         return KC[:, n:n + 1]
+    v = V(fill(T.F[:, 0:512], 0.0))
+    for y in range(1, 8):
+        sF = S(act(T.F[:, 512 * y:512 * y + 512], T.F[:, 0:512]), v)
     V(ts(ci[:, 0:1], T.cp[:, 0:1], 15, A.bitwise_and), g1)
     V(ts(ci[:, 1:2], T.cp[:, 0:1], 4, A.arith_shift_right))
-    V(cpy(kc(0), T.cp[:, 0:1]))
-    v = V(ts(T.cola[:, :], col[:, 0:192], 15, A.bitwise_and), g2)
-    V(cpy(kc(1), ci[:, 0:1]), v)
-    v = V(cpy(kc(2), ci[:, 1:2]))
-    V(ts(T.DM[:, :], T.cola[:, :], kc(1), A.is_equal), v)
+    v = V(cpy(kc(0), T.cp[:, 0:1]))
+    V(cpy(KC[:, 1:3], ci[:, 0:2]), v)
+    V(ts(kc(4), ci[:, 0:1], 12.0, A.mult))
+    v = V(ts(T.cola[:, :], col[:, 0:256], 15, A.bitwise_and), g2)
+    V(ts(T.t12b[:, 0:12], col[:, 0:12], kc(4), A.add), v)
+    V(ts(T.DM[:, :], T.cola[:, 0:192], kc(1), A.is_equal))
     v = V(ts(KC[:, 16:24], col[:, 0:8], kc(2), A.is_equal))
+    V(ts(T.t12b[:, 12:24], T.t12b[:, 0:12], 4, A.arith_shift_right), v)
     for y in range(8):
-        V(ts(T.GY[:, 128 * y:128 * y + 128], T.DM[:, 0:128], kc(16 + y), A.mult), v)
-    V(ts(kc(3), ci[:, 1:2], 4.0, A.mult, 3.0, A.add))
+        v = V(ts(T.GY[:, 128 * y:128 * y + 128], T.DM[:, 0:128], kc(16 + y), A.mult))
+    V(cpy(T.LI[:, :], T.t12b[:, :]), v)
+    LI, LB = T.LI[:, 0:12], T.LI[:, 12:24]
+    v = V(ts(T.OT[:, 0:60], T.OT[:, 0:60], 511, A.bitwise_and), tH)
+    v = V(cpy(T.PO[:, 384:456], T.OT[:, :]), v)
+    V(cpy(T.PO[:, 192:384], T.RH[:, :].indirect(LI)))
+    v = V(cpy(T.PO[:, 0:192], T.TkH[:, :].indirect(T.PO[:, 384:396])), v)
+    xP = exchange("PO", "stP", "landP", "dP", "arrP", v)
     vPh = V(ts(T.P2h[:, :], T.P2[:, :], -2048.0, A.add), tP2)
     for y in range(8):
         m = MM([vPh], (T[_BANKS[y]][:, :], T.GY[:, 128 * y:128 * y + 128], T.P2h[:, :], True, True))
         tP = S(act(T.P[:, 512 * y:512 * y + 512], T[_BANKS[y]][:, :], AF.Identity, bias=-2048.0), m)
-    V(ts(T.C4[:, :], col[:, 0:36], kc(3), A.is_equal), vPh)
+    v = V(cpy(T.TO[:, :], T.TkH[:, :]))
+    xT = exchange("TO", "stT", "landT", "dT", "arrT", v)
+    xA = send(lambda n: T.PO[:, 432:456], T.AO[:, :], "arrA", to=[(me + RO - 1) % 8], each=8)
+    v = V(ts(kc(3), ci[:, 1:2], 4.0, A.mult, 3.0, A.add))
     vN0 = V(ts(T.N0[:, :], T.P2[:, :], 4096.0, A.is_ge))
+    vN0 = V(ts(T.C4[:, :], col[:, 0:36], kc(3), A.is_equal), v)
 
-    def count_none(n, last):
-        return [(T.pD[0:32, 0:128], T.C4[:, 3 - u:35 - u], n[:, 128 * u:128 * u + 128], u == 0, last and u == 3) for u in range(4)]
-    m = MM([vN0, tP], *count_none(T.N0, True))
+    def count_none(n, first, last):
+        return [(T.pD[0:32, 0:128], T.C4[:, 3 - u:35 - u], n[:, 128 * u:128 * u + 128], first and u == 0, last and u == 3)
+                for u in range(4)]
+    m = MM([vN0, tP], *count_none(T.N0, True, True))
     vD = S(act(T.D[:, :], T.pD[0:32, 0:128], AF.Sign, bias=-15.5), m)
 
     def flags_to_F(*tok):
         for q in range(8):
             t = dma("ys"[q % 2], T.F[16 * q:16 * q + 1, :], T.D[:, :], "dF", *tok)
         return t
-    vZ0 = V(fill(T.Z[:, :], 0.0))
+    tF = flags_to_F(vD, sF)
     V(ts(T.cq8[:, :], col[:, 0:256], 4, A.arith_shift_right, 7, A.bitwise_and))
     V(ts(T.iia[:, :], T.ii[:, :], 15, A.bitwise_and), g3)
-    V(ts(kc(4), ci[:, 0:1], 12.0, A.mult))
-    V(ts(kc(5), ci[:, 1:2], 512.0, A.mult))
     V(ts(kc(6), ci[:, 0:1], 0.0, A.is_equal, 1024.0, A.mult))
     V(ts(kc(7), ci[:, 0:1], 5.0, A.is_lt))
     V(ts(kc(8), ci[:, 0:1], 5.0, A.is_ge, -5.0, A.mult))
     V(ts(kc(9), T.cp[:, 0:1], 5.0, A.add))
     V(ts(kc(10), T.cp[:, 0:1], 0.0, A.is_equal, 16.0, A.mult))
     v = V(ts(kc(11), T.cp[:, 0:1], kc(2), A.add, 1.0, A.add))
-    V(ts(T.t12b[:, :], col[:, 0:12], kc(4), A.add), v)
-    V(ts(kc(12), ci[:, 0:1], kc(8), A.add, 112.0, A.add))
+    V(ts(kc(12), ci[:, 0:1], kc(8), A.add, 112.0, A.add), v)
     V(ts(T.EM[:, :], T.iia[:, :], kc(1), A.is_equal))
-    v = V(ts(T.REPf[:, :], T.cq8[:, :], kc(2), A.is_equal))
-    V(cpy(T.LI[:, :], T.t12b[:, :]), v)
+    V(ts(T.REPf[:, :], T.cq8[:, :], kc(2), A.is_equal))
     V(cpy(T.LC[:, :], col[:, 0:12]))
-    v = V(ts(T.Cti[:, :], T.t12b[:, :], 4, A.arith_shift_right))
+    V(ts(T.LH[:, 0:8], col[:, 0:8], 12.0, A.mult, float(me), A.add))
+    V(ts(T.LH[:, 8:16], col[:, 0:8], 12.0, A.mult, float(8 + me % 4), A.add))
     V(ts(T.SH1[:, :], col[:, 0:128], kc(9), A.is_equal, kc(7), A.mult))
     V(ts(T.S0[:, 0:128], col[:, 0:128], kc(0), A.is_equal, kc(7), A.mult))
-    V(ts(T.SM[:, :], T.cola[:, :], 0.0, A.not_equal))
-    v = V(cpy(T.LB[:, :], T.Cti[:, :]), v)
+    v = V(ts(T.SM[:, :], T.cola[:, 0:192], 0.0, A.not_equal))
     V(tt(T.SH2[:, :], T.S0[:, 0:128], T.SH1[:, :], A.subtract), v)
     V(ts(T.YS[:, :], col[:, 0:240], kc(12), A.is_equal))
     V(ts(T.Ih[:, :], col[:, 0:128], kc(0), A.is_equal))
@@ -211,49 +228,27 @@ def rank_program(g, core, T, topo):
     V(ts(T.C15[:, :], T.cola[:, :], -1.0, A.mult, 15.0, A.add))
     V(ts(T.iotA[:, :], col[:, 0:32], -1.0, A.mult, 31.0, A.add))
     V(ts(T.iotB[:, :], col[:, 0:128], -1.0, A.mult, 127.0, A.add))
-    vC = V(ts(T.R8b[:, :], T.cq8[0:8, 0:128], KC[0:8, 0:1], A.is_equal, 4096.0, A.mult))
+    V(ts(T.R8b[:, :], T.cq8[0:8, 0:128], KC[0:8, 0:1], A.is_equal, 4096.0, A.mult))
+    vC = V(fill(T.Z[:, :], 0.0))
 
-    need("y", [("arrR", 14), tR])
-    tRl = dma("y", T.R[:, :], T.landR[:, 0:96, :], "dRl")
-    tCl = dma("y", T.Cl[:, :], T.landR[:, 96:102, :], "dCl")
-    for t in range(RO):
-        tO = dma("y", T.OT[16 * t:128, 12 * t:12 * t + 12], T.landR[0:8 - t, 6 * t:6 * t + 6, :], "dO")
-        if t:
-            tO = dma("y", T.OT[0:16 * t, 12 * t:12 * t + 12], T.landR[8 - t:8, 6 * t:6 * t + 6, :], "dO")
-    need("y", [("arrT", 14), tT])
-    tTk = dma("y", T.Tki[:, :], T.landT[:], "dTk")
-    tF = flags_to_F(vD, vF)
+    tPI = dma("y", T.PI[:, :], T.landP[:], "dPI", *xP)
+    tTI = dma("y", T.TI[:, :], T.landT[:], "dTI", *xT)
+
+    def turn(dst, src, u, sem, *deps):
+        dma("y", dst(16 * u, 128), src(0, 128 - 16 * u), sem, *deps)
+        return dma("y", dst(0, 16 * u), src(128 - 16 * u, 128), sem)
 
     def rep(t):
         return T.REPf[:, 16 * (8 - t):16 * (16 - t)]
-    vRJ = V(ts(T.RJ[:, :], T.R[:, :].indirect(T.LI[:, :]), -4096.0, A.add), tRl, vC)
-    v = V(cpy(T.Clf[:, :], T.Cl[:, :]), tCl)
-    V(ts(T.Cti[:, :], T.Cl[:, :], 3584, A.bitwise_and))
-    v = V(tt(T.E[:, :], T.Clf[:, :].indirect(T.LB[:, :]), T.EM[:, :], A.mult), v)
-    pS = MM([v, tP], (T.pE[:, 0:192], rep(0), T.E[:, :], True, True))
-    v = V(cpy(T.Ctf[:, :], T.Cti[:, :]), v)
-    vE = V(tt(T.Et[:, :], T.Ctf[:, :].indirect(T.LB[:, :]), T.EM[:, :], A.mult), v)
-    s = S(act(T.hib[:, :], T.RJ[:, :]), vRJ)
-    m = MM([s], (T.pW[:, 0:192], T.SH1[:, :], T.RJ[:, :], True, False), (T.pW[:, 0:192], T.SH2[:, :], T.hib[:, :], False, True))
     RR = [T["RR%d" % t] for t in range(RO)]
-    for p in range(11):
-        b = S(act(T.RR0[:, p::16], T.RJ[:, :]), vRJ)
-        if p == 3:
-            sZV = S(act(T.ZV[:, :], T.pW[:, 0:192]), m)
-    v = V(tt(T.S0[:, :], T.pE[:, 0:192], T.DM[:, :], A.mult), pS)
-    v = V(scan(T.S1[:, :], T.SM[:, :], T.S0[:, :], A.mult, A.add), v)
-    vSN = V(cpy(T.SN[:, 0:12], T.S1[:, 15::16]), v)
-    for u in range(1, RO):
-        dma("y", T.SN[16 * u:128, 12 * u:12 * u + 12], T.SN[0:128 - 16 * u, 0:12], "dSN", vSN)
-        tSN = dma("y", T.SN[0:16 * u, 12 * u:12 * u + 12], T.SN[128 - 16 * u:128, 0:12], "dSN")
-    for p in range(11, 16):
-        a = V(cpy(T.RR0[:, p::16], T.RJ[:, :]), vRJ)
-    rr = [[a, b]] + [None] * 4
-    vZ = V(cpy(T.Z[:, :].indirect(T.SN[:, 0:12]), T.ZV[:, :]), sZV, vSN, vZ0)
-    pz = MM([vZ], (T.pZ[:, :], T.Ih[:, :], T.P2h[:, :], True, False),
-            *[(T.pZ[:, :], T.YS[:, 112 - 16 * q:240 - 16 * q], T.Z[:, 512 * q:512 * q + 512], False, q == 7) for q in range(8)])
-    vAT = V(ts(T.AT[:, :], T.OT[:, :], kc(5), A.subtract), tO)
-    vTk = V(cpy(T.Tk[:, :], T.Tki[:, :]), tTk)
+    vRJ = V(ts(T.RJ[:, :], T.PI[:, 192:384], -4096.0, A.add), tPI, vC)
+    for p in range(8):
+        a = V(cpy(T.RR0[:, 2048 + p::16], T.RJ[:, 128:192]), vRJ)
+        b = S(act(T.RR0[:, 2056 + p::16], T.RJ[:, 128:192]), vRJ)
+    for p in range(16):
+        c = S(act(T.RR0[:, p:2048:16], T.RJ[:, 0:128]))
+    rr = [[[a, b], [c]]] + [None] * 4
+    sH = S(act(T.hib[:, :], T.RJ[:, :]))
 
     def to_seekers(out, l, w, o, last):
         return [(out[0:64, 136:204], l[:, 128:192], w[:, o:o + 68], False, False),
@@ -270,44 +265,68 @@ def rank_program(g, core, T, topo):
         return [m for p in range(16) for m in slots(out, (tab[:, p:2048:16], tab[:, 2048 + p:3072:16]), sel, 1 + p, part, alone, p == 15)]
 
     for t in range(RO):
-        at = T.AT[:, 12 * t:12 * t + 12]
-        h16 = V(cpy(T.H16[:, :], T.Tk[:, :].indirect(at)), vTk, vAT)
-        hf = S(act(T.Hf[:, :], T.Tk[:, :].indirect(at)), vTk, vAT)
-        if t < 4:
-            n = 16 * (t + 1)
-            dma("y", RR[t + 1][n:128, :], T.RR0[0:128 - n, :], "dRR%d" % t, tF, *rr[0])
-            rr[t + 1] = [dma("y", RR[t + 1][0:n, :], T.RR0[128 - n:128, :], "dRR%d" % t)]
+        if t == 0:
+            at, H, h16 = T.PI[:, 384:396], T.PI, tPI
+            hf = V(cpy(T.Hf[:, :], T.PI[:, 0:192]))
+        else:
+            at, H = T.AT[:, 12 * t:12 * t + 12], T.H16
+            h16 = V(cpy(T.H16[:, :], T.Tk[:, :].indirect(at)), vTk, tAT)
+            hf = S(act(T.Hf[:, :], T.Tk[:, :].indirect(at)), vTk, tAT)
+        if t == RO - 1:
+            xY = exchange("YO", "stY", "landY", "dY", "arrY", V(cpy(T.YO[:, :], T.Tk[:, :])))
+            tYI = dma("y", T.YI[:, :], T.landY[:], "dYI", *xY)
+        else:
+            x = turn(lambda a, b: RR[t + 1][a:b, :], lambda a, b: T.RR0[a:b, :], t + 1, "dRR%d" % t, tF, *(rr[0][0] + rr[0][1]))
+            rr[t + 1] = [[x], [x]]
+
+        def eq(a, b, part):
+            return V(tt(T.EQ[:, 16 * a:16 * b], T.P[:, :].indirect(H[:, a:b]), RR[t][:, 16 * a:16 * b], A.is_equal), h16, tP, *rr[t][part])
+
+        def fg(q, a, b):
+            o, w = T.FG[:, 16 * a:16 * b], T.F[:, :].indirect(H[:, a:b])
+            return op(q, act(o, w) if q == "s" else cpy(o, w), h16, tF)
+        e1 = eq(128, 192, 0)
+        if t == 0:
+            V(cpy(T.Cl[:, :], T.PI[:, 444:456]))
+            v = V(cpy(T.Clf[:, :], T.PI[:, 444:456]))
+            V(ts(T.Cti[:, :], T.Cl[:, :], 3584, A.bitwise_and), v)
+            v = V(tt(T.E[:, :], T.Clf[:, :].indirect(LB), T.EM[:, :], A.mult))
+            pS = MM([v, tP], (T.pE[:, 0:192], rep(0), T.E[:, :], True, True))
+            v = V(cpy(T.Ctf[:, :], T.Cti[:, :]), v)
+            vE = V(tt(T.Et[:, :], T.Ctf[:, :].indirect(LB), T.EM[:, :], A.mult), v)
+            m = MM([sH], (T.pW[:, 0:192], T.SH1[:, :], T.RJ[:, :], True, False), (T.pW[:, 0:192], T.SH2[:, :], T.hib[:, :], False, True))
+            sZV = S(act(T.ZV[:, :], T.pW[:, 0:192]), m)
+            v = V(tt(T.S0[:, :], T.pE[:, 0:192], T.DM[:, :], A.mult), pS)
+            v = V(scan(T.S1[:, :], T.SM[:, :], T.S0[:, :], A.mult, A.add), v)
+            vSN = V(cpy(T.SN[:, 0:12], T.S1[:, 15::16]), v)
+            vZ = V(cpy(T.Z[:, :].indirect(T.SN[:, 0:12]), T.ZV[:, :]), sZV, vSN)
+            for u in range(1, RO):
+                tAT = turn(lambda a, b: T.AT[a:b, 12 * u:12 * u + 12], lambda a, b: T.PI[a:b, 384 + 12 * u:396 + 12 * u], u, "dAT")
+                tSN = turn(lambda a, b: T.SN[a:b, 12 * u:12 * u + 12], lambda a, b: T.SN[a:b, 0:12], u, "dSN", vSN)
+        e0 = eq(0, 128, 1)
         o = 17 * (8 - t)
         pm = MM([hf, vE], (T.pM[:, 0:204], T.NEG[:, :], T.C16[:, :], True, False),
                 *(to_seekers(T.pM, T.Et, T.RS, o, False) + to_seekers(T.pM, T.Hf, T.IJ, 0, True)))
+        if t < RO - 1:
+            pg = MM([], (T.pG[:, 0:192], rep(t), T.E[:, :], True, False), (T.pG[:, 0:192], T.IN[:, :], T.Hf[:, :], False, True))
         sM = S(act(T.M[:, :], T.pM[:, 0:204], AF.Sign), pm)
-        pg = MM([], (T.pG[:, 0:192], rep(t), T.E[:, :], True, False), (T.pG[:, 0:192], T.IN[:, :], T.Hf[:, :], False, True))
+        f1 = fg("s", 128, 192)
         MM([sM], (T.pA[:, 0:204], T.IM[:, :], T.M[:, :], True, False),
            *(to_seekers(T.pA, T.Hf, T.IJ, 0, False) + to_seekers(T.pA, T.E, T.R0, o, False)))
-
-        def eq(a, b):
-            return V(tt(T.EQ[:, 16 * a:16 * b], T.P[:, :].indirect(T.H16[:, a:b]), RR[t][:, 16 * a:16 * b], A.is_equal), h16, tP, *rr[t])
-
-        def fg(a, b):
-            return S(act(T.FG[:, 16 * a:16 * b], T.F[:, :].indirect(T.H16[:, a:b])), h16, tF)
-        e1 = eq(128, 192)
-        e0 = eq(0, 128)
-        if t:
-            fs = S(act(T.FS[:, :], T.F[:, :].indirect(T.SN[:, 12 * t:12 * t + 12])), tSN, tF)
-        f1 = fg(128, 192)
-        sG = S(act(T.Dg[:, :], T.pG[:, 0:192]), pg)
-        if t == 0:
-            sN = S(act(T.N1[:, :], T.pZ[:, :], AF.Relu, bias=-2047.0), pz)
-        f0 = fg(0, 128)
         MM([e1], *trunks(T.pA, T.EQ, T.SelE, 1, False))
-        mine = (T.FS[:, 0:128], T.FS[:, 128:192]) if t else (T.NEG[:, 0:128], T.NEG[:, 0:64])
-        MM([f1], *(slots(T.pX, mine, T.SelF, 0, 0, True) + slots(T.pX, mine, T.SelF, 0, 1, True) + trunks(T.pX, T.FG, T.SelF, 1, True)))
+        MM([f1], *trunks(T.pX, T.FG, T.SelF, 1, True))
+        if t == 0:
+            pz = MM([vZ], (T.pZ[:, :], T.Ih[:, :], T.P2h[:, :], True, False),
+                    *[(T.pZ[:, :], T.YS[:, 112 - 16 * q:240 - 16 * q], T.Z[:, 512 * q:512 * q + 512], False, q == 7) for q in range(8)])
+        f0 = fg("s", NV, 128)
         if t:
+            fs = V(cpy(T.FS[:, :], T.F[:, :].indirect(T.SN[:, 12 * t:12 * t + 12])), tSN, tF)
             MM([vD], (T.pD[0:32, 0:128], T.Ib[0:32, 0:32], T.D[:, :], True, False))
-        else:
-            MM([sN], *count_none(T.N1, False))
         pa = MM([e0], *trunks(T.pA, T.EQ, T.SelE, 0, False))
-        px = MM([f0], *trunks(T.pX, T.FG, T.SelF, 0, True))
+        mine = (T.FS[:, 0:128], T.FS[:, 128:192]) if t else (T.NEG[:, 0:128], T.NEG[:, 0:64])
+        MM([fs if t else None], *(slots(T.pX, mine, T.SelF, 0, 0, True) + slots(T.pX, mine, T.SelF, 0, 1, True)))
+        fv = fg("v", 0, NV)
+        px = MM([f0, fv], *trunks(T.pX, T.FG, T.SelF, 0, True))
         v = V(scan(T.AS[:, :], T.INC[:, :], T.pA[:, 0:204], A.add, A.max), pa)
         v = V(ts(T.BI[:, :], T.AS[:, 16::17], 131040.0, A.add), v)
         V(ts(T.UI[:, 12:24], T.BI[:, :], 12, A.arith_shift_right, 31, A.bitwise_and), v)
@@ -315,44 +334,61 @@ def rank_program(g, core, T, topo):
         vP = V(ts(T.UI[:, 24:36], T.BI[:, :], 31, A.bitwise_and))
         va = V(cpy(T.UF[:, 12:24], T.UI[:, 12:24]), v)
         vb = V(ts(T.UF[:, 0:12], T.UI[:, 0:12], 1008.0, A.add))
-        for c in range(12):
-            s = S(act(T.TA[:, 32 * c:32 * c + 32], T.iotA[:, :], AF.Abs, bias=T.UF[:, 12 + c:13 + c], scale=-1.0), va)
-        sA = S(act(T.OA[:, :], T.TA[:, :], AF.Relu, bias=16.0, scale=-16.0), s)
+        if t == 0:
+            sN = S(act(T.N1[:, :], T.pZ[:, :], AF.Relu, bias=-2047.0), pz)
+        if t < RO - 1:
+            sG = S(act(T.Dg[:, :], T.pG[:, 0:192]), pg)
+        sA = []
+        for h in range(2):
+            for c in range(6 * h, 6 * h + 6):
+                s = S(act(T.TA[:, 32 * c:32 * c + 32], T.iotA[:, :], AF.Abs, bias=T.UF[:, 12 + c:13 + c], scale=-1.0), va)
+            sA += [S(act(T.OA[:, 192 * h:192 * h + 192], T.TA[:, 192 * h:192 * h + 192], AF.Relu, bias=16.0, scale=-16.0), s)] * 6
         vX = V(scan(T.XS[:, :], T.INC[:, :], T.pX[:, 0:204], A.add, A.max), px)
+        v = V(tt(T.FI[:, :], T.XS[:, 16::17], T.UI[:, 24:36], A.max), vP, vX)
+        v5 = V(ts(T.F5[:, :], T.FI[:, :], 31, A.bitwise_and), v)
+        if t == 0:
+            MM([sN], *count_none(T.N1, True, False))
+        if t == RO - 1:
+            xW = send(lambda n: T.F5[:, :], T.FIN[:, 12 * me:12 * me + 12], "arrW", v5)
+        else:
+            v = V(tt(T.Wt[:, 0:192], T.F5[:, :].indirect(T.LC[:, :]), T.C15[:, 0:192], A.is_equal), v5)
+            m = MM([v], (T.pW[:, 0:128], T.Wt[:, 0:128], T.Ib[:, :], True, True),
+                   (T.pW[0:64, 128:192], T.Wt[:, 128:192], T.Ib[:, 0:64], True, True),
+                   (T.pW[64:128, 128:192], T.Wt[:, 128:192], T.Ib[:, 64:128], True, True))
         for c in range(12):
             x = V(ts(T.OB[:, 128 * c:128 * c + 128], T.iotB[:, :], T.XS[:, 17 * c + 16:17 * c + 17], A.subtract,
                      T.UF[:, c:c + 1], A.is_equal), vX, vb)
-            pd = MM([x, sA], (T.pD[0:32, 0:128], T.OA[:, 32 * c:32 * c + 32], T.OB[:, 128 * c:128 * c + 128], False, c == 11))
+            pd = MM([x, sA[c]], (T.pD[0:32, 0:128], T.OA[:, 32 * c:32 * c + 32], T.OB[:, 128 * c:128 * c + 128], False, c == 11))
         vD = S(act(T.D[:, :], T.pD[0:32, 0:128], AF.Sign, bias=(0.0 if t else -15.5)), pd, tF)
-        if t < 4:
-            tF = flags_to_F(vD)
+        if t == RO - 1:
+            break
+        tF = flags_to_F(vD)
         if t == 0:
+            vTk = V(cpy(T.Tk[:, :], T.TI[:, :]), tTI)
             sV = S(act(T.VAL[:, :], T.pZ[:, :], AF.Identity, bias=2048.0))
-            dma("y", T.stV[:], T.VAL[:, :], "dV", sV)
-            tV = dma("y", T.landV[me], T.VAL[lo:hi, :], "dV")
-            send("stV", "landV", "arrV", tV)
-        v = V(tt(T.FI[:, :], T.XS[:, 16::17], T.UI[:, 24:36], A.max), vP)
-        v = V(ts(T.F5[:, :], T.FI[:, :], 31, A.bitwise_and), v)
-        v = V(tt(T.Wt[:, :], T.F5[:, :].indirect(T.LC[:, :]), T.C15[:, :], A.is_equal), v)
-        m = MM([v], (T.pW[:, 0:128], T.Wt[:, 0:128], T.Ib[:, :], True, True),
-               (T.pW[0:64, 128:192], T.Wt[:, 128:192], T.Ib[:, 0:64], True, True),
-               (T.pW[64:128, 128:192], T.Wt[:, 128:192], T.Ib[:, 64:128], True, True))
+            xV = exchange("VAL", "stV", "landV", "dV", "arrV", sV)
+        if t == 1:
+            v = V(cpy(T.COf[:, :], T.AO[:, 12:24]), xA)
+            v = V(tt(T.EO[:, :], T.COf[:, :].indirect(LB), T.EM[:, :], A.mult), v)
+            pO = MM([v], (T.pE[:, 0:192], rep(0), T.EO[:, :], True, True))
+            tVR = dma("y", T.VR[:, :], T.landV[:], "dVR", *xV)
         v = V(tt(T.WD[:, :], T.pW[:, 0:192], T.Dg[:, :], A.mult), m, sG)
-        vTk = V(lambda e: e.tensor_tensor(T.Tk[:, :].indirect(at), T.Hf[:, :], T.WD[:, :], A.add), v)
+        vTk = V(lambda e: e.tensor_tensor(T.Tk[:, :].indirect(at), T.Hf[:, :], T.WD[:, :], A.add), v, vTk)
     dma("y", T.stD[:], T.D[:, :], "dD", vD)
-    tD = dma("y", T.landD[me], T.D[4 * me:4 * me + 4, :], "dD")
-    tVR = dma("y", T.VR[:, :], T.landV[:], "dVR", ("arrV", 14), tV)
-    tY = dma("y", T.stY[:], T.Tk[:, :], "dY", vTk)
-    dma("s", T.yt[lo:hi, :], T.Tk[lo:hi, :], "oY1", vTk)
-    send("stD", "landD", "arrD", tD)
-    send("stY", "landY", "arrY", tY)
-    tKD = dma("y", T.KD[:, :], T.landD[:], "dKD", ("arrD", 14), tD)
+    tD = dma("s", T.landD[me], T.D[4 * me:4 * me + 4, :], "dD", vD)
+    xD = send(lambda n: T.stD[n], T.landD[me], "arrD", tD)
+    tKD = dma("y", T.KD[:, :], T.landD[:], "dKD", xD, tD)
+    vW = V(cpy(T.FIN[:, 12 * me:12 * me + 12], T.F5[:, :]), v5)
+    v = V(cpy(T.TkO[:, :], T.YI[:, :]), tYI)
+    v = V(cpy(T.HO[:, :], T.TkO[:, :].indirect(T.AO[:, 0:12])), v)
+    vG = V(tt(T.DgO[:, :], T.pE[:, 0:192], T.HO[:, :], A.subtract), v, pO)
+    v = V(tt(T.Wt[:, :], T.FIN[:, :].indirect(T.LH[:, :]), T.C15[:, :], A.is_equal), xW, vW)
+    h = 64 * (me // 4)
+    m = MM([v], (T.pW[:, 0:128], T.Wt[:, 0:128], T.Ib[:, :], True, True), (T.pW[:, 128:192], T.Wt[:, 128:256], T.Ib[:, h:h + 64], True, True))
+    v = V(tt(T.WD[:, :], T.pW[:, 0:192], T.DgO[:, :], A.mult), m, vG)
+    v = V(lambda e: e.tensor_tensor(T.TkO[:, :].indirect(T.AO[:, 0:12]), T.HO[:, :], T.WD[:, :], A.add), v)
+    dma("s", T.yt[:], T.TkO[:, :], "oY", v)
     m = MM([tKD, sV], (T.pZ[:, :], T.R8b[:, :], T.KD[:, :], True, True))
     v = V(tt(T.YP[:, :], T.pZ[:, :], T.VR[:, :], A.max), m, tVR)
     dma("y", T.yp[:], T.YP[:, :], "oP", v)
-    need("s", [("arrY", 14)])
-    if me > 0:
-        dma("s", T.yt[0:lo, :], T.landY[0:me], "oY2")
-    if me < 7:
-        dma("s", T.yt[hi:128, :], T.landY[me + 1:8], "oY2")
     need("g", [(s, n) for s, n in cnt.items() if n])

@@ -3,6 +3,7 @@ from concourse.mybir import AluOpType, ActivationFunctionType
 
 RO = 5
 NV = 16
+NV0 = 0
 F32, BF, FH, I32, U16 = "float32", "bfloat16", "float16", "int32", "uint16"
 SCRATCH = {}
 
@@ -12,23 +13,24 @@ def _b(where, dtype, **kw):
         SCRATCH[k] = (where, s, dtype)
 
 
-_b("dram", U16, stP=[8, 128, 57], landP=[8, 128, 57], stT=[8, 128, 64], landT=[8, 128, 64], stY=[8, 128, 64], landY=[8, 128, 64])
+_b("dram", U16, stP=[8, 128, 50], landP=[8, 128, 50], stT=[8, 128, 72], landT=[8, 128, 72], stY=[8, 128, 64], landY=[8, 128, 64])
 _b("dram", F32, stV=[8, 128, 64], landV=[8, 128, 64])
 _b("dram", BF, stD=[8, 128, 4], landD=[8, 128, 4])
 _b("sbuf", I32, P2=[128, 512], ii=[128, 192], col=[128, 272], cp=[128, 1], ci=[128, 4], cq8=[128, 256], iia=[128, 192],
    cola=[128, 256], t12b=[128, 24], seg=[128, 272], slot=[128, 272], Cl=[128, 12], Cti=[128, 12], RH=[128, 192], OT=[128, 72],
    TkH=[128, 512], BI=[128, 12], UI=[128, 36], FI=[128, 12], F5=[128, 12], FIN=[128, 96])
-_b("sbuf", U16, LI=[128, 24], LC=[128, 12], LH=[128, 16], AT=[128, 60], SN=[128, 60], H16=[128, 192], PO=[128, 456],
-   PI=[128, 456], TO=[128, 512], TI=[128, 512], YO=[128, 512], YI=[128, 512], AO=[128, 24])
-_b("sbuf", F32, P=[128, 4096], KC=[128, 24], IN=[128, 128], IJ=[128, 136], REPf=[128, 256], R0=[128, 272], EM=[128, 192],
-   DM=[128, 192], SM=[128, 192], C15=[128, 256], INC=[128, 204], SH1=[128, 128], Clf=[128, 12], Ctf=[128, 12], E=[128, 192],
+_b("sbuf", U16, LI=[128, 24], LC=[128, 12], LH=[128, 16], AT=[128, 60], SN=[128, 60], H16=[128, 192], PO=[128, 400],
+   PI=[128, 400], TO=[128, 576], TI=[128, 576], YO=[128, 512], YI=[128, 512], AH=[128, 24], AO=[128, 24])
+_b("sbuf", F32, P=[128, 4096], KC=[128, 24], EM=[128, 192], HO2=[128, 192],
+   DM=[128, 192], SM=[128, 192], C15=[128, 256], INC=[128, 204], SH1=[128, 128], Clf=[128, 12],
    RJ=[128, 192], RR0=[128, 3072], RR1=[128, 3072], RR2=[128, 3072], RR3=[128, 3072], RR4=[128, 3072], Tk=[128, 512],
    Hf=[128, 192], Dg=[128, 192], WD=[128, 192], AS=[128, 204], XS=[128, 204], UF=[128, 24], S0=[128, 192], S1=[128, 192],
-   VAL=[128, 512], VR=[128, 512], YP=[128, 512], COf=[128, 12], EO=[128, 192], TkO=[128, 512], HO=[128, 192], DgO=[128, 192])
-_b("sbuf", FH, P2h=[128, 512], GY=[128, 1024], Ih=[128, 128])
+   VAL=[128, 512], VR=[128, 512], YP=[128, 512], COf=[128, 12], TkO=[128, 512], HO=[128, 192], DgO=[128, 192])
+_b("sbuf", FH, P2h=[128, 512], GY=[128, 1024], Ih=[128, 128], IN=[128, 128], IJ=[128, 136], REPf=[128, 256], R0=[128, 272],
+   E=[128, 192], EO=[128, 192], Hh=[128, 192])
 _b("sbuf", BF, iotA=[128, 32], iotB=[128, 128], SelF=[128, 8], SelE=[128, 8], Ib=[128, 128], IM=[128, 128], RS=[128, 272],
    NEG=[128, 128], C16=[128, 204], C4=[128, 36], SH2=[128, 128], YS=[128, 240], R8b=[8, 128], Et=[128, 192], N0=[128, 512],
-   N1=[128, 512], hib=[128, 192], ZV=[128, 192], F=[128, 4096], Z=[128, 4096], EQ=[128, 3072], FG=[128, 3072], FS=[128, 192],
+   Y32=[128, 64], hib=[128, 192], ZV=[128, 192], F=[128, 4096], Z=[128, 4096], EQ=[128, 3072], FG=[128, 3072], FS=[128, 192],
    M=[128, 204], Wt=[128, 256], TA=[128, 384], OA=[128, 384], OB=[128, 1536], D=[32, 128], KD=[8, 512])
 _BANKS = ["pA", "pX", "pM", "pG", "pW", "pD", "pZ", "pE"]
 _b("psum", F32, **{k: [128, 512] for k in _BANKS})
@@ -130,19 +132,19 @@ def rank_program(g, core, T, topo):
         t = dma("y", T[land][me], T[buf][lo:hi, :], sem)
         return [t, send(lambda n: T[st][n], T[land][me], arr, t)]
 
-    dma("y", T.OT[:, 0:12], T.routes[0::16, :], "dH")
-    dma("y", T.RH[:, :], T.routes[:], "dH")
     dma("y", T.TkH[:, :], T.trunk[:], "dH")
-    for t in range(1, RO):
-        dma("s", T.OT[:, 12 * t:12 * t + 12], T.routes[t::16, :], "dH")
+    dma("s", T.OT[:, 0:12], T.routes[0::16, :], "dH")
+    dma("y", T.RH[:, :], T.routes[:], "dH")
     tH = dma("s", T.OT[:, 60:72], T.calls[:], "dH")
+    for t in range(RO - 1, 0, -1):
+        tO = dma("ys"[t % 2], T.OT[:, 12 * t:12 * t + 12], T.routes[t::16, :], "dO")
     for q in range(8):
         tP2 = dma("ys"[q % 2], T.P2[16 * q:16 * q + 16, :], T.paths[lo:hi, 512 * q:512 * q + 512], "dP2")
     g1 = op("g", lambda e: e.iota(T.cp[:, 0:1], [[0, 1]], 0, 1))
     g2 = op("g", lambda e: e.iota(T.col[:, :], [[1, 272]], 0, 0))
     g3 = op("g", lambda e: e.iota(T.ii[:, :], [[1, 12], [12, 16]], 0, 0))
     g4 = op("g", lambda e: e.iota(T.seg[:, :], [[0, 2], [1, 8], [0, 17]], 0, 0))
-    g5 = op("g", lambda e: e.iota(T.slot[:, :], [[0, 16], [1, 17]], 0, 0))
+    g5 = op("g", lambda e: e.iota(T.slot[:, :], [[0, 2], [1, 8], [8, 17]], 0, 0))
     KC, col, ci = T.KC, T.col, T.ci
 
     def kc(n):
@@ -164,18 +166,23 @@ def rank_program(g, core, T, topo):
         v = V(ts(T.GY[:, 128 * y:128 * y + 128], T.DM[:, 0:128], kc(16 + y), A.mult))
     V(cpy(T.LI[:, :], T.t12b[:, :]), v)
     LI, LB = T.LI[:, 0:12], T.LI[:, 12:24]
-    v = V(ts(T.OT[:, 0:60], T.OT[:, 0:60], 511, A.bitwise_and), tH)
-    v = V(cpy(T.PO[:, 384:456], T.OT[:, :]), v)
+    V(fill(T.PO[:, 396:400], 0))
+    v = V(fill(T.TO[:, 572:576], 0))
+    V(ts(T.TO[:, 512:524], T.OT[:, 0:12], -512.0 * me, A.add), tH, v)
+    v = V(cpy(T.PO[:, 384:396], T.OT[:, 60:72]))
     V(cpy(T.PO[:, 192:384], T.RH[:, :].indirect(LI)))
-    v = V(cpy(T.PO[:, 0:192], T.TkH[:, :].indirect(T.PO[:, 384:396])), v)
-    xP = exchange("PO", "stP", "landP", "dP", "arrP", v)
+    vPO = V(cpy(T.PO[:, 0:192], T.TkH[:, :].indirect(T.TO[:, 512:524])), v)
+    v = V(ts(T.OT[:, 12:60], T.OT[:, 12:60], 511, A.bitwise_and), tO)
+    v = V(cpy(T.AH[:, :], T.OT[:, 48:72]), v)
+    xA = send(lambda n: T.AH[:, :], T.AO[:, :], "arrA", v, to=[(me + RO - 1) % 8], each=8)
+    xP = exchange("PO", "stP", "landP", "dP", "arrP", vPO)
     vPh = V(ts(T.P2h[:, :], T.P2[:, :], -2048.0, A.add), tP2)
     for y in range(8):
         m = MM([vPh], (T[_BANKS[y]][:, :], T.GY[:, 128 * y:128 * y + 128], T.P2h[:, :], True, True))
         tP = S(act(T.P[:, 512 * y:512 * y + 512], T[_BANKS[y]][:, :], AF.Identity, bias=-2048.0), m)
-    v = V(cpy(T.TO[:, :], T.TkH[:, :]))
+    V(cpy(T.TO[:, 524:572], T.OT[:, 12:60]))
+    v = V(cpy(T.TO[:, 0:512], T.TkH[:, :]))
     xT = exchange("TO", "stT", "landT", "dT", "arrT", v)
-    xA = send(lambda n: T.PO[:, 432:456], T.AO[:, :], "arrA", to=[(me + RO - 1) % 8], each=8)
     v = V(ts(kc(3), ci[:, 1:2], 4.0, A.mult, 3.0, A.add))
     vN0 = V(ts(T.N0[:, :], T.P2[:, :], 4096.0, A.is_ge))
     vN0 = V(ts(T.C4[:, :], col[:, 0:36], kc(3), A.is_equal), v)
@@ -197,8 +204,11 @@ def rank_program(g, core, T, topo):
     V(ts(kc(7), ci[:, 0:1], 5.0, A.is_lt))
     V(ts(kc(8), ci[:, 0:1], 5.0, A.is_ge, -5.0, A.mult))
     V(ts(kc(9), T.cp[:, 0:1], 5.0, A.add))
-    V(ts(kc(10), T.cp[:, 0:1], 0.0, A.is_equal, 16.0, A.mult))
+    V(ts(kc(14), T.cp[:, 0:1], 0.0, A.is_equal, 16.0, A.mult))
+    V(ts(kc(15), T.cp[:, 0:1], 1.0, A.is_equal, float(3 * 2 ** 24), A.mult))
+    V(ts(kc(13), ci[:, 0:1], 0.0, A.is_equal))
     v = V(ts(kc(11), T.cp[:, 0:1], kc(2), A.add, 1.0, A.add))
+    V(tt(kc(10), kc(14), kc(15), A.add), v)
     V(ts(kc(12), ci[:, 0:1], kc(8), A.add, 112.0, A.add), v)
     V(ts(T.EM[:, :], T.iia[:, :], kc(1), A.is_equal))
     V(ts(T.REPf[:, :], T.cq8[:, :], kc(2), A.is_equal))
@@ -218,37 +228,45 @@ def rank_program(g, core, T, topo):
     V(ts(T.SelF[:, :], col[:, 0:8], kc(2), A.is_equal, kc(6), A.mult))
     V(ts(T.SelE[:, :], col[:, 0:8], kc(2), A.is_equal, float(2 ** 17), A.mult))
     V(fill(T.NEG[:, :], -1.0))
-    V(ts(T.C16[:, :], T.slot[:, 0:204], 0.0, A.not_equal, kc(10), A.mult), g5)
-    V(ts(T.INC[:, :], T.slot[:, 0:204], 0.0, A.is_equal, -float(2 ** 24), A.mult))
-    V(fill(T.R0[:, :], 0.0))
-    v = V(ts(T.RS[:, :], T.seg[:, :], kc(2), A.is_equal, 32.0, A.mult), g4)
-    V(ts(T.R0[:, 0::17], T.seg[:, 0::17], kc(2), A.is_equal, -32.0, A.mult), v)
-    V(fill(T.RS[:, 0::17], 0.0))
+    V(ts(T.C16[:, :], T.slot[:, 0:204], 8.0, A.is_ge, kc(10), A.mult), g5)
+    V(ts(T.INC[:, :], T.slot[:, 0:204], 8.0, A.is_lt, -float(2 ** 24), A.mult))
+    v = V(ts(T.RS[:, :], T.seg[:, :], kc(2), A.is_equal, 16384.0, A.mult), g4)
+    V(ts(T.R0[:, :], T.slot[:, :], kc(2), A.is_equal, -32.0, A.mult))
+    V(fill(T.RS[:, 0::17], 0.0), v)
     V(ts(T.INC[:, :], T.INC[:, :], 1.0, A.add))
     V(ts(T.C15[:, :], T.cola[:, :], -1.0, A.mult, 15.0, A.add))
     V(ts(T.iotA[:, :], col[:, 0:32], -1.0, A.mult, 31.0, A.add))
     V(ts(T.iotB[:, :], col[:, 0:128], -1.0, A.mult, 127.0, A.add))
     V(ts(T.R8b[:, :], T.cq8[0:8, 0:128], KC[0:8, 0:1], A.is_equal, 4096.0, A.mult))
-    vC = V(fill(T.Z[:, :], 0.0))
+    V(ts(T.Y32[:, :], col[:, 0:64], 31.0, A.is_equal, kc(13), A.mult))
+    vC = V(fill(T.Z[:, 0:2048], 0.0))
+    sZ = S(act(T.Z[:, 2048:4096], T.P[:, 0:2048], scale=0.0), tP)
 
     tPI = dma("y", T.PI[:, :], T.landP[:], "dPI", *xP)
-    tTI = dma("y", T.TI[:, :], T.landT[:], "dTI", *xT)
 
     def turn(dst, src, u, sem, *deps):
         dma("y", dst(16 * u, 128), src(0, 128 - 16 * u), sem, *deps)
         return dma("y", dst(0, 16 * u), src(128 - 16 * u, 128), sem)
+    tTI = dma("y", T.TI[:, :], T.landT[:], "dTI", *xT)
+    for u in range(1, RO):
+        tAT = turn(lambda a, b: T.AT[a:b, 12 * u:12 * u + 12], lambda a, b: T.TI[a:b, 512 + 12 * u:524 + 12 * u], u, "dAT", tTI)
 
     def rep(t):
         return T.REPf[:, 16 * (8 - t):16 * (16 - t)]
     RR = [T["RR%d" % t] for t in range(RO)]
     vRJ = V(ts(T.RJ[:, :], T.PI[:, 192:384], -4096.0, A.add), tPI, vC)
-    for p in range(8):
-        a = V(cpy(T.RR0[:, 2048 + p::16], T.RJ[:, 128:192]), vRJ)
-        b = S(act(T.RR0[:, 2056 + p::16], T.RJ[:, 128:192]), vRJ)
+    v = V(ts(T.Clf[:, :], T.PI[:, 384:396], -2048.0, A.add))
+    V(ts(T.Hh[:, :], T.PI[:, 0:192], -2048.0, A.add))
+    v = V(tt(T.E[:, :], T.Clf[:, :].indirect(LB), T.EM[:, :], A.mult), v)
+    for p in range(16):
+        if p < 5:
+            a = V(cpy(T.RR0[:, 2048 + p::16], T.RJ[:, 128:192]), vRJ)
+        else:
+            b = S(act(T.RR0[:, 2048 + p::16], T.RJ[:, 128:192]), vRJ)
+    hh = V(ts(T.Et[:, :], T.E[:, :], 1.0 / 512, A.mult, 192.0 - 255.5 / 512, A.add), v)
     for p in range(16):
         c = S(act(T.RR0[:, p:2048:16], T.RJ[:, 0:128]))
     rr = [[[a, b], [c]]] + [None] * 4
-    sH = S(act(T.hib[:, :], T.RJ[:, :]))
 
     def to_seekers(out, l, w, o, last):
         return [(out[0:64, 136:204], l[:, 128:192], w[:, o:o + 68], False, False),
@@ -266,14 +284,15 @@ def rank_program(g, core, T, topo):
 
     for t in range(RO):
         if t == 0:
-            at, H, h16 = T.PI[:, 384:396], T.PI, tPI
-            hf = V(cpy(T.Hf[:, :], T.PI[:, 0:192]))
+            at, H, h16 = T.TI[:, 512:524], T.PI, tPI
         else:
             at, H = T.AT[:, 12 * t:12 * t + 12], T.H16
             h16 = V(cpy(T.H16[:, :], T.Tk[:, :].indirect(at)), vTk, tAT)
             hf = S(act(T.Hf[:, :], T.Tk[:, :].indirect(at)), vTk, tAT)
+            hh = V(ts(T.Hh[:, :], T.H16[:, :], -2048.0, A.add), h16)
         if t == RO - 1:
             xY = exchange("YO", "stY", "landY", "dY", "arrY", V(cpy(T.YO[:, :], T.Tk[:, :])))
+            tVR = dma("y", T.VR[:, :], T.landV[:], "dVR", *xV)
             tYI = dma("y", T.YI[:, :], T.landY[:], "dYI", *xY)
         else:
             x = turn(lambda a, b: RR[t + 1][a:b, :], lambda a, b: T.RR0[a:b, :], t + 1, "dRR%d" % t, tF, *(rr[0][0] + rr[0][1]))
@@ -286,109 +305,119 @@ def rank_program(g, core, T, topo):
             o, w = T.FG[:, 16 * a:16 * b], T.F[:, :].indirect(H[:, a:b])
             return op(q, act(o, w) if q == "s" else cpy(o, w), h16, tF)
         e1 = eq(128, 192, 0)
-        if t == 0:
-            V(cpy(T.Cl[:, :], T.PI[:, 444:456]))
-            v = V(cpy(T.Clf[:, :], T.PI[:, 444:456]))
-            V(ts(T.Cti[:, :], T.Cl[:, :], 3584, A.bitwise_and), v)
-            v = V(tt(T.E[:, :], T.Clf[:, :].indirect(LB), T.EM[:, :], A.mult))
-            pS = MM([v, tP], (T.pE[:, 0:192], rep(0), T.E[:, :], True, True))
-            v = V(cpy(T.Ctf[:, :], T.Cti[:, :]), v)
-            vE = V(tt(T.Et[:, :], T.Ctf[:, :].indirect(LB), T.EM[:, :], A.mult), v)
-            m = MM([sH], (T.pW[:, 0:192], T.SH1[:, :], T.RJ[:, :], True, False), (T.pW[:, 0:192], T.SH2[:, :], T.hib[:, :], False, True))
-            sZV = S(act(T.ZV[:, :], T.pW[:, 0:192]), m)
-            v = V(tt(T.S0[:, :], T.pE[:, 0:192], T.DM[:, :], A.mult), pS)
-            v = V(scan(T.S1[:, :], T.SM[:, :], T.S0[:, :], A.mult, A.add), v)
-            vSN = V(cpy(T.SN[:, 0:12], T.S1[:, 15::16]), v)
-            vZ = V(cpy(T.Z[:, :].indirect(T.SN[:, 0:12]), T.ZV[:, :]), sZV, vSN)
-            for u in range(1, RO):
-                tAT = turn(lambda a, b: T.AT[a:b, 12 * u:12 * u + 12], lambda a, b: T.PI[a:b, 384 + 12 * u:396 + 12 * u], u, "dAT")
-                tSN = turn(lambda a, b: T.SN[a:b, 12 * u:12 * u + 12], lambda a, b: T.SN[a:b, 0:12], u, "dSN", vSN)
         e0 = eq(0, 128, 1)
         o = 17 * (8 - t)
-        pm = MM([hf, vE], (T.pM[:, 0:204], T.NEG[:, :], T.C16[:, :], True, False),
-                *(to_seekers(T.pM, T.Et, T.RS, o, False) + to_seekers(T.pM, T.Hf, T.IJ, 0, True)))
-        if t < RO - 1:
-            pg = MM([], (T.pG[:, 0:192], rep(t), T.E[:, :], True, False), (T.pG[:, 0:192], T.IN[:, :], T.Hf[:, :], False, True))
+        pm = MM([hh, tP], (T.pM[:, 0:204], T.NEG[:, :], T.C16[:, :], True, False),
+                *(to_seekers(T.pM, T.Et, T.RS, o, False) + to_seekers(T.pM, T.Hh, T.IJ, 0, True)))
         sM = S(act(T.M[:, :], T.pM[:, 0:204], AF.Sign), pm)
+        if t == 0:
+            sH = S(act(T.hib[:, :], T.RJ[:, :]))
         f1 = fg("s", 128, 192)
         MM([sM], (T.pA[:, 0:204], T.IM[:, :], T.M[:, :], True, False),
-           *(to_seekers(T.pA, T.Hf, T.IJ, 0, False) + to_seekers(T.pA, T.E, T.R0, o, False)))
-        MM([e1], *trunks(T.pA, T.EQ, T.SelE, 1, False))
-        MM([f1], *trunks(T.pX, T.FG, T.SelF, 1, True))
+           *(to_seekers(T.pA, T.Hh, T.IJ, 0, False) + to_seekers(T.pA, T.E, T.R0, o, False)))
         if t == 0:
-            pz = MM([vZ], (T.pZ[:, :], T.Ih[:, :], T.P2h[:, :], True, False),
-                    *[(T.pZ[:, :], T.YS[:, 112 - 16 * q:240 - 16 * q], T.Z[:, 512 * q:512 * q + 512], False, q == 7) for q in range(8)])
-        f0 = fg("s", NV, 128)
+            m = MM([sH], (T.pW[:, 0:192], T.SH1[:, :], T.RJ[:, :], True, False), (T.pW[:, 0:192], T.SH2[:, :], T.hib[:, :], False, True))
+            pS = MM([], (T.pE[:, 0:192], rep(0), T.E[:, :], True, True))
+        MM([e1], *trunks(T.pA, T.EQ, T.SelE, 1, False))
+        if t < RO - 1:
+            pg = MM([], (T.pG[:, 0:192], rep(t), T.E[:, :], True, False), (T.pG[:, 0:192], T.IN[:, :], T.Hh[:, :], False, True))
+        if t == 0:
+            sZV = S(act(T.ZV[:, :], T.pW[:, 0:192]), m)
+            v = V(tt(T.S0[:, :], T.pE[:, 0:192], T.DM[:, :], A.mult), pS)
+            hf = V(cpy(T.Hf[:, :], T.PI[:, 0:192]))
+            v = V(scan(T.S1[:, :], T.SM[:, :], T.S0[:, :], A.mult, A.add), v)
+            vSN = V(ts(T.SN[:, 0:12], T.S1[:, 15::16], 2048.0, A.add), v)
+            vZ = V(cpy(T.Z[:, :].indirect(T.SN[:, 0:12]), T.ZV[:, :]), sZV, vSN, sZ)
+            for u in range(1, RO):
+                tSN = turn(lambda a, b: T.SN[a:b, 12 * u:12 * u + 12], lambda a, b: T.SN[a:b, 0:12], u, "dSN", vSN)
+        MM([f1], *trunks(T.pX, T.FG, T.SelF, 1, True))
+        nv = NV if t else NV0
+        f0 = fg("s", nv, 128)
         if t:
             fs = V(cpy(T.FS[:, :], T.F[:, :].indirect(T.SN[:, 12 * t:12 * t + 12])), tSN, tF)
             MM([vD], (T.pD[0:32, 0:128], T.Ib[0:32, 0:32], T.D[:, :], True, False))
         pa = MM([e0], *trunks(T.pA, T.EQ, T.SelE, 0, False))
         mine = (T.FS[:, 0:128], T.FS[:, 128:192]) if t else (T.NEG[:, 0:128], T.NEG[:, 0:64])
         MM([fs if t else None], *(slots(T.pX, mine, T.SelF, 0, 0, True) + slots(T.pX, mine, T.SelF, 0, 1, True)))
-        fv = fg("v", 0, NV)
+        fv = fg("v", 0, nv) if nv else None
         px = MM([f0, fv], *trunks(T.pX, T.FG, T.SelF, 0, True))
+        if t == 0:
+            MM([vZ], *(count_none(T.N0, True, False) + [(T.pD[0:32, 0:128], T.Y32[:, 31 - a:63 - a], T.Z[:, 128 * a:128 * a + 128],
+                                                         False, False) for a in range(32)]))
         v = V(scan(T.AS[:, :], T.INC[:, :], T.pA[:, 0:204], A.add, A.max), pa)
-        v = V(ts(T.BI[:, :], T.AS[:, 16::17], 131040.0, A.add), v)
-        V(ts(T.UI[:, 12:24], T.BI[:, :], 12, A.arith_shift_right, 31, A.bitwise_and), v)
-        v = V(ts(T.UI[:, 0:12], T.BI[:, :], 5, A.arith_shift_right, 127, A.bitwise_and))
+        v = V(ts(T.BI[:, :], T.AS[:, 16::17], 32.0 * 2047, A.add), v)
+        v = V(ts(T.UI[:, 12:24], T.BI[:, :], 12, A.arith_shift_right, 31, A.bitwise_and), v)
+        w = V(ts(T.UI[:, 0:12], T.BI[:, :], 5, A.arith_shift_right, 127, A.bitwise_and))
         vP = V(ts(T.UI[:, 24:36], T.BI[:, :], 31, A.bitwise_and))
         va = V(cpy(T.UF[:, 12:24], T.UI[:, 12:24]), v)
-        vb = V(ts(T.UF[:, 0:12], T.UI[:, 0:12], 1008.0, A.add))
-        if t == 0:
-            sN = S(act(T.N1[:, :], T.pZ[:, :], AF.Relu, bias=-2047.0), pz)
+        vb = V(ts(T.UF[:, 0:12], T.UI[:, 0:12], 1008.0, A.add), w)
         if t < RO - 1:
             sG = S(act(T.Dg[:, :], T.pG[:, 0:192]), pg)
         sA = []
         for h in range(2):
             for c in range(6 * h, 6 * h + 6):
                 s = S(act(T.TA[:, 32 * c:32 * c + 32], T.iotA[:, :], AF.Abs, bias=T.UF[:, 12 + c:13 + c], scale=-1.0), va)
-            sA += [S(act(T.OA[:, 192 * h:192 * h + 192], T.TA[:, 192 * h:192 * h + 192], AF.Relu, bias=16.0, scale=-16.0), s)] * 6
+            sA += [S(act(T.OA[:, 192 * h:192 * h + 192], T.TA[:, 192 * h:192 * h + 192], AF.Relu, bias=8192.0, scale=-8192.0), s)] * 6
         vX = V(scan(T.XS[:, :], T.INC[:, :], T.pX[:, 0:204], A.add, A.max), px)
+        ob = []
+
+        def kills(n):
+            for c in range(len(ob), len(ob) + n):
+                ob.append(V(ts(T.OB[:, 128 * c:128 * c + 128], T.iotB[:, :], T.XS[:, 17 * c + 16:17 * c + 17], A.subtract,
+                               T.UF[:, c:c + 1], A.is_equal), vX, vb))
+        if t == RO - 1:
+            kills(8)
         v = V(tt(T.FI[:, :], T.XS[:, 16::17], T.UI[:, 24:36], A.max), vP, vX)
+        kills(2)
         v5 = V(ts(T.F5[:, :], T.FI[:, :], 31, A.bitwise_and), v)
-        if t == 0:
-            MM([sN], *count_none(T.N1, True, False))
+        kills(2)
         if t == RO - 1:
             xW = send(lambda n: T.F5[:, :], T.FIN[:, 12 * me:12 * me + 12], "arrW", v5)
         else:
             v = V(tt(T.Wt[:, 0:192], T.F5[:, :].indirect(T.LC[:, :]), T.C15[:, 0:192], A.is_equal), v5)
-            m = MM([v], (T.pW[:, 0:128], T.Wt[:, 0:128], T.Ib[:, :], True, True),
-                   (T.pW[0:64, 128:192], T.Wt[:, 128:192], T.Ib[:, 0:64], True, True),
-                   (T.pW[64:128, 128:192], T.Wt[:, 128:192], T.Ib[:, 64:128], True, True))
+            kills(8)
         for c in range(12):
-            x = V(ts(T.OB[:, 128 * c:128 * c + 128], T.iotB[:, :], T.XS[:, 17 * c + 16:17 * c + 17], A.subtract,
-                     T.UF[:, c:c + 1], A.is_equal), vX, vb)
-            pd = MM([x, sA[c]], (T.pD[0:32, 0:128], T.OA[:, 32 * c:32 * c + 32], T.OB[:, 128 * c:128 * c + 128], False, c == 11))
+            pd = MM([ob[c], sA[c]], (T.pD[0:32, 0:128], T.OA[:, 32 * c:32 * c + 32], T.OB[:, 128 * c:128 * c + 128], False, c == 11))
+            if c == 3 and t < RO - 1:
+                m = MM([v], (T.pW[:, 0:128], T.Wt[:, 0:128], T.Ib[:, :], True, True),
+                       (T.pW[0:64, 128:192], T.Wt[:, 128:192], T.Ib[:, 0:64], True, True),
+                       (T.pW[64:128, 128:192], T.Wt[:, 128:192], T.Ib[:, 64:128], True, True))
         vD = S(act(T.D[:, :], T.pD[0:32, 0:128], AF.Sign, bias=(0.0 if t else -15.5)), pd, tF)
         if t == RO - 1:
             break
         tF = flags_to_F(vD)
         if t == 0:
-            vTk = V(cpy(T.Tk[:, :], T.TI[:, :]), tTI)
-            sV = S(act(T.VAL[:, :], T.pZ[:, :], AF.Identity, bias=2048.0))
+            vTk = V(cpy(T.Tk[:, :], T.TI[:, 0:512]), tTI)
+        if t < 3:
+            ms = [(T.pZ[:, :], T.Ih[:, :], T.P2h[:, :], True, False)] + [
+                (T.pZ[:, :], T.YS[:, 112 - 16 * q:240 - 16 * q], T.Z[:, 512 * q:512 * q + 512], False, q == 7) for q in range(8)]
+            pz = MM([], *ms[3 * t:3 * t + 3])
+        if t == 2:
+            sV = S(act(T.VAL[:, :], T.pZ[:, :], AF.Identity, bias=2048.0), pz)
             xV = exchange("VAL", "stV", "landV", "dV", "arrV", sV)
-        if t == 1:
-            v = V(cpy(T.COf[:, :], T.AO[:, 12:24]), xA)
-            v = V(tt(T.EO[:, :], T.COf[:, :].indirect(LB), T.EM[:, :], A.mult), v)
-            pO = MM([v], (T.pE[:, 0:192], rep(0), T.EO[:, :], True, True))
-            tVR = dma("y", T.VR[:, :], T.landV[:], "dVR", *xV)
         v = V(tt(T.WD[:, :], T.pW[:, 0:192], T.Dg[:, :], A.mult), m, sG)
-        vTk = V(lambda e: e.tensor_tensor(T.Tk[:, :].indirect(at), T.Hf[:, :], T.WD[:, :], A.add), v, vTk)
-    dma("y", T.stD[:], T.D[:, :], "dD", vD)
+        if t == 1:
+            w = V(ts(T.COf[:, :], T.AO[:, 12:24], -2048.0, A.add), xA)
+        vTk = V(lambda e: e.tensor_tensor(T.Tk[:, :].indirect(at), T.Hf[:, :], T.WD[:, :], A.add), v, vTk, hf)
+        if t == 1:
+            w = V(tt(T.EO[:, :], T.COf[:, :].indirect(LB), T.EM[:, :], A.mult), w)
+            pO = MM([w], (T.pE[:, 0:192], rep(0), T.EO[:, :], True, True))
+    dma("s", T.stD[:], T.D[:, :], "dD", vD)
     tD = dma("s", T.landD[me], T.D[4 * me:4 * me + 4, :], "dD", vD)
     xD = send(lambda n: T.stD[n], T.landD[me], "arrD", tD)
-    tKD = dma("y", T.KD[:, :], T.landD[:], "dKD", xD, tD)
+    tKD = dma("s", T.KD[:, :], T.landD[:], "dKD", xD, tD)
     vW = V(cpy(T.FIN[:, 12 * me:12 * me + 12], T.F5[:, :]), v5)
     v = V(cpy(T.TkO[:, :], T.YI[:, :]), tYI)
-    v = V(cpy(T.HO[:, :], T.TkO[:, :].indirect(T.AO[:, 0:12])), v)
-    vG = V(tt(T.DgO[:, :], T.pE[:, 0:192], T.HO[:, :], A.subtract), v, pO)
+    v = V(ts(T.HO2[:, :], T.TkO[:, :].indirect(T.AO[:, 0:12]), -2048.0, A.add), v)
+    V(cpy(T.HO[:, :], T.TkO[:, :].indirect(T.AO[:, 0:12])))
+    vG = V(tt(T.DgO[:, :], T.pE[:, 0:192], T.HO2[:, :], A.subtract), v, pO)
     v = V(tt(T.Wt[:, :], T.FIN[:, :].indirect(T.LH[:, :]), T.C15[:, :], A.is_equal), xW, vW)
     h = 64 * (me // 4)
     m = MM([v], (T.pW[:, 0:128], T.Wt[:, 0:128], T.Ib[:, :], True, True), (T.pW[:, 128:192], T.Wt[:, 128:256], T.Ib[:, h:h + 64], True, True))
     v = V(tt(T.WD[:, :], T.pW[:, 0:192], T.DgO[:, :], A.mult), m, vG)
     v = V(lambda e: e.tensor_tensor(T.TkO[:, :].indirect(T.AO[:, 0:12]), T.HO[:, :], T.WD[:, :], A.add), v)
-    dma("s", T.yt[:], T.TkO[:, :], "oY", v)
+    dma("y", T.yt[:], T.TkO[:, :], "oY", v)
     m = MM([tKD, sV], (T.pZ[:, :], T.R8b[:, :], T.KD[:, :], True, True))
     v = V(tt(T.YP[:, :], T.pZ[:, :], T.VR[:, :], A.max), m, tVR)
-    dma("y", T.yp[:], T.YP[:, :], "oP", v)
+    dma("s", T.yp[:], T.YP[:, :], "oP", v)
     need("g", [(s, n) for s, n in cnt.items() if n])

@@ -4,6 +4,8 @@ from concourse.mybir import AluOpType, ActivationFunctionType
 RO = 5
 NV = 16
 NV0 = 0
+RV = 5
+K1 = 2
 F32, BF, FH, I32, U16 = "float32", "bfloat16", "float16", "int32", "uint16"
 SCRATCH = {}
 
@@ -13,14 +15,14 @@ def _b(where, dtype, **kw):
         SCRATCH[k] = (where, s, dtype)
 
 
-_b("dram", U16, stP=[8, 128, 50], landP=[8, 128, 50], stT=[8, 128, 72], landT=[8, 128, 72], stY=[8, 128, 64], landY=[8, 128, 64])
+_b("dram", I32, stR=[8, 128, 32], landR=[8, 128, 32])
+_b("dram", U16, stP=[8, 128, 24], landP=[8, 128, 24], stT=[8, 128, 64], landT=[8, 128, 64], stY=[8, 128, 64], landY=[8, 128, 64])
 _b("dram", F32, stV=[8, 128, 64], landV=[8, 128, 64])
-_b("dram", BF, stD=[8, 128, 4], landD=[8, 128, 4])
-_b("sbuf", I32, P2=[128, 512], ii=[128, 192], col=[128, 272], cp=[128, 1], ci=[128, 4], cq8=[128, 256], iia=[128, 192],
-   cola=[128, 256], t12b=[128, 24], seg=[128, 272], slot=[128, 272], Cl=[128, 12], Cti=[128, 12], RH=[128, 192], OT=[128, 72],
-   TkH=[128, 512], BI=[128, 12], UI=[128, 36], FI=[128, 12], F5=[128, 12], FIN=[128, 96])
-_b("sbuf", U16, LI=[128, 24], LC=[128, 12], LH=[128, 16], AT=[128, 60], SN=[128, 60], H16=[128, 192], PO=[128, 400],
-   PI=[128, 400], TO=[128, 576], TI=[128, 576], YO=[128, 512], YI=[128, 512], AH=[128, 24], AO=[128, 24])
+_b("sbuf", I32, P2=[128, 512], ii=[128, 192], c12=[128, 12], cp=[128, 1], ci=[128, 4], iia=[128, 192], t12b=[128, 24],
+   R=[128, 192], Cl=[128, 12], OH=[128, 36], OT=[128, 60], TkH=[128, 512], BI=[128, 12], UI=[128, 24], FI=[128, 12], F5=[128, 12])
+_b("sbuf", BF, col=[128, 256], cola=[128, 192], cq8=[128, 256], seg=[128, 272], slot=[128, 272])
+_b("sbuf", U16, LI=[128, 24], LC=[128, 12], LH=[128, 16], AT=[128, 60], SN=[128, 60], H16=[128, 192], PO=[128, 192],
+   PI=[128, 192], TO=[128, 512], TI=[128, 512], YO=[128, 512], YI=[128, 512], A0=[128, 12], AH=[128, 24], AO=[128, 24])
 _b("sbuf", F32, P=[128, 4096], KC=[128, 24], EM=[128, 192], HO2=[128, 192],
    DM=[128, 192], SM=[128, 192], C15=[128, 256], INC=[128, 204], SH1=[128, 128], Clf=[128, 12],
    RJ=[128, 192], RR0=[128, 3072], RR1=[128, 3072], RR2=[128, 3072], RR3=[128, 3072], RR4=[128, 3072], Tk=[128, 512],
@@ -31,13 +33,14 @@ _b("sbuf", FH, P2h=[128, 512], GY=[128, 1024], Ih=[128, 128], IN=[128, 128], IJ=
 _b("sbuf", BF, iotA=[128, 32], iotB=[128, 128], SelF=[128, 8], SelE=[128, 8], Ib=[128, 128], IM=[128, 128], RS=[128, 272],
    NEG=[128, 128], C16=[128, 204], C4=[128, 36], SH2=[128, 128], YS=[128, 240], R8b=[8, 128], Et=[128, 192], N0=[128, 512],
    Y32=[128, 64], hib=[128, 192], ZV=[128, 192], F=[128, 4096], Z=[128, 4096], EQ=[128, 3072], FG=[128, 3072], FS=[128, 192],
-   M=[128, 204], Wt=[128, 256], TA=[128, 384], OA=[128, 384], OB=[128, 1536], D=[32, 128], KD=[8, 512])
+   M=[128, 204], Wt=[128, 256], TA=[128, 384], OA=[128, 384], OB=[128, 1536], D=[32, 128], KD=[8, 512],
+   LO=[128, 64], LN=[128, 64])
 _BANKS = ["pA", "pX", "pM", "pG", "pW", "pD", "pZ", "pE"]
 _b("psum", F32, **{k: [128, 512] for k in _BANKS})
 
-_ARR = ["arrP", "arrT", "arrA", "arrV", "arrY", "arrW", "arrD"]
-_DMA = ["dH", "dO", "dP2", "dP", "dT", "dF", "dPI", "dTI", "dAT", "dRR0", "dRR1", "dRR2", "dRR3", "dSN", "dV", "dVR", "dY", "dYI",
-        "dD", "dKD", "oY", "oP"]
+_ARR = ["arrR", "arrP", "arrT", "arrA", "arrV", "arrY", "arrW"]
+_DMA = ["dR", "dRl", "dCl", "dH", "dO", "dP2", "dP", "dT", "dF", "dPI", "dTI", "dAT", "dRR0", "dRR1", "dRR2", "dRR3", "dSN", "dV", "dVR", "dY", "dYI",
+        "oY", "oP"]
 SEMAPHORES = ["cv", "cs", "cpe", "cg", "sent"] + _ARR + _DMA
 
 
@@ -132,19 +135,28 @@ def rank_program(g, core, T, topo):
         t = dma("y", T[land][me], T[buf][lo:hi, :], sem)
         return [t, send(lambda n: T[st][n], T[land][me], arr, t)]
 
+    dma("y", T.stR[:, 0:96, :], T.routes[:], "dR")
+    dma("s", T.stR[:, 96:102, :], T.calls[:], "dR")
+    dma("s", T.stR[:, 102:128, :], T.trunk[0:13, :], "dR")
+    dma("y", T.landR[me, 0:96, :], T.routes[lo:hi, :], "dR")
+    tR = dma("s", T.landR[me, 96:102, :], T.calls[lo:hi, :], "dR")
     dma("y", T.TkH[:, :], T.trunk[:], "dH")
-    dma("s", T.OT[:, 0:12], T.routes[0::16, :], "dH")
-    dma("y", T.RH[:, :], T.routes[:], "dH")
-    tH = dma("s", T.OT[:, 60:72], T.calls[:], "dH")
-    for t in range(RO - 1, 0, -1):
-        tO = dma("ys"[t % 2], T.OT[:, 12 * t:12 * t + 12], T.routes[t::16, :], "dO")
+    tH = dma("s", T.OH[:, 24:36], T.routes[0::16, :], "dH")
     for q in range(8):
         tP2 = dma("ys"[q % 2], T.P2[16 * q:16 * q + 16, :], T.paths[lo:hi, 512 * q:512 * q + 512], "dP2")
+    dma("y", T.OH[:, 0:12], T.routes[RO - 1::16, :], "dO")
+    tO = dma("s", T.OH[:, 12:24], T.calls[:], "dO")
+    def iota(out, pattern, base=0):
+        return op("g", lambda e: e.iota(out, pattern, base, 0, allow_small_or_imprecise_dtypes=True))
     g1 = op("g", lambda e: e.iota(T.cp[:, 0:1], [[0, 1]], 0, 1))
-    g2 = op("g", lambda e: e.iota(T.col[:, :], [[1, 272]], 0, 0))
-    g3 = op("g", lambda e: e.iota(T.ii[:, :], [[1, 12], [12, 16]], 0, 0))
-    g4 = op("g", lambda e: e.iota(T.seg[:, :], [[0, 2], [1, 8], [0, 17]], 0, 0))
-    g5 = op("g", lambda e: e.iota(T.slot[:, :], [[0, 2], [1, 8], [8, 17]], 0, 0))
+    op("g", lambda e: e.iota(T.c12[:, :], [[1, 12]], 0, 0))
+    g2 = iota(T.cola[:, :], [[0, 12], [1, 16]])
+    g3 = iota(T.col[:, :], [[1, 256]])
+    xR = [tR, send(lambda n: T.stR[n], T.landR[me], "arrR", tR)]
+    op("g", lambda e: e.iota(T.ii[:, :], [[1, 12], [12, 16]], 0, 0))
+    g4 = iota(T.cq8[:, :], [[0, 2], [1, 8], [0, 16]])
+    iota(T.seg[:, :], [[0, 2], [1, 8], [0, 17]])
+    g5 = iota(T.slot[:, :], [[0, 2], [1, 8], [8, 17]])
     KC, col, ci = T.KC, T.col, T.ci
 
     def kc(n):
@@ -157,67 +169,67 @@ def rank_program(g, core, T, topo):
     v = V(cpy(kc(0), T.cp[:, 0:1]))
     V(cpy(KC[:, 1:3], ci[:, 0:2]), v)
     V(ts(kc(4), ci[:, 0:1], 12.0, A.mult))
-    v = V(ts(T.cola[:, :], col[:, 0:256], 15, A.bitwise_and), g2)
-    V(ts(T.t12b[:, 0:12], col[:, 0:12], kc(4), A.add), v)
-    V(ts(T.DM[:, :], T.cola[:, 0:192], kc(1), A.is_equal))
-    v = V(ts(KC[:, 16:24], col[:, 0:8], kc(2), A.is_equal))
+    v = V(ts(kc(3), ci[:, 1:2], 4.0, A.mult, 3.0, A.add))
+    V(ts(T.t12b[:, 0:12], T.c12[:, :], kc(4), A.add), v, g2)
+    v = V(ts(KC[:, 16:24], T.c12[:, 0:8], kc(2), A.is_equal))
     V(ts(T.t12b[:, 12:24], T.t12b[:, 0:12], 4, A.arith_shift_right), v)
     for y in range(8):
-        v = V(ts(T.GY[:, 128 * y:128 * y + 128], T.DM[:, 0:128], kc(16 + y), A.mult))
+        v = V(ts(T.GY[:, 128 * y:128 * y + 128], T.cola[:, 0:128], kc(1), A.is_equal, kc(16 + y), A.mult))
     V(cpy(T.LI[:, :], T.t12b[:, :]), v)
-    LI, LB = T.LI[:, 0:12], T.LI[:, 12:24]
-    V(fill(T.PO[:, 396:400], 0))
-    v = V(fill(T.TO[:, 572:576], 0))
-    V(ts(T.TO[:, 512:524], T.OT[:, 0:12], -512.0 * me, A.add), tH, v)
-    v = V(cpy(T.PO[:, 384:396], T.OT[:, 60:72]))
-    V(cpy(T.PO[:, 192:384], T.RH[:, :].indirect(LI)))
-    vPO = V(cpy(T.PO[:, 0:192], T.TkH[:, :].indirect(T.TO[:, 512:524])), v)
-    v = V(ts(T.OT[:, 12:60], T.OT[:, 12:60], 511, A.bitwise_and), tO)
-    v = V(cpy(T.AH[:, :], T.OT[:, 48:72]), v)
-    xA = send(lambda n: T.AH[:, :], T.AO[:, :], "arrA", v, to=[(me + RO - 1) % 8], each=8)
-    xP = exchange("PO", "stP", "landP", "dP", "arrP", vPO)
-    vPh = V(ts(T.P2h[:, :], T.P2[:, :], -2048.0, A.add), tP2)
-    for y in range(8):
-        m = MM([vPh], (T[_BANKS[y]][:, :], T.GY[:, 128 * y:128 * y + 128], T.P2h[:, :], True, True))
-        tP = S(act(T.P[:, 512 * y:512 * y + 512], T[_BANKS[y]][:, :], AF.Identity, bias=-2048.0), m)
-    V(cpy(T.TO[:, 524:572], T.OT[:, 12:60]))
-    v = V(cpy(T.TO[:, 0:512], T.TkH[:, :]))
-    xT = exchange("TO", "stT", "landT", "dT", "arrT", v)
-    v = V(ts(kc(3), ci[:, 1:2], 4.0, A.mult, 3.0, A.add))
-    vN0 = V(ts(T.N0[:, :], T.P2[:, :], 4096.0, A.is_ge))
-    vN0 = V(ts(T.C4[:, :], col[:, 0:36], kc(3), A.is_equal), v)
-
-    def count_none(n, first, last):
-        return [(T.pD[0:32, 0:128], T.C4[:, 3 - u:35 - u], n[:, 128 * u:128 * u + 128], first and u == 0, last and u == 3)
-                for u in range(4)]
-    m = MM([vN0, tP], *count_none(T.N0, True, True))
-    vD = S(act(T.D[:, :], T.pD[0:32, 0:128], AF.Sign, bias=-15.5), m)
-
-    def flags_to_F(*tok):
-        for q in range(8):
-            t = dma("ys"[q % 2], T.F[16 * q:16 * q + 1, :], T.D[:, :], "dF", *tok)
-        return t
-    tF = flags_to_F(vD, sF)
-    V(ts(T.cq8[:, :], col[:, 0:256], 4, A.arith_shift_right, 7, A.bitwise_and))
-    V(ts(T.iia[:, :], T.ii[:, :], 15, A.bitwise_and), g3)
-    V(ts(kc(6), ci[:, 0:1], 0.0, A.is_equal, 1024.0, A.mult))
+    V(ts(T.C4[:, :], col[:, 0:36], kc(3), A.is_equal), g3)
+    V(ts(kc(6), ci[:, 0:1], 0.0, A.is_equal, 2.0 ** 23, A.mult))
     V(ts(kc(7), ci[:, 0:1], 5.0, A.is_lt))
     V(ts(kc(8), ci[:, 0:1], 5.0, A.is_ge, -5.0, A.mult))
     V(ts(kc(9), T.cp[:, 0:1], 5.0, A.add))
     V(ts(kc(14), T.cp[:, 0:1], 0.0, A.is_equal, 16.0, A.mult))
     V(ts(kc(15), T.cp[:, 0:1], 1.0, A.is_equal, float(3 * 2 ** 24), A.mult))
     V(ts(kc(13), ci[:, 0:1], 0.0, A.is_equal))
-    v = V(ts(kc(11), T.cp[:, 0:1], kc(2), A.add, 1.0, A.add))
-    V(tt(kc(10), kc(14), kc(15), A.add), v)
-    V(ts(kc(12), ci[:, 0:1], kc(8), A.add, 112.0, A.add), v)
-    V(ts(T.EM[:, :], T.iia[:, :], kc(1), A.is_equal))
+    V(ts(kc(11), T.cp[:, 0:1], kc(2), A.add, 1.0, A.add))
+    LI, LB = T.LI[:, 0:12], T.LI[:, 12:24]
+    v = V(ts(T.A0[:, :], T.OH[:, 24:36], -512.0 * me, A.add), tH)
+    vPO = V(cpy(T.PO[:, :], T.TkH[:, :].indirect(T.A0[:, :])), v)
+    xP = exchange("PO", "stP", "landP", "dP", "arrP", vPO)
+    iota(T.C15[:, :], [[0, 16], [-1, 16]], 15)
+    iota(T.iotA[:, :], [[-1, 32]], 31)
+    iota(T.iotB[:, :], [[-1, 128]], 127)
+    vPh = V(ts(T.P2h[:, :], T.P2[:, :], -2048.0, A.add), tP2)
+    vN0 = V(ts(T.N0[:, :], T.P2h[:, :], 2048.0, A.is_ge), vPh)
+
+    def count_none(n, first, last):
+        return [(T.pD[0:32, 0:128], T.C4[:, 3 - u:35 - u], n[:, 128 * u:128 * u + 128], first and u == 0, last and u == 3)
+                for u in range(4)]
+    for y in range(8):
+        m = MM([vPh, vD if y > 1 else None], (T[_BANKS[y]][:, :], T.GY[:, 128 * y:128 * y + 128], T.P2h[:, :], True, True))
+        tP = S(act(T.P[:, 512 * y:512 * y + 512], T[_BANKS[y]][:, :], AF.Identity, bias=-2048.0), m)
+        if y == 1:
+            vD = S(act(T.D[:, :], T.pD[0:32, 0:128], AF.Sign, bias=-15.5), MM([vN0], *count_none(T.N0, True, True)))
+    xT = exchange("TO", "stT", "landT", "dT", "arrT", V(cpy(T.TO[:, :], T.TkH[:, :])))
+    V(ts(T.AH[:, 0:12], T.OH[:, 0:12], -512.0 * ((me + RO - 1) % 8), A.add), tO)
+    v = V(cpy(T.AH[:, 12:24], T.OH[:, 12:24]))
+    xA = send(lambda n: T.AH[:, :], T.AO[:, :], "arrA", v, to=[(me + RO - 1) % 8], each=8)
+    gZ = iota(T.Z[:, 0:1024], [[0, 1024]])
+    sZ = S(act(T.Z[:, 1024:2048], T.P[:, 0:1024], scale=0.0), tP)
+    tRl = dma("y", T.R[:, :], T.landR[:, 0:96, :], "dRl", *xR)
+    tCl = dma("y", T.Cl[:, :], T.landR[:, 96:102, :], "dCl")
+
+    def flags_to_F(queues, *tok):
+        for q in range(8):
+            t = dma(queues[q % len(queues)], T.F[16 * q:16 * q + 1, :], T.D[:, :], "dF", *tok)
+        return t
+    tF = flags_to_F("y", vD, sF)
+    V(ts(T.iia[:, :], T.ii[:, :], 15, A.bitwise_and), g4)
+    V(tt(kc(10), kc(14), kc(15), A.add))
+    v = V(ts(kc(12), ci[:, 0:1], kc(8), A.add, 112.0, A.add))
     V(ts(T.REPf[:, :], T.cq8[:, :], kc(2), A.is_equal))
-    V(cpy(T.LC[:, :], col[:, 0:12]))
-    V(ts(T.LH[:, 0:8], col[:, 0:8], 12.0, A.mult, float(me), A.add))
-    V(ts(T.LH[:, 8:16], col[:, 0:8], 12.0, A.mult, float(8 + me % 4), A.add))
+    V(ts(T.EM[:, :], T.iia[:, :], kc(1), A.is_equal), v)
+    V(ts(T.DM[:, :], T.cola[:, :], kc(1), A.is_equal))
+    V(cpy(T.LC[:, :], T.c12[:, :]))
+    V(ts(T.LH[:, 0:8], T.c12[:, 0:8], 8.0, A.mult, 4.0, A.add))
+    V(ts(T.LH[:, 8:16], T.c12[:, 0:8], 8.0, A.mult, 5.0, A.add))
+    V(fill(T.LO[:, :], 0.0))
     V(ts(T.SH1[:, :], col[:, 0:128], kc(9), A.is_equal, kc(7), A.mult))
     V(ts(T.S0[:, 0:128], col[:, 0:128], kc(0), A.is_equal, kc(7), A.mult))
-    v = V(ts(T.SM[:, :], T.cola[:, 0:192], 0.0, A.not_equal))
+    v = V(ts(T.SM[:, :], T.cola[:, :], 0.0, A.not_equal))
     V(tt(T.SH2[:, :], T.S0[:, 0:128], T.SH1[:, :], A.subtract), v)
     V(ts(T.YS[:, :], col[:, 0:240], kc(12), A.is_equal))
     V(ts(T.Ih[:, :], col[:, 0:128], kc(0), A.is_equal))
@@ -229,44 +241,42 @@ def rank_program(g, core, T, topo):
     V(ts(T.SelE[:, :], col[:, 0:8], kc(2), A.is_equal, float(2 ** 17), A.mult))
     V(fill(T.NEG[:, :], -1.0))
     V(ts(T.C16[:, :], T.slot[:, 0:204], 8.0, A.is_ge, kc(10), A.mult), g5)
-    V(ts(T.INC[:, :], T.slot[:, 0:204], 8.0, A.is_lt, -float(2 ** 24), A.mult))
-    v = V(ts(T.RS[:, :], T.seg[:, :], kc(2), A.is_equal, 16384.0, A.mult), g4)
+    V(fill(T.INC[:, :], 1.0))
+    v = V(ts(T.RS[:, :], T.seg[:, :], kc(2), A.is_equal, 16384.0, A.mult))
     V(ts(T.R0[:, :], T.slot[:, :], kc(2), A.is_equal, -32.0, A.mult))
     V(fill(T.RS[:, 0::17], 0.0), v)
-    V(ts(T.INC[:, :], T.INC[:, :], 1.0, A.add))
-    V(ts(T.C15[:, :], T.cola[:, :], -1.0, A.mult, 15.0, A.add))
-    V(ts(T.iotA[:, :], col[:, 0:32], -1.0, A.mult, 31.0, A.add))
-    V(ts(T.iotB[:, :], col[:, 0:128], -1.0, A.mult, 127.0, A.add))
+    V(fill(T.INC[:, 0::17], -float(2 ** 25)))
     V(ts(T.R8b[:, :], T.cq8[0:8, 0:128], KC[0:8, 0:1], A.is_equal, 4096.0, A.mult))
     V(ts(T.Y32[:, :], col[:, 0:64], 31.0, A.is_equal, kc(13), A.mult))
-    vC = V(fill(T.Z[:, 0:2048], 0.0))
-    sZ = S(act(T.Z[:, 2048:4096], T.P[:, 0:2048], scale=0.0), tP)
+    vC = V(fill(T.Z[:, 2048:4096], 0.0))
 
     tPI = dma("y", T.PI[:, :], T.landP[:], "dPI", *xP)
-
-    def turn(dst, src, u, sem, *deps):
-        dma("y", dst(16 * u, 128), src(0, 128 - 16 * u), sem, *deps)
-        return dma("y", dst(0, 16 * u), src(128 - 16 * u, 128), sem)
+    for t in range(RO):
+        tOT = dma("y", T.OT[16 * t:128, 12 * t:12 * t + 12], T.landR[0:8 - t, 6 * t:6 * t + 6, :], "dAT")
+        if t:
+            tOT = dma("y", T.OT[0:16 * t, 12 * t:12 * t + 12], T.landR[8 - t:8, 6 * t:6 * t + 6, :], "dAT")
     tTI = dma("y", T.TI[:, :], T.landT[:], "dTI", *xT)
-    for u in range(1, RO):
-        tAT = turn(lambda a, b: T.AT[a:b, 12 * u:12 * u + 12], lambda a, b: T.TI[a:b, 512 + 12 * u:524 + 12 * u], u, "dAT", tTI)
+
+    def turn(q, dst, src, u, sem, *deps):
+        dma(q, dst(16 * u, 128), src(0, 128 - 16 * u), sem, *deps)
+        return dma(q, dst(0, 16 * u), src(128 - 16 * u, 128), sem)
 
     def rep(t):
         return T.REPf[:, 16 * (8 - t):16 * (16 - t)]
     RR = [T["RR%d" % t] for t in range(RO)]
-    vRJ = V(ts(T.RJ[:, :], T.PI[:, 192:384], -4096.0, A.add), tPI, vC)
-    v = V(ts(T.Clf[:, :], T.PI[:, 384:396], -2048.0, A.add))
-    V(ts(T.Hh[:, :], T.PI[:, 0:192], -2048.0, A.add))
+    vRJ = V(ts(T.RJ[:, :], T.R[:, :].indirect(LI), -4096.0, A.add), tRl, vC)
+    v = V(ts(T.Clf[:, :], T.Cl[:, :], -2048.0, A.add), tCl)
     v = V(tt(T.E[:, :], T.Clf[:, :].indirect(LB), T.EM[:, :], A.mult), v)
     for p in range(16):
-        if p < 5:
+        if p < RV:
             a = V(cpy(T.RR0[:, 2048 + p::16], T.RJ[:, 128:192]), vRJ)
         else:
             b = S(act(T.RR0[:, 2048 + p::16], T.RJ[:, 128:192]), vRJ)
-    hh = V(ts(T.Et[:, :], T.E[:, :], 1.0 / 512, A.mult, 192.0 - 255.5 / 512, A.add), v)
-    for p in range(16):
-        c = S(act(T.RR0[:, p:2048:16], T.RJ[:, 0:128]))
-    rr = [[[a, b], [c]]] + [None] * 4
+    sH = S(act(T.hib[:, :], T.RJ[:, :]), vRJ)
+    m = MM([sH, tP], (T.pW[:, 0:192], T.SH1[:, :], T.RJ[:, :], True, False), (T.pW[:, 0:192], T.SH2[:, :], T.hib[:, :], False, True))
+    pS = MM([v], (T.pE[:, 0:192], rep(0), T.E[:, :], True, True))
+    V(ts(T.Et[:, :], T.E[:, :], 1.0 / 512, A.mult, 192.0 - 255.5 / 512, A.add), v)
+    hh = V(ts(T.Hh[:, :], T.PI[:, :], -2048.0, A.add), tPI)
 
     def to_seekers(out, l, w, o, last):
         return [(out[0:64, 136:204], l[:, 128:192], w[:, o:o + 68], False, False),
@@ -282,11 +292,24 @@ def rank_program(g, core, T, topo):
     def trunks(out, tab, sel, part, alone):
         return [m for p in range(16) for m in slots(out, (tab[:, p:2048:16], tab[:, 2048 + p:3072:16]), sel, 1 + p, part, alone, p == 15)]
 
+    def may(t, hh):
+        pm = MM([hh, tP], (T.pM[:, 0:204], T.NEG[:, :], T.C16[:, :], True, False),
+                *(to_seekers(T.pM, T.Et, T.RS, 17 * (8 - t), False) + to_seekers(T.pM, T.Hh, T.IJ, 0, True)))
+        return S(act(T.M[:, :], T.pM[:, 0:204], AF.Sign), pm)
+    for p in range(16):
+        c = S(act(T.RR0[:, p:2048:16], T.RJ[:, 0:128]))
+        if p == 5:
+            sZV = S(act(T.ZV[:, :], T.pW[:, 0:192]), m)
+        if p == 9:
+            sM = may(0, hh)
+    rr = [[a, b, c]] + [None] * 4
+
     for t in range(RO):
+        at = T.AT[:, 12 * t:12 * t + 12]
         if t == 0:
-            at, H, h16 = T.TI[:, 512:524], T.PI, tPI
+            H, h16 = T.PI, tPI
         else:
-            at, H = T.AT[:, 12 * t:12 * t + 12], T.H16
+            H = T.H16
             h16 = V(cpy(T.H16[:, :], T.Tk[:, :].indirect(at)), vTk, tAT)
             hf = S(act(T.Hf[:, :], T.Tk[:, :].indirect(at)), vTk, tAT)
             hh = V(ts(T.Hh[:, :], T.H16[:, :], -2048.0, A.add), h16)
@@ -295,62 +318,61 @@ def rank_program(g, core, T, topo):
             tVR = dma("y", T.VR[:, :], T.landV[:], "dVR", *xV)
             tYI = dma("y", T.YI[:, :], T.landY[:], "dYI", *xY)
         else:
-            x = turn(lambda a, b: RR[t + 1][a:b, :], lambda a, b: T.RR0[a:b, :], t + 1, "dRR%d" % t, tF, *(rr[0][0] + rr[0][1]))
-            rr[t + 1] = [[x], [x]]
+            x = turn("y", lambda a, b: RR[t + 1][a:b, :], lambda a, b: T.RR0[a:b, :], t + 1, "dRR%d" % t, tF, tTI, *rr[0])
+            rr[t + 1] = [x]
 
-        def eq(a, b, part):
-            return V(tt(T.EQ[:, 16 * a:16 * b], T.P[:, :].indirect(H[:, a:b]), RR[t][:, 16 * a:16 * b], A.is_equal), h16, tP, *rr[t][part])
+        def eq(a, b):
+            return V(tt(T.EQ[:, 16 * a:16 * b], T.P[:, :].indirect(H[:, a:b]), RR[t][:, 16 * a:16 * b], A.is_equal), h16, tP,
+                     *rr[t][0:2 if a else 3])
 
         def fg(q, a, b):
             o, w = T.FG[:, 16 * a:16 * b], T.F[:, :].indirect(H[:, a:b])
             return op(q, act(o, w) if q == "s" else cpy(o, w), h16, tF)
-        e1 = eq(128, 192, 0)
-        e0 = eq(0, 128, 1)
-        o = 17 * (8 - t)
-        pm = MM([hh, tP], (T.pM[:, 0:204], T.NEG[:, :], T.C16[:, :], True, False),
-                *(to_seekers(T.pM, T.Et, T.RS, o, False) + to_seekers(T.pM, T.Hh, T.IJ, 0, True)))
-        sM = S(act(T.M[:, :], T.pM[:, 0:204], AF.Sign), pm)
+        e1 = eq(128, 192)
         if t == 0:
-            sH = S(act(T.hib[:, :], T.RJ[:, :]))
+            v = V(tt(T.S0[:, :], T.pE[:, 0:192], T.DM[:, :], A.mult), pS)
+            w = V(ts(T.OT[:, :], T.OT[:, :], 511, A.bitwise_and), tOT)
+            v = V(scan(T.S1[:, :], T.SM[:, :], T.S0[:, :], A.mult, A.add), v)
+            tAT = V(cpy(T.AT[:, :], T.OT[:, :]), w)
+            vSN = V(ts(T.SN[:, 0:12], T.S1[:, 15::16], 2048.0, A.add), v)
+            vZ = V(cpy(T.Z[:, :].indirect(T.SN[:, 0:12]), T.ZV[:, :]), sZV, vSN, gZ, sZ)
+            for u in range(1, RO):
+                tSN = turn("y", lambda a, b: T.SN[a:b, 12 * u:12 * u + 12], lambda a, b: T.SN[a:b, 0:12], u, "dSN", vSN)
+        e0 = eq(0, 128)
+        o = 17 * (8 - t)
+        if t:
+            sM = may(t, hh)
         f1 = fg("s", 128, 192)
         MM([sM], (T.pA[:, 0:204], T.IM[:, :], T.M[:, :], True, False),
            *(to_seekers(T.pA, T.Hh, T.IJ, 0, False) + to_seekers(T.pA, T.E, T.R0, o, False)))
-        if t == 0:
-            m = MM([sH], (T.pW[:, 0:192], T.SH1[:, :], T.RJ[:, :], True, False), (T.pW[:, 0:192], T.SH2[:, :], T.hib[:, :], False, True))
-            pS = MM([], (T.pE[:, 0:192], rep(0), T.E[:, :], True, True))
         MM([e1], *trunks(T.pA, T.EQ, T.SelE, 1, False))
         if t < RO - 1:
             pg = MM([], (T.pG[:, 0:192], rep(t), T.E[:, :], True, False), (T.pG[:, 0:192], T.IN[:, :], T.Hh[:, :], False, True))
         if t == 0:
-            sZV = S(act(T.ZV[:, :], T.pW[:, 0:192]), m)
-            v = V(tt(T.S0[:, :], T.pE[:, 0:192], T.DM[:, :], A.mult), pS)
+            MM([vZ], *(count_none(T.N0, True, False) + [(T.pD[0:32, 0:128], T.Y32[:, 31 - a:63 - a], T.Z[:, 128 * a:128 * a + 128],
+                                                         False, False) for a in range(32)]))
             hf = V(cpy(T.Hf[:, :], T.PI[:, 0:192]))
-            v = V(scan(T.S1[:, :], T.SM[:, :], T.S0[:, :], A.mult, A.add), v)
-            vSN = V(ts(T.SN[:, 0:12], T.S1[:, 15::16], 2048.0, A.add), v)
-            vZ = V(cpy(T.Z[:, :].indirect(T.SN[:, 0:12]), T.ZV[:, :]), sZV, vSN, sZ)
-            for u in range(1, RO):
-                tSN = turn(lambda a, b: T.SN[a:b, 12 * u:12 * u + 12], lambda a, b: T.SN[a:b, 0:12], u, "dSN", vSN)
+            vTk = V(cpy(T.Tk[:, :], T.TI[:, 0:512]), tTI)
         MM([f1], *trunks(T.pX, T.FG, T.SelF, 1, True))
         nv = NV if t else NV0
         f0 = fg("s", nv, 128)
-        if t:
-            fs = V(cpy(T.FS[:, :], T.F[:, :].indirect(T.SN[:, 12 * t:12 * t + 12])), tSN, tF)
+        if 0 < t < RO - 1:
             MM([vD], (T.pD[0:32, 0:128], T.Ib[0:32, 0:32], T.D[:, :], True, False))
+        elif t:
+            MM([vD], (T.pD[:, 0:32], T.D[:, :], T.Ib[0:32, 0:32], True, False))
         pa = MM([e0], *trunks(T.pA, T.EQ, T.SelE, 0, False))
-        mine = (T.FS[:, 0:128], T.FS[:, 128:192]) if t else (T.NEG[:, 0:128], T.NEG[:, 0:64])
-        MM([fs if t else None], *(slots(T.pX, mine, T.SelF, 0, 0, True) + slots(T.pX, mine, T.SelF, 0, 1, True)))
         fv = fg("v", 0, nv) if nv else None
-        px = MM([f0, fv], *trunks(T.pX, T.FG, T.SelF, 0, True))
-        if t == 0:
-            MM([vZ], *(count_none(T.N0, True, False) + [(T.pD[0:32, 0:128], T.Y32[:, 31 - a:63 - a], T.Z[:, 128 * a:128 * a + 128],
-                                                         False, False) for a in range(32)]))
-        v = V(scan(T.AS[:, :], T.INC[:, :], T.pA[:, 0:204], A.add, A.max), pa)
-        v = V(ts(T.BI[:, :], T.AS[:, 16::17], 32.0 * 2047, A.add), v)
+        fs = V(cpy(T.FS[:, :], T.F[:, :].indirect(T.SN[:, 12 * t:12 * t + 12])), tSN, tF) if t else None
+        mine = (T.FS[:, 0:128], T.FS[:, 128:192]) if t else (T.NEG[:, 0:128], T.NEG[:, 0:64])
+        MM([f0, fv], *trunks(T.pX, T.FG, T.SelF, 0, True))
+        px = MM([fs], *(slots(T.pX, mine, T.SelF, 0, 0, True) + slots(T.pX, mine, T.SelF, 0, 1, True)))
+        vA = V(scan(T.AS[:, :], T.INC[:, :], T.pA[:, 0:204], A.add, A.max), pa)
+        v = V(ts(T.BI[:, :], T.AS[:, 16::17], 32.0 * 2047, A.add), vA)
         v = V(ts(T.UI[:, 12:24], T.BI[:, :], 12, A.arith_shift_right, 31, A.bitwise_and), v)
         w = V(ts(T.UI[:, 0:12], T.BI[:, :], 5, A.arith_shift_right, 127, A.bitwise_and))
-        vP = V(ts(T.UI[:, 24:36], T.BI[:, :], 31, A.bitwise_and))
         va = V(cpy(T.UF[:, 12:24], T.UI[:, 12:24]), v)
-        vb = V(ts(T.UF[:, 0:12], T.UI[:, 0:12], 1008.0, A.add), w)
+        vX = V(scan(T.XS[:, :], T.INC[:, :], T.pX[:, 0:204], A.add, A.max), px)
+        vb = V(ts(T.UF[:, 0:12], T.UI[:, 0:12], 2.0 ** 23 - 16, A.add), w)
         if t < RO - 1:
             sG = S(act(T.Dg[:, :], T.pG[:, 0:192]), pg)
         sA = []
@@ -358,7 +380,6 @@ def rank_program(g, core, T, topo):
             for c in range(6 * h, 6 * h + 6):
                 s = S(act(T.TA[:, 32 * c:32 * c + 32], T.iotA[:, :], AF.Abs, bias=T.UF[:, 12 + c:13 + c], scale=-1.0), va)
             sA += [S(act(T.OA[:, 192 * h:192 * h + 192], T.TA[:, 192 * h:192 * h + 192], AF.Relu, bias=8192.0, scale=-8192.0), s)] * 6
-        vX = V(scan(T.XS[:, :], T.INC[:, :], T.pX[:, 0:204], A.add, A.max), px)
         ob = []
 
         def kills(n):
@@ -366,58 +387,62 @@ def rank_program(g, core, T, topo):
                 ob.append(V(ts(T.OB[:, 128 * c:128 * c + 128], T.iotB[:, :], T.XS[:, 17 * c + 16:17 * c + 17], A.subtract,
                                T.UF[:, c:c + 1], A.is_equal), vX, vb))
         if t == RO - 1:
-            kills(8)
-        v = V(tt(T.FI[:, :], T.XS[:, 16::17], T.UI[:, 24:36], A.max), vP, vX)
+            kills(10)
+        v = V(tt(T.FI[:, :], T.XS[:, 16::17], T.AS[:, 16::17], A.max), vX)
         kills(2)
         v5 = V(ts(T.F5[:, :], T.FI[:, :], 31, A.bitwise_and), v)
-        kills(2)
+        if t < RO - 1:
+            kills(K1)
         if t == RO - 1:
-            xW = send(lambda n: T.F5[:, :], T.FIN[:, 12 * me:12 * me + 12], "arrW", v5)
-        else:
-            v = V(tt(T.Wt[:, 0:192], T.F5[:, :].indirect(T.LC[:, :]), T.C15[:, 0:192], A.is_equal), v5)
-            kills(8)
+            for c in range(12):
+                pd = MM([ob[c], sA[c]], (T.pD[:, 0:32], T.OB[:, 128 * c:128 * c + 128], T.OA[:, 32 * c:32 * c + 32], False, c == 11))
+            break
+        v = V(tt(T.Wt[:, 0:192], T.F5[:, :].indirect(T.LC[:, :]), T.C15[:, 0:192], A.is_equal), v5)
+        kills(8 - K1)
         for c in range(12):
+            if c == 10:
+                vW = V(tt(T.WD[:, :], T.pW[:, 0:192], T.Dg[:, :], A.mult), m, sG)
+                kills(2)
             pd = MM([ob[c], sA[c]], (T.pD[0:32, 0:128], T.OA[:, 32 * c:32 * c + 32], T.OB[:, 128 * c:128 * c + 128], False, c == 11))
-            if c == 3 and t < RO - 1:
+            if c == K1 + 1:
                 m = MM([v], (T.pW[:, 0:128], T.Wt[:, 0:128], T.Ib[:, :], True, True),
                        (T.pW[0:64, 128:192], T.Wt[:, 128:192], T.Ib[:, 0:64], True, True),
                        (T.pW[64:128, 128:192], T.Wt[:, 128:192], T.Ib[:, 64:128], True, True))
         vD = S(act(T.D[:, :], T.pD[0:32, 0:128], AF.Sign, bias=(0.0 if t else -15.5)), pd, tF)
-        if t == RO - 1:
-            break
-        tF = flags_to_F(vD)
-        if t == 0:
-            vTk = V(cpy(T.Tk[:, :], T.TI[:, 0:512]), tTI)
-        if t < 3:
+        tF = flags_to_F("ys", vD)
+        if t < 2:
             ms = [(T.pZ[:, :], T.Ih[:, :], T.P2h[:, :], True, False)] + [
                 (T.pZ[:, :], T.YS[:, 112 - 16 * q:240 - 16 * q], T.Z[:, 512 * q:512 * q + 512], False, q == 7) for q in range(8)]
-            pz = MM([], *ms[3 * t:3 * t + 3])
-        if t == 2:
+            pz = MM([], *ms[5 * t:5 * t + 5])
+        if t == 1:
             sV = S(act(T.VAL[:, :], T.pZ[:, :], AF.Identity, bias=2048.0), pz)
             xV = exchange("VAL", "stV", "landV", "dV", "arrV", sV)
-        v = V(tt(T.WD[:, :], T.pW[:, 0:192], T.Dg[:, :], A.mult), m, sG)
         if t == 1:
             w = V(ts(T.COf[:, :], T.AO[:, 12:24], -2048.0, A.add), xA)
-        vTk = V(lambda e: e.tensor_tensor(T.Tk[:, :].indirect(at), T.Hf[:, :], T.WD[:, :], A.add), v, vTk, hf)
+        vTk = V(lambda e: e.tensor_tensor(T.Tk[:, :].indirect(at), T.Hf[:, :], T.WD[:, :], A.add), vW, vTk, hf)
         if t == 1:
             w = V(tt(T.EO[:, :], T.COf[:, :].indirect(LB), T.EM[:, :], A.mult), w)
             pO = MM([w], (T.pE[:, 0:192], rep(0), T.EO[:, :], True, True))
-    dma("s", T.stD[:], T.D[:, :], "dD", vD)
-    tD = dma("s", T.landD[me], T.D[4 * me:4 * me + 4, :], "dD", vD)
-    xD = send(lambda n: T.stD[n], T.landD[me], "arrD", tD)
-    tKD = dma("s", T.KD[:, :], T.landD[:], "dKD", xD, tD)
-    vW = V(cpy(T.FIN[:, 12 * me:12 * me + 12], T.F5[:, :]), v5)
+    V(cpy(T.LO[:, 4::8], T.F5[:, 0:8]), v5)
+    V(cpy(T.LO[:, 5:32:8], T.F5[:, 8:12]))
+    v = V(cpy(T.LO[:, 37::8], T.F5[:, 8:12]))
+    for u in range(4):
+        s = S(act(T.LO[:, u::8], T.pD[:, u:32:4], AF.Sign), pd)
+    xW = send(lambda n: T.LO[:, 8 * n:8 * n + 8], T.LN[:, 8 * me:8 * me + 8], "arrW", v, s)
+    vW = V(cpy(T.LN[:, 8 * me:8 * me + 8], T.LO[:, 8 * me:8 * me + 8]), v, s)
     v = V(cpy(T.TkO[:, :], T.YI[:, :]), tYI)
     v = V(ts(T.HO2[:, :], T.TkO[:, :].indirect(T.AO[:, 0:12]), -2048.0, A.add), v)
     V(cpy(T.HO[:, :], T.TkO[:, :].indirect(T.AO[:, 0:12])))
     vG = V(tt(T.DgO[:, :], T.pE[:, 0:192], T.HO2[:, :], A.subtract), v, pO)
-    v = V(tt(T.Wt[:, :], T.FIN[:, :].indirect(T.LH[:, :]), T.C15[:, :], A.is_equal), xW, vW)
+    v = V(tt(T.Wt[:, :], T.LN[:, :].indirect(T.LH[:, :]), T.C15[:, :], A.is_equal), xW, vW)
+    m = MM([xW, vW], *[(T.pM[0:8, 128 * u:128 * u + 128], T.LN[:, u::8], T.Ib[:, :], True, True) for u in range(4)])
+    s = S(act(T.KD[:, :], T.pM[0:8, :]), m)
     h = 64 * (me // 4)
     m = MM([v], (T.pW[:, 0:128], T.Wt[:, 0:128], T.Ib[:, :], True, True), (T.pW[:, 128:192], T.Wt[:, 128:256], T.Ib[:, h:h + 64], True, True))
     v = V(tt(T.WD[:, :], T.pW[:, 0:192], T.DgO[:, :], A.mult), m, vG)
     v = V(lambda e: e.tensor_tensor(T.TkO[:, :].indirect(T.AO[:, 0:12]), T.HO[:, :], T.WD[:, :], A.add), v)
     dma("y", T.yt[:], T.TkO[:, :], "oY", v)
-    m = MM([tKD, sV], (T.pZ[:, :], T.R8b[:, :], T.KD[:, :], True, True))
+    m = MM([s, sV], (T.pZ[:, :], T.R8b[:, :], T.KD[:, :], True, True))
     v = V(tt(T.YP[:, :], T.pZ[:, :], T.VR[:, :], A.max), m, tVR)
     dma("s", T.yp[:], T.YP[:, :], "oP", v)
     need("g", [(s, n) for s, n in cnt.items() if n])

from concourse.bass import DstId, RemoteDMATransfer
from concourse.mybir import AluOpType, ActivationFunctionType

RO = 5
NV = 16
NV0 = 0
RV = 5
K1 = 2
F32, BF, FH, I32, U16 = "float32", "bfloat16", "float16", "int32", "uint16"
SCRATCH = {}


def _b(where, dtype, **kw):
    for k, s in kw.items():
        SCRATCH[k] = (where, s, dtype)


_b("dram", I32, stR=[8, 128, 32], landR=[8, 128, 32])
_b("dram", U16, stP=[8, 128, 24], landP=[8, 128, 24], stT=[8, 128, 64], landT=[8, 128, 64], stY=[8, 128, 64], landY=[8, 128, 64])
_b("dram", F32, stV=[8, 128, 64], landV=[8, 128, 64])
_b("sbuf", I32, P2=[128, 512], ii=[128, 192], c12=[128, 12], cp=[128, 1], ci=[128, 4], iia=[128, 192], t12b=[128, 24],
   R=[128, 192], Cl=[128, 12], OH=[128, 36], OT=[128, 60], TkH=[128, 512], BI=[128, 12], UI=[128, 24], FI=[128, 12], F5=[128, 12])
_b("sbuf", BF, col=[128, 256], cola=[128, 192], cq8=[128, 256], seg=[128, 272], slot=[128, 272])
_b("sbuf", U16, LI=[128, 24], LC=[128, 12], LH=[128, 16], AT=[128, 60], SN=[128, 60], H16=[128, 192], PO=[128, 192],
   PI=[128, 192], TO=[128, 512], TI=[128, 512], YO=[128, 512], YI=[128, 512], A0=[128, 12], AH=[128, 24], AO=[128, 24])
_b("sbuf", F32, P=[128, 4096], KC=[128, 24], EM=[128, 192], HO2=[128, 192],
   DM=[128, 192], SM=[128, 192], C15=[128, 256], INC=[128, 204], SH1=[128, 128], Clf=[128, 12],
   RJ=[128, 192], RR0=[128, 3072], RR1=[128, 3072], RR2=[128, 3072], RR3=[128, 3072], RR4=[128, 3072], Tk=[128, 512],
   Hf=[128, 192], Dg=[128, 192], WD=[128, 192], AS=[128, 204], XS=[128, 204], UF=[128, 24], S0=[128, 192], S1=[128, 192],
   VAL=[128, 512], VR=[128, 512], YP=[128, 512], COf=[128, 12], TkO=[128, 512], HO=[128, 192], DgO=[128, 192])
_b("sbuf", FH, P2h=[128, 512], GY=[128, 1024], Ih=[128, 128], IN=[128, 128], IJ=[128, 136], REPf=[128, 256], R0=[128, 272],
   E=[128, 192], EO=[128, 192], Hh=[128, 192])
_b("sbuf", BF, iotA=[128, 32], iotB=[128, 128], SelF=[128, 8], SelE=[128, 8], Ib=[128, 128], IM=[128, 128], RS=[128, 272],
   NEG=[128, 128], C16=[128, 204], C4=[128, 36], SH2=[128, 128], YS=[128, 240], R8b=[8, 128], Et=[128, 192], N0=[128, 512],
   Y32=[128, 64], hib=[128, 192], ZV=[128, 192], F=[128, 4096], Z=[128, 4096], EQ=[128, 3072], FG=[128, 3072], FS=[128, 192],
   M=[128, 204], Wt=[128, 256], TA=[128, 384], OA=[128, 384], OB=[128, 1536], D=[32, 128], KD=[8, 512],
   LO=[128, 64], LN=[128, 64])
_BANKS = ["pA", "pX", "pM", "pG", "pW", "pD", "pZ", "pE"]
_b("psum", F32, **{k: [128, 512] for k in _BANKS})

_ARR = ["arrR", "arrP", "arrT", "arrA", "arrV", "arrY", "arrW"]
_DMA = ["dR", "dRl", "dCl", "dH", "dO", "dP2", "dP", "dT", "dF", "dPI", "dTI", "dAT", "dRR0", "dRR1", "dRR2", "dRR3", "dSN", "dV", "dVR", "dY", "dYI",
        "oY", "oP"]
SEMAPHORES = ["cv", "cs", "cpe", "cg", "sent"] + _ARR + _DMA


def rank_program(g, core, T, topo):
    me = T.rank_of(core)
    if me is None:
        return
    A, AF = AluOpType, ActivationFunctionType
    eng = {"v": g.vector, "s": g.scalar, "p": g.tensor, "g": g, "y": g.sync}
    own = {"v": "cv", "s": "cs", "p": "cpe", "g": "cg"}
    cnt = {s: 0 for s in SEMAPHORES}
    seen = {q: {} for q in eng}

    def need(q, deps):
        best = {}
        for d in deps:
            if d is not None:
                best[d[0]] = max(best.get(d[0], 0), d[1])
        for s, n in best.items():
            if seen[q].get(s, 0) < n:
                eng[q].wait_ge(T.sem[s], n)
                seen[q][s] = n

    def op(q, f, *deps):
        need(q, deps)
        s = own[q]
        f(eng[q]).then_inc(T.sem[s], 1)
        cnt[s] += 1
        return (s, cnt[s])

    def V(f, *deps):
        return op("v", f, *deps)

    def S(f, *deps):
        return op("s", f, *deps)

    def MM(deps, *ms):
        need("p", deps)
        for n, m in enumerate(ms):
            i = eng["p"].matmul(m[0], m[1], m[2], start=m[3], stop=m[4])
            if n == len(ms) - 1:
                i.then_inc(T.sem["cpe"], 1)
        cnt["cpe"] += 1
        return ("cpe", cnt["cpe"])

    def dma(q, out, in_, sem, *deps):
        need(q, deps)
        eng[q].dma_start(out, in_).then_inc(T.sem[sem], 16)
        cnt[sem] += 16
        return (sem, cnt[sem])

    def ts(out, in0, s1, op0, s2=None, op1=None):
        if op1 is None:
            return lambda e: e.tensor_scalar(out, in0, s1, None, op0)
        return lambda e: e.tensor_scalar(out, in0, s1, s2, op0, op1)

    def tt(out, a, b, o):
        return lambda e: e.tensor_tensor(out, a, b, o)

    def cpy(out, in_):
        return lambda e: e.tensor_copy(out, in_)

    def act(out, in_, f=AF.Copy, **kw):
        return lambda e: e.activation(out, in_, f, **kw)

    def scan(out, d0, d1, o0, o1):
        return lambda e: e.tensor_tensor_scan(out, d0, d1, 0.0, o0, o1)

    def fill(out, x):
        return lambda e: e.memset(out, x)

    def send(src, dst, sem, *deps, to=None, each=2):
        need("g", deps)
        order = sorted(to or [(me + k) % 8 for k in range(1, 8)], key=lambda n: len(topo.engines(core, T.cores[n])))
        used, tr = [], []
        for n in order:
            c = T.cores[n]
            es = [e for e in topo.engines(core, c) if e not in used][:each]
            used += es
            a = topo.addr(c)
            tr.append(RemoteDMATransfer(dst_ids=[DstId(rid=a[0], pnc=a[1])], dma_engine_mask=sum(1 << e for e in es),
                                        remote_sem=T.sem[sem], srcs=[src(n)], dsts=[dst], alu_op=0))
        g.remote_dma_fused(tr, local_sem=T.sem["sent"])
        cnt["sent"] += len(used)
        cnt[sem] += len(used)
        return (sem, cnt[sem])

    lo, hi = 16 * me, 16 * me + 16

    def exchange(buf, st, land, sem, arr, *deps):
        dma("y", T[st][:], T[buf][:, :], sem, *deps)
        t = dma("y", T[land][me], T[buf][lo:hi, :], sem)
        return [t, send(lambda n: T[st][n], T[land][me], arr, t)]

    dma("y", T.stR[:, 0:96, :], T.routes[:], "dR")
    dma("s", T.stR[:, 96:102, :], T.calls[:], "dR")
    dma("s", T.stR[:, 102:128, :], T.trunk[0:13, :], "dR")
    dma("y", T.landR[me, 0:96, :], T.routes[lo:hi, :], "dR")
    tR = dma("s", T.landR[me, 96:102, :], T.calls[lo:hi, :], "dR")
    dma("y", T.TkH[:, :], T.trunk[:], "dH")
    tH = dma("s", T.OH[:, 24:36], T.routes[0::16, :], "dH")
    for q in range(8):
        tP2 = dma("ys"[q % 2], T.P2[16 * q:16 * q + 16, :], T.paths[lo:hi, 512 * q:512 * q + 512], "dP2")
    dma("y", T.OH[:, 0:12], T.routes[RO - 1::16, :], "dO")
    tO = dma("s", T.OH[:, 12:24], T.calls[:], "dO")
    def iota(out, pattern, base=0):
        return op("g", lambda e: e.iota(out, pattern, base, 0, allow_small_or_imprecise_dtypes=True))
    g1 = op("g", lambda e: e.iota(T.cp[:, 0:1], [[0, 1]], 0, 1))
    op("g", lambda e: e.iota(T.c12[:, :], [[1, 12]], 0, 0))
    g2 = iota(T.cola[:, :], [[0, 12], [1, 16]])
    g3 = iota(T.col[:, :], [[1, 256]])
    xR = [tR, send(lambda n: T.stR[n], T.landR[me], "arrR", tR)]
    op("g", lambda e: e.iota(T.ii[:, :], [[1, 12], [12, 16]], 0, 0))
    g4 = iota(T.cq8[:, :], [[0, 2], [1, 8], [0, 16]])
    iota(T.seg[:, :], [[0, 2], [1, 8], [0, 17]])
    g5 = iota(T.slot[:, :], [[0, 2], [1, 8], [8, 17]])
    KC, col, ci = T.KC, T.col, T.ci

    def kc(n):
        return KC[:, n:n + 1]
    v = V(fill(T.F[:, 0:512], 0.0))
    for y in range(1, 8):
        sF = S(act(T.F[:, 512 * y:512 * y + 512], T.F[:, 0:512]), v)
    V(ts(ci[:, 0:1], T.cp[:, 0:1], 15, A.bitwise_and), g1)
    V(ts(ci[:, 1:2], T.cp[:, 0:1], 4, A.arith_shift_right))
    v = V(cpy(kc(0), T.cp[:, 0:1]))
    V(cpy(KC[:, 1:3], ci[:, 0:2]), v)
    V(ts(kc(4), ci[:, 0:1], 12.0, A.mult))
    v = V(ts(kc(3), ci[:, 1:2], 4.0, A.mult, 3.0, A.add))
    V(ts(T.t12b[:, 0:12], T.c12[:, :], kc(4), A.add), v, g2)
    v = V(ts(KC[:, 16:24], T.c12[:, 0:8], kc(2), A.is_equal))
    V(ts(T.t12b[:, 12:24], T.t12b[:, 0:12], 4, A.arith_shift_right), v)
    for y in range(8):
        v = V(ts(T.GY[:, 128 * y:128 * y + 128], T.cola[:, 0:128], kc(1), A.is_equal, kc(16 + y), A.mult))
    V(cpy(T.LI[:, :], T.t12b[:, :]), v)
    V(ts(T.C4[:, :], col[:, 0:36], kc(3), A.is_equal), g3)
    V(ts(kc(6), ci[:, 0:1], 0.0, A.is_equal, 2.0 ** 23, A.mult))
    V(ts(kc(7), ci[:, 0:1], 5.0, A.is_lt))
    V(ts(kc(8), ci[:, 0:1], 5.0, A.is_ge, -5.0, A.mult))
    V(ts(kc(9), T.cp[:, 0:1], 5.0, A.add))
    V(ts(kc(14), T.cp[:, 0:1], 0.0, A.is_equal, 16.0, A.mult))
    V(ts(kc(15), T.cp[:, 0:1], 1.0, A.is_equal, float(3 * 2 ** 24), A.mult))
    V(ts(kc(13), ci[:, 0:1], 0.0, A.is_equal))
    V(ts(kc(11), T.cp[:, 0:1], kc(2), A.add, 1.0, A.add))
    LI, LB = T.LI[:, 0:12], T.LI[:, 12:24]
    v = V(ts(T.A0[:, :], T.OH[:, 24:36], -512.0 * me, A.add), tH)
    vPO = V(cpy(T.PO[:, :], T.TkH[:, :].indirect(T.A0[:, :])), v)
    xP = exchange("PO", "stP", "landP", "dP", "arrP", vPO)
    iota(T.C15[:, :], [[0, 16], [-1, 16]], 15)
    iota(T.iotA[:, :], [[-1, 32]], 31)
    iota(T.iotB[:, :], [[-1, 128]], 127)
    vPh = V(ts(T.P2h[:, :], T.P2[:, :], -2048.0, A.add), tP2)
    vN0 = V(ts(T.N0[:, :], T.P2h[:, :], 2048.0, A.is_ge), vPh)

    def count_none(n, first, last):
        return [(T.pD[0:32, 0:128], T.C4[:, 3 - u:35 - u], n[:, 128 * u:128 * u + 128], first and u == 0, last and u == 3)
                for u in range(4)]
    for y in range(8):
        m = MM([vPh, vD if y > 1 else None], (T[_BANKS[y]][:, :], T.GY[:, 128 * y:128 * y + 128], T.P2h[:, :], True, True))
        tP = S(act(T.P[:, 512 * y:512 * y + 512], T[_BANKS[y]][:, :], AF.Identity, bias=-2048.0), m)
        if y == 1:
            vD = S(act(T.D[:, :], T.pD[0:32, 0:128], AF.Sign, bias=-15.5), MM([vN0], *count_none(T.N0, True, True)))
    xT = exchange("TO", "stT", "landT", "dT", "arrT", V(cpy(T.TO[:, :], T.TkH[:, :])))
    V(ts(T.AH[:, 0:12], T.OH[:, 0:12], -512.0 * ((me + RO - 1) % 8), A.add), tO)
    v = V(cpy(T.AH[:, 12:24], T.OH[:, 12:24]))
    xA = send(lambda n: T.AH[:, :], T.AO[:, :], "arrA", v, to=[(me + RO - 1) % 8], each=8)
    gZ = iota(T.Z[:, 0:1024], [[0, 1024]])
    sZ = S(act(T.Z[:, 1024:2048], T.P[:, 0:1024], scale=0.0), tP)
    tRl = dma("y", T.R[:, :], T.landR[:, 0:96, :], "dRl", *xR)
    tCl = dma("y", T.Cl[:, :], T.landR[:, 96:102, :], "dCl")

    def flags_to_F(queues, *tok):
        for q in range(8):
            t = dma(queues[q % len(queues)], T.F[16 * q:16 * q + 1, :], T.D[:, :], "dF", *tok)
        return t
    tF = flags_to_F("y", vD, sF)
    V(ts(T.iia[:, :], T.ii[:, :], 15, A.bitwise_and), g4)
    V(tt(kc(10), kc(14), kc(15), A.add))
    v = V(ts(kc(12), ci[:, 0:1], kc(8), A.add, 112.0, A.add))
    V(ts(T.REPf[:, :], T.cq8[:, :], kc(2), A.is_equal))
    V(ts(T.EM[:, :], T.iia[:, :], kc(1), A.is_equal), v)
    V(ts(T.DM[:, :], T.cola[:, :], kc(1), A.is_equal))
    V(cpy(T.LC[:, :], T.c12[:, :]))
    V(ts(T.LH[:, 0:8], T.c12[:, 0:8], 8.0, A.mult, 4.0, A.add))
    V(ts(T.LH[:, 8:16], T.c12[:, 0:8], 8.0, A.mult, 5.0, A.add))
    V(fill(T.LO[:, :], 0.0))
    V(ts(T.SH1[:, :], col[:, 0:128], kc(9), A.is_equal, kc(7), A.mult))
    V(ts(T.S0[:, 0:128], col[:, 0:128], kc(0), A.is_equal, kc(7), A.mult))
    v = V(ts(T.SM[:, :], T.cola[:, :], 0.0, A.not_equal))
    V(tt(T.SH2[:, :], T.S0[:, 0:128], T.SH1[:, :], A.subtract), v)
    V(ts(T.YS[:, :], col[:, 0:240], kc(12), A.is_equal))
    V(ts(T.Ih[:, :], col[:, 0:128], kc(0), A.is_equal))
    V(ts(T.IN[:, :], col[:, 0:128], kc(0), A.is_equal, -1.0, A.mult))
    V(ts(T.IJ[:, :], col[:, 0:136], kc(11), A.is_equal, -32.0, A.mult))
    V(ts(T.Ib[:, :], col[:, 0:128], kc(0), A.is_equal))
    V(ts(T.IM[:, :], col[:, 0:128], kc(0), A.is_equal, float(2 ** 22), A.mult))
    V(ts(T.SelF[:, :], col[:, 0:8], kc(2), A.is_equal, kc(6), A.mult))
    V(ts(T.SelE[:, :], col[:, 0:8], kc(2), A.is_equal, float(2 ** 17), A.mult))
    V(fill(T.NEG[:, :], -1.0))
    V(ts(T.C16[:, :], T.slot[:, 0:204], 8.0, A.is_ge, kc(10), A.mult), g5)
    V(fill(T.INC[:, :], 1.0))
    v = V(ts(T.RS[:, :], T.seg[:, :], kc(2), A.is_equal, 16384.0, A.mult))
    V(ts(T.R0[:, :], T.slot[:, :], kc(2), A.is_equal, -32.0, A.mult))
    V(fill(T.RS[:, 0::17], 0.0), v)
    V(fill(T.INC[:, 0::17], -float(2 ** 25)))
    V(ts(T.R8b[:, :], T.cq8[0:8, 0:128], KC[0:8, 0:1], A.is_equal, 4096.0, A.mult))
    V(ts(T.Y32[:, :], col[:, 0:64], 31.0, A.is_equal, kc(13), A.mult))
    vC = V(fill(T.Z[:, 2048:4096], 0.0))

    tPI = dma("y", T.PI[:, :], T.landP[:], "dPI", *xP)
    for t in range(RO):
        tOT = dma("y", T.OT[16 * t:128, 12 * t:12 * t + 12], T.landR[0:8 - t, 6 * t:6 * t + 6, :], "dAT")
        if t:
            tOT = dma("y", T.OT[0:16 * t, 12 * t:12 * t + 12], T.landR[8 - t:8, 6 * t:6 * t + 6, :], "dAT")
    tTI = dma("y", T.TI[:, :], T.landT[:], "dTI", *xT)

    def turn(q, dst, src, u, sem, *deps):
        dma(q, dst(16 * u, 128), src(0, 128 - 16 * u), sem, *deps)
        return dma(q, dst(0, 16 * u), src(128 - 16 * u, 128), sem)

    def rep(t):
        return T.REPf[:, 16 * (8 - t):16 * (16 - t)]
    RR = [T["RR%d" % t] for t in range(RO)]
    vRJ = V(ts(T.RJ[:, :], T.R[:, :].indirect(LI), -4096.0, A.add), tRl, vC)
    v = V(ts(T.Clf[:, :], T.Cl[:, :], -2048.0, A.add), tCl)
    v = V(tt(T.E[:, :], T.Clf[:, :].indirect(LB), T.EM[:, :], A.mult), v)
    for p in range(16):
        if p < RV:
            a = V(cpy(T.RR0[:, 2048 + p::16], T.RJ[:, 128:192]), vRJ)
        else:
            b = S(act(T.RR0[:, 2048 + p::16], T.RJ[:, 128:192]), vRJ)
    sH = S(act(T.hib[:, :], T.RJ[:, :]), vRJ)
    m = MM([sH, tP], (T.pW[:, 0:192], T.SH1[:, :], T.RJ[:, :], True, False), (T.pW[:, 0:192], T.SH2[:, :], T.hib[:, :], False, True))
    pS = MM([v], (T.pE[:, 0:192], rep(0), T.E[:, :], True, True))
    V(ts(T.Et[:, :], T.E[:, :], 1.0 / 512, A.mult, 192.0 - 255.5 / 512, A.add), v)
    hh = V(ts(T.Hh[:, :], T.PI[:, :], -2048.0, A.add), tPI)

    def to_seekers(out, l, w, o, last):
        return [(out[0:64, 136:204], l[:, 128:192], w[:, o:o + 68], False, False),
                (out[64:128, 136:204], l[:, 128:192], w[:, o + 68:o + 136], False, False),
                (out[:, 0:136], l[:, 0:128], w[:, o:o + 136], False, last)]

    def slots(out, tab, sel, s, part, alone, last=False):
        if part == 0:
            return [(out[:, s:136:17], tab[0], sel[:, 0:8], alone, alone or last)]
        return [(out[0:64, 136 + s:204:17], tab[1], sel[:, 0:4], alone, alone),
                (out[64:128, 136 + s:204:17], tab[1], sel[:, 4:8], alone, alone)]

    def trunks(out, tab, sel, part, alone):
        return [m for p in range(16) for m in slots(out, (tab[:, p:2048:16], tab[:, 2048 + p:3072:16]), sel, 1 + p, part, alone, p == 15)]

    def may(t, hh):
        pm = MM([hh, tP], (T.pM[:, 0:204], T.NEG[:, :], T.C16[:, :], True, False),
                *(to_seekers(T.pM, T.Et, T.RS, 17 * (8 - t), False) + to_seekers(T.pM, T.Hh, T.IJ, 0, True)))
        return S(act(T.M[:, :], T.pM[:, 0:204], AF.Sign), pm)
    for p in range(16):
        c = S(act(T.RR0[:, p:2048:16], T.RJ[:, 0:128]))
        if p == 5:
            sZV = S(act(T.ZV[:, :], T.pW[:, 0:192]), m)
        if p == 9:
            sM = may(0, hh)
    rr = [[a, b, c]] + [None] * 4

    for t in range(RO):
        at = T.AT[:, 12 * t:12 * t + 12]
        if t == 0:
            H, h16 = T.PI, tPI
        else:
            H = T.H16
            h16 = V(cpy(T.H16[:, :], T.Tk[:, :].indirect(at)), vTk, tAT)
            hf = S(act(T.Hf[:, :], T.Tk[:, :].indirect(at)), vTk, tAT)
            hh = V(ts(T.Hh[:, :], T.H16[:, :], -2048.0, A.add), h16)
        if t == RO - 1:
            xY = exchange("YO", "stY", "landY", "dY", "arrY", V(cpy(T.YO[:, :], T.Tk[:, :])))
            tVR = dma("y", T.VR[:, :], T.landV[:], "dVR", *xV)
            tYI = dma("y", T.YI[:, :], T.landY[:], "dYI", *xY)
        else:
            x = turn("y", lambda a, b: RR[t + 1][a:b, :], lambda a, b: T.RR0[a:b, :], t + 1, "dRR%d" % t, tF, tTI, *rr[0])
            rr[t + 1] = [x]

        def eq(a, b):
            return V(tt(T.EQ[:, 16 * a:16 * b], T.P[:, :].indirect(H[:, a:b]), RR[t][:, 16 * a:16 * b], A.is_equal), h16, tP,
                     *rr[t][0:2 if a else 3])

        def fg(q, a, b):
            o, w = T.FG[:, 16 * a:16 * b], T.F[:, :].indirect(H[:, a:b])
            return op(q, act(o, w) if q == "s" else cpy(o, w), h16, tF)
        e1 = eq(128, 192)
        if t == 0:
            v = V(tt(T.S0[:, :], T.pE[:, 0:192], T.DM[:, :], A.mult), pS)
            w = V(ts(T.OT[:, :], T.OT[:, :], 511, A.bitwise_and), tOT)
            v = V(scan(T.S1[:, :], T.SM[:, :], T.S0[:, :], A.mult, A.add), v)
            tAT = V(cpy(T.AT[:, :], T.OT[:, :]), w)
            vSN = V(ts(T.SN[:, 0:12], T.S1[:, 15::16], 2048.0, A.add), v)
            vZ = V(cpy(T.Z[:, :].indirect(T.SN[:, 0:12]), T.ZV[:, :]), sZV, vSN, gZ, sZ)
            for u in range(1, RO):
                tSN = turn("y", lambda a, b: T.SN[a:b, 12 * u:12 * u + 12], lambda a, b: T.SN[a:b, 0:12], u, "dSN", vSN)
        e0 = eq(0, 128)
        o = 17 * (8 - t)
        if t:
            sM = may(t, hh)
        f1 = fg("s", 128, 192)
        MM([sM], (T.pA[:, 0:204], T.IM[:, :], T.M[:, :], True, False),
           *(to_seekers(T.pA, T.Hh, T.IJ, 0, False) + to_seekers(T.pA, T.E, T.R0, o, False)))
        MM([e1], *trunks(T.pA, T.EQ, T.SelE, 1, False))
        if t < RO - 1:
            pg = MM([], (T.pG[:, 0:192], rep(t), T.E[:, :], True, False), (T.pG[:, 0:192], T.IN[:, :], T.Hh[:, :], False, True))
        if t == 0:
            MM([vZ], *(count_none(T.N0, True, False) + [(T.pD[0:32, 0:128], T.Y32[:, 31 - a:63 - a], T.Z[:, 128 * a:128 * a + 128],
                                                         False, False) for a in range(32)]))
            hf = V(cpy(T.Hf[:, :], T.PI[:, 0:192]))
            vTk = V(cpy(T.Tk[:, :], T.TI[:, 0:512]), tTI)
        MM([f1], *trunks(T.pX, T.FG, T.SelF, 1, True))
        nv = NV if t else NV0
        f0 = fg("s", nv, 128)
        if 0 < t < RO - 1:
            MM([vD], (T.pD[0:32, 0:128], T.Ib[0:32, 0:32], T.D[:, :], True, False))
        elif t:
            MM([vD], (T.pD[:, 0:32], T.D[:, :], T.Ib[0:32, 0:32], True, False))
        pa = MM([e0], *trunks(T.pA, T.EQ, T.SelE, 0, False))
        fv = fg("v", 0, nv) if nv else None
        fs = V(cpy(T.FS[:, :], T.F[:, :].indirect(T.SN[:, 12 * t:12 * t + 12])), tSN, tF) if t else None
        mine = (T.FS[:, 0:128], T.FS[:, 128:192]) if t else (T.NEG[:, 0:128], T.NEG[:, 0:64])
        MM([f0, fv], *trunks(T.pX, T.FG, T.SelF, 0, True))
        px = MM([fs], *(slots(T.pX, mine, T.SelF, 0, 0, True) + slots(T.pX, mine, T.SelF, 0, 1, True)))
        vA = V(scan(T.AS[:, :], T.INC[:, :], T.pA[:, 0:204], A.add, A.max), pa)
        v = V(ts(T.BI[:, :], T.AS[:, 16::17], 32.0 * 2047, A.add), vA)
        v = V(ts(T.UI[:, 12:24], T.BI[:, :], 12, A.arith_shift_right, 31, A.bitwise_and), v)
        w = V(ts(T.UI[:, 0:12], T.BI[:, :], 5, A.arith_shift_right, 127, A.bitwise_and))
        va = V(cpy(T.UF[:, 12:24], T.UI[:, 12:24]), v)
        vX = V(scan(T.XS[:, :], T.INC[:, :], T.pX[:, 0:204], A.add, A.max), px)
        vb = V(ts(T.UF[:, 0:12], T.UI[:, 0:12], 2.0 ** 23 - 16, A.add), w)
        if t < RO - 1:
            sG = S(act(T.Dg[:, :], T.pG[:, 0:192]), pg)
        sA = []
        for h in range(2):
            for c in range(6 * h, 6 * h + 6):
                s = S(act(T.TA[:, 32 * c:32 * c + 32], T.iotA[:, :], AF.Abs, bias=T.UF[:, 12 + c:13 + c], scale=-1.0), va)
            sA += [S(act(T.OA[:, 192 * h:192 * h + 192], T.TA[:, 192 * h:192 * h + 192], AF.Relu, bias=8192.0, scale=-8192.0), s)] * 6
        ob = []

        def kills(n):
            for c in range(len(ob), len(ob) + n):
                ob.append(V(ts(T.OB[:, 128 * c:128 * c + 128], T.iotB[:, :], T.XS[:, 17 * c + 16:17 * c + 17], A.subtract,
                               T.UF[:, c:c + 1], A.is_equal), vX, vb))
        if t == RO - 1:
            kills(10)
        v = V(tt(T.FI[:, :], T.XS[:, 16::17], T.AS[:, 16::17], A.max), vX)
        kills(2)
        v5 = V(ts(T.F5[:, :], T.FI[:, :], 31, A.bitwise_and), v)
        if t < RO - 1:
            kills(K1)
        if t == RO - 1:
            for c in range(12):
                pd = MM([ob[c], sA[c]], (T.pD[:, 0:32], T.OB[:, 128 * c:128 * c + 128], T.OA[:, 32 * c:32 * c + 32], False, c == 11))
            break
        v = V(tt(T.Wt[:, 0:192], T.F5[:, :].indirect(T.LC[:, :]), T.C15[:, 0:192], A.is_equal), v5)
        kills(8 - K1)
        for c in range(12):
            if c == 10:
                vW = V(tt(T.WD[:, :], T.pW[:, 0:192], T.Dg[:, :], A.mult), m, sG)
                kills(2)
            pd = MM([ob[c], sA[c]], (T.pD[0:32, 0:128], T.OA[:, 32 * c:32 * c + 32], T.OB[:, 128 * c:128 * c + 128], False, c == 11))
            if c == K1 + 1:
                m = MM([v], (T.pW[:, 0:128], T.Wt[:, 0:128], T.Ib[:, :], True, True),
                       (T.pW[0:64, 128:192], T.Wt[:, 128:192], T.Ib[:, 0:64], True, True),
                       (T.pW[64:128, 128:192], T.Wt[:, 128:192], T.Ib[:, 64:128], True, True))
        vD = S(act(T.D[:, :], T.pD[0:32, 0:128], AF.Sign, bias=(0.0 if t else -15.5)), pd, tF)
        tF = flags_to_F("ys", vD)
        if t < 2:
            ms = [(T.pZ[:, :], T.Ih[:, :], T.P2h[:, :], True, False)] + [
                (T.pZ[:, :], T.YS[:, 112 - 16 * q:240 - 16 * q], T.Z[:, 512 * q:512 * q + 512], False, q == 7) for q in range(8)]
            pz = MM([], *ms[5 * t:5 * t + 5])
        if t == 1:
            sV = S(act(T.VAL[:, :], T.pZ[:, :], AF.Identity, bias=2048.0), pz)
            xV = exchange("VAL", "stV", "landV", "dV", "arrV", sV)
        if t == 1:
            w = V(ts(T.COf[:, :], T.AO[:, 12:24], -2048.0, A.add), xA)
        vTk = V(lambda e: e.tensor_tensor(T.Tk[:, :].indirect(at), T.Hf[:, :], T.WD[:, :], A.add), vW, vTk, hf)
        if t == 1:
            w = V(tt(T.EO[:, :], T.COf[:, :].indirect(LB), T.EM[:, :], A.mult), w)
            pO = MM([w], (T.pE[:, 0:192], rep(0), T.EO[:, :], True, True))
    V(cpy(T.LO[:, 4::8], T.F5[:, 0:8]), v5)
    V(cpy(T.LO[:, 5:32:8], T.F5[:, 8:12]))
    v = V(cpy(T.LO[:, 37::8], T.F5[:, 8:12]))
    for u in range(4):
        s = S(act(T.LO[:, u::8], T.pD[:, u:32:4], AF.Sign), pd)
    xW = send(lambda n: T.LO[:, 8 * n:8 * n + 8], T.LN[:, 8 * me:8 * me + 8], "arrW", v, s)
    vW = V(cpy(T.LN[:, 8 * me:8 * me + 8], T.LO[:, 8 * me:8 * me + 8]), v, s)
    v = V(cpy(T.TkO[:, :], T.YI[:, :]), tYI)
    v = V(ts(T.HO2[:, :], T.TkO[:, :].indirect(T.AO[:, 0:12]), -2048.0, A.add), v)
    V(cpy(T.HO[:, :], T.TkO[:, :].indirect(T.AO[:, 0:12])))
    vG = V(tt(T.DgO[:, :], T.pE[:, 0:192], T.HO2[:, :], A.subtract), v, pO)
    v = V(tt(T.Wt[:, :], T.LN[:, :].indirect(T.LH[:, :]), T.C15[:, :], A.is_equal), xW, vW)
    m = MM([xW, vW], *[(T.pM[0:8, 128 * u:128 * u + 128], T.LN[:, u::8], T.Ib[:, :], True, True) for u in range(4)])
    s = S(act(T.KD[:, :], T.pM[0:8, :]), m)
    h = 64 * (me // 4)
    m = MM([v], (T.pW[:, 0:128], T.Wt[:, 0:128], T.Ib[:, :], True, True), (T.pW[:, 128:192], T.Wt[:, 128:256], T.Ib[:, h:h + 64], True, True))
    v = V(tt(T.WD[:, :], T.pW[:, 0:192], T.DgO[:, :], A.mult), m, vG)
    v = V(lambda e: e.tensor_tensor(T.TkO[:, :].indirect(T.AO[:, 0:12]), T.HO[:, :], T.WD[:, :], A.add), v)
    dma("y", T.yt[:], T.TkO[:, :], "oY", v)
    m = MM([s, sV], (T.pZ[:, :], T.R8b[:, :], T.KD[:, :], True, True))
    v = V(tt(T.YP[:, :], T.pZ[:, :], T.VR[:, :], A.max), m, tVR)
    dma("s", T.yp[:], T.YP[:, :], "oP", v)
    need("g", [(s, n) for s, n in cnt.items() if n])
